import numpy as np, ml_dtypes
CORES = [10,34,74,98]
N = 4
BF = ml_dtypes.bfloat16
W, S, M, CAP, RO, DX = 8192, 1024, 8, 96, 3, 2
def places(g, w, k):
    u = np.add.reduce(w[..., :, None] * g, axis=-2) & 4095
    return ((u * u >> 5)[..., None, :] + k[..., :, None] * u[..., None, :]) & (W - 1)
def parts(rng):
    return (rng.integers(0, 256, (N, 8, 16, W), dtype=np.int32), rng.integers(0, 256, (N, 8, 16, S)), rng.integers(0, 256, (N, 8, 16, RO)),
            rng.integers(0, 3969, (N, 8, M)), rng.integers(620, 1000, (N, 8)))
def pack(x, g, w, k, t):
    return {"xs": x.reshape(N, 128, W).astype(np.float32).astype(BF), "gd": g.reshape(N, 128, S).astype(np.float32).astype(BF), "wt": w.reshape(N, 128, RO).astype(np.int32),
            "km": np.repeat(k, 16, axis=1).astype(np.int32), "th": np.repeat(t, 16, axis=1)[:, :, None].astype(np.int32)}
def plant(x, g, j, c, i, d):
    v = 255 - g[:, j]; n = np.arange(len(j)); a = v[i, n]
    v[i, n] = np.where(a < 128, a + d, a - d); x[:, c] = v
def lone(rng, x, g, w, k, s0, s1, lo, hi):
    c = places(g, w, k)[:, s0:s1]; m, j = np.nonzero((c >= lo) & (c < hi))
    if len(m):
        i = int(rng.integers(0, len(m))); x[:, c[m[i], j[i]]] = 255 - g[:, s0 + j[i]]
def setup_inputs(rng):
    x, g, w, k, t = parts(rng); h = rng.integers(0, 8)
    t[0, h] = 995; t[1, h] = 620; t[DX, h] = 620
    return pack(x, g, w, k, t)
def setup_inputs_room(rng):
    x, g, w, k, t = parts(rng); t = rng.integers(60, 129, (N, 8)); k = np.minimum(k | 1, 3967)
    for q in range(N):
        room = rng.permutation(np.array([0, 1, CAP - 1, CAP, CAP + 1, 2 * CAP, 0, CAP]))
        for h in range(8):
            c = places(g[q, h], w[q, h, :, 0], k[q, h])[rng.integers(0, M, S), np.arange(S)]
            o = rng.permutation(S); o = o[c[o] < W - 96]; first = np.unique(c[o], return_index=True)[1]
            o = o[np.sort(first)][:int(room[h])]; n = len(o)
            plant(x[q, h], g[q, h], o, c[o], rng.integers(0, 16, n), rng.integers(0, t[q, h], n))
    return pack(x, g, w, k, t)
def setup_inputs_ties(rng):
    x, g, w, k, t = parts(rng)
    w[:, :, 2, 0] = w[:, :, 1, 0]; g[:, :, 1] = np.minimum(g[:, :, 1], 254); g[:, :, 2] = np.maximum(g[:, :, 2], 1)
    for q in range(N):
        for h in (0, 2, 4, 6):
            n = int(rng.choice(np.array([CAP // 4, CAP // 2, CAP]))); t[q, h] = 3 if h == 2 * (q % 4) else rng.integers(1, 4)
            o = rng.permutation(S); a = np.minimum(o[:n], o[n:2 * n]); b = np.maximum(o[:n], o[n:2 * n]); e = o[2 * n:3 * n]
            kd = rng.integers(0, 4, n); kd[:4] = np.arange(4); s = (kd > 0).astype(np.int64)
            v = g[q, h][:, a].copy(); v[1] += s; v[2] -= s; g[q, h][:, b] = v
            c = places(g[q, h], w[q, h, :, 0], k[q, h])
            ca = c[rng.integers(0, M, n), a]; m = rng.integers(0, M, n); c1 = c[m, e]; c2 = c[(m + rng.integers(1, M, n)) % M, e]
            al = np.concatenate([ca, c1, c2]); one = np.bincount(al, minlength=W)[al] == 1
            pa = one[:n] & (ca < W - 96); pe = one[n:2 * n] & one[2 * n:]
            v = 255 - g[q, h][:, a]; v[1] -= ((kd == 1) | (kd == 2)).astype(np.int64); v[2] += (kd == 1).astype(np.int64); x[q, h][:, ca[pa]] = v[:, pa]
            i = rng.integers(0, 16, n); d = rng.integers(0, t[q, h], n)
            plant(x[q, h], g[q, h], e[pe], c1[pe], i[pe], d[pe]); plant(x[q, h], g[q, h], e[pe], c2[pe], i[pe], d[pe])
    a = int(rng.integers(0, S // 4)); b = a + int(rng.integers(1, S // 4))
    w[:, 1, :, 0] = 0; w[:, 1, 0, 0] = 1; k[:, 1, 0] = 0; k[:, 1, 1] = 3; t[:, 1] = 20
    g[:, 1, :, b] = g[:, 1, :, a].copy(); g[:, 1, 0, a] = 32; g[:, 1, 0, b] = 64
    x[:, 1, :, 128] = 255 - g[:, 1, :, a]; x[:, 1, 0, 128] = 207
    return pack(x, g, w, k, t)
def setup_inputs_ends(rng):
    x, g, w, k, t = parts(rng); o = rng.permutation(8); w[:, :, 0, 0] |= 1
    low = rng.integers(0, 192, (N, 4, W)); few = rng.integers(0, 64, (N, W)) == 0
    x[:, o[0], 0] = low[:, 0]; x[:, o[1], 0] = rng.integers(192, 256, (N, W))
    x[:, o[2], 0] = low[:, 1]; x[:, o[2], 0, 0] = 192; x[::2, o[2], 0, W - 1] = 255
    x[1::2, o[2], 0, W - 40] = 192; x[1::2, o[2], 0, W - 20] = 192
    x[:, o[3], 0, W // 2:] = low[:, 2, W // 2:]; x[:, o[4], 0] = np.where(few, 192, low[:, 3])
    x[:, o[6], 0, W - 81:] = low[:, 0, W - 81:]; x[:, o[7], 0, W - 81:] = low[:, 1, W - 81:]; x[:, o[7], 0, W - 4] = 192
    t[::2, o[0]] = 4080; t[1::2, o[0]] = 4; t[1::2, o[2]] = 4
    for q in range(1, N, 2):
        lone(rng, x[q, o[0]], g[q, o[0]], w[q, o[0], :, 0], k[q, o[0]], 0, S // 4, W // 2, W - 96)
        lone(rng, x[q, o[0]], g[q, o[0]], w[q, o[0], :, 1], k[q, o[0]], S // 4, S - 3 * CAP, 0, W // 4)
        lone(rng, x[q, o[2]], g[q, o[2]], w[q, o[2], :, 0], k[q, o[2]], 0, S, 0, W // 4)
    for q in range(N):
        for h in o[5:]:
            u = np.add.reduce(w[q, h, :, 0][:, None] * g[q, h], axis=0) & 4095; used = []
            for m, c in enumerate((W - 97, W - 96, 0)):
                for j in range(S):
                    if u[j] & 1 and j not in used:
                        v = int(u[j]); kk = (c - (v * v >> 5)) * pow(v, -1, W) % W
                        if kk <= 3968:
                            k[q, h, m] = kk; used.append(j)
                            plant(x[q, h], g[q, h], np.array([j]), np.array([c]), np.array([3 + m]), np.array([m])); break
    return pack(x, g, w, k, t)
def setup_inputs_alike(rng):
    x, g, w, k, t = parts(rng); o = rng.permutation(8)
    g[:, o[0]] = g[:, o[0], :, :1].copy()
    for q in range(N):
        c = places(g[q, o[0]], w[q, o[0], :, 0], k[q, o[0]])[:, 0]; m = np.flatnonzero(c < W - 96)[:1]
        plant(x[q, o[0]], g[q, o[0]], np.zeros(len(m), np.int64), c[m], m, np.full(len(m), 3))
    w[:, o[1]] = 0
    for q in range(N):
        e = np.arange(1, CAP + 1); d = np.append(e[::-1] if q % 2 == 0 else e, 0); n = np.arange(CAP + 1); i = rng.integers(0, 16, CAP + 1)
        v = np.repeat(255 - x[q, o[1], :, :1], CAP + 1, axis=1); a = v[i, n]
        v[i, n] = np.where(a < 128, a + d, a - d); g[q, o[1], :, :CAP + 1] = v
    k[:, o[2]] = k[:, o[2], :1].copy()
    g[:, o[3]] = g[:, o[3]][:, :, rng.integers(0, 4, S)]
    b = x[:, o[4], :, :8].copy(); b[:, 0, 0] = 200
    x[:, o[4]] = b[:, :, rng.integers(0, 8, W)]; g[:, o[4]] = 255 - b[:, :, rng.integers(0, 8, S)]
    k[:, o[5]] = rng.choice(np.array([0, 1, 3968]), (N, M))
    x[:, o[6]] = 255 * rng.integers(0, 2, (N, 16, W)); g[:, o[6]] = 255 * rng.integers(0, 2, (N, 16, S))
    w[:, o[7], :, 0] = 0; w[:, o[7], 0, 0] = 1; k[:, o[7]] = rng.integers(0, 8, (N, M)); t[:, o[7]] = 4080
    g[:, o[7], 0] = np.minimum(g[:, o[7], 0], 254); g[:, o[7], 0, S - 1] = 255
    for q in range(N):
        c = int(places(g[q, o[7]], w[q, o[7], :, 0], k[q, o[7]])[0, S - 1]); x[q, o[7], :, c] = 255 - g[q, o[7], :, S - 1]
    return pack(x, g, w, k, t)
def setup_inputs_spread(rng):
    x, g, w, k, t = parts(rng)
    def uneven(n):
        v = np.minimum((np.exp2(8 * rng.random((N, 8, 1, n))) * rng.random((N, 8, 16, n))).astype(np.int64), 255)
        return np.where(rng.random((N, 8, 1, n)) < 0.5, v, 255 - v)
    x = uneven(W); g = uneven(S)
    w = np.minimum(np.exp2(8 * rng.random(w.shape)).astype(np.int64), 255); k = np.minimum(np.exp2(12 * rng.random(k.shape)).astype(np.int64), 3968)
    t = np.minimum(np.maximum(np.exp2(12 * rng.random((N, 8))).astype(np.int64), 1), 4080); t[:, rng.integers(0, 8)] = rng.integers(1500, 2500, N)
    return pack(x, g, w, k, t)
def check_inputs(d):
    bad = []
    for n, lo, hi in (("xs", 0, 255), ("gd", 0, 255), ("wt", 0, 255), ("km", 0, 3968), ("th", 1, 4080)):
        a = np.asarray(d[n]).astype(np.float64)
        if not np.all((a >= lo) & (a <= hi) & (np.floor(a) == a)): bad.append("range of " + n)
    for n in ("km", "th"):
        a = np.asarray(d[n]).reshape(N, 8, 16, -1)
        if np.any(a != a[:, :, :1]): bad.append("rows of a group alike in " + n)
    return bad
def reference(xs, gd, wt, km, th):
    x = xs.astype(np.float32).astype(np.int32).reshape(N, 8, 16, W); g = gd.astype(np.float32).astype(np.int32).reshape(N, 8, 16, S)
    w = wt.astype(np.int64).reshape(N, 8, 16, RO); k = km.astype(np.int64).reshape(N, 8, 16, M)[:, :, 0]; t = th.astype(np.int64).reshape(N, 8, 16)[:, :, 0]
    log = np.zeros((N, 8, W), np.int64); place = np.arange(W); slot = np.arange(S); rows = np.arange(8)[:, None]
    for rnd in range(RO):
        cuts = []; gives = []; nx = []
        for a in range(N):
            c = places(g[a], w[a, :, :, rnd], k[a])
            v = np.take_along_axis(x[a], c.reshape(8, 1, M * S), 2).reshape(8, 16, M, S)
            D = np.add.reduce(np.abs(g[a][:, :, None, :] + v - 255), axis=1)
            m = np.argmin(D, axis=1)[:, None]
            D = np.take_along_axis(D, m, 1)[:, 0].astype(np.int64); c = np.take_along_axis(c, m, 1)[:, 0]
            fit = (D < t[a][:, None]) & (c < W - 96)
            cand = fit & (np.add.accumulate(fit.astype(np.int64), axis=1) <= CAP)
            key = D * S + slot; low = np.full((8, W), 2 ** 40, np.int64)
            np.minimum.at(low, (rows, c), np.where(cand, key, 2 ** 40))
            cut = cand & (np.take_along_axis(low, c, 1) == key)
            ok = (x[a][:, 0] >= 192) & (x[a][:, 0] <= 255)
            U = np.minimum.accumulate(np.where(ok, place, W - 1)[:, ::-1], axis=1)[:, ::-1]
            e1 = np.take_along_axis(U, np.minimum(c + 16, W - 1), 1); e2 = np.take_along_axis(U, np.minimum(e1 + 8, W - 1), 1)
            gives.append([np.maximum(255 - np.take_along_axis(x[a], e[:, None, :], 2), 0) for e in (np.minimum(c + 10, W - 1), e1, e2)])
            reach = np.full((8, W), -1, np.int64); np.maximum.at(reach, (rows, c), np.where(cut, e2, -1))
            gone = np.maximum.accumulate(reach, axis=1) >= place
            log[a] = np.where(gone & (log[a] == 0), rnd + 1, log[a])
            nx.append(np.where(gone[:, None, :], np.int32(512), x[a])); cuts.append(cut)
        ng = []
        for a in range(N):
            p, q = a ^ 1, a ^ DX
            every = np.concatenate([gives[p][0], gives[q][1], gives[q][2], g[a], g[a]], axis=2)
            there = np.concatenate([cuts[p], cuts[q], cuts[q], ~cuts[a], cuts[a]], axis=1)
            o = np.argsort(~there, axis=1, kind="stable")[:, :S]
            ng.append(np.take_along_axis(every, o[:, None, :], 2))
        x = np.stack(nx); g = np.stack(ng)
    return {"yg": g.reshape(N, 128, S).astype(np.float32).astype(BF), "yc": log.astype(np.float32)}

@@ -1,0 +1,543 @@
+from concourse.bass import DstId, RemoteDMATransfer
+from concourse.mybir import AluOpType as O, ActivationFunctionType as AF, AxisListType
+
+W, S, M, CAP, RO = 8192, 1024, 8, 96, 3
+BIG = 16384.0
+FWW = W + 2 * CAP
+
+F32, B16, I32, U16 = "float32", "bfloat16", "int32", "uint16"
+_OWN = {
+    "X": (W, B16), "FW": (FWW, F32), "G0": (S + CAP, B16), "G1": (S + CAP, B16), "X0": (512, B16),
+    "wti": (3, I32), "kmi": (8, I32), "thi": (1, I32), "LW": (512, F32), "U2": (512, F32), "YC": (512, F32),
+    "UL": (512, F32), "NO": (512, F32), "PL": (512, F32), "D0": (S, F32), "D1": (S, F32), "D2": (S, F32), "C": (512, I32), "OFF": (512, U16),
+}
+for _r in range(RO):
+    _OWN.update({"SI%d" % _r: (8, F32), "SP%d" % _r: (96, B16), "ST%d" % _r: (192, B16), "RI%d" % _r: (8, F32), "RJ%d" % _r: (8, F32), "Z%d" % _r: (288 + S, B16)})
+_PART = {
+    F32: {"wtf": 3, "kmf": 8, "th16": 1, "one": 128, "GB": 128, "GBt": 128, "GB8": 128, "GB32": 128, "B0": 128, "ID": 128, "IDB": 128, "USf": 128,
+          "PI": 1, "P512": 1, "P513": 1, "P5K": 1, "CB": 16, "QM": 96, "MW": 96, "RST": 96, "Q0": 96, "Q1": 96, "QT": 96, "NMW": 96, "BI": 64, "QB0": 6, "QB": 6, "QBK": 6, "BK": 6,
+          "i16": 16, "I16": 16, "LM": 16, "PL0": 512, "NEG": 512, "gwA": 8, "gwB": 8, "Uf": 64, "KM": 64, "F0": 64, "PW": 72, "LWn": 72, "BQ": 6, "OH": 96,
+          "LG": 96, "KG": 96, "WL": 96, "SL": 96, "INV": 96, "CG": 96, "WK": 96, "SK": 96, "WC": 96, "SC": 96, "EG": 96, "EG2": 96, "W1": 96, "S1": 96,
+          "W2": 96, "S2": 96, "KB": 576, "SGN": 576, "C6": 6, "R6": 6, "CR": 96, "CUT": 96, "NCQ": 96, "RK": 96, "CD": 96, "WD": 96, "SD": 96, "LEN": 96, "ZR": 96,
+          "M1": 96, "M2": 96, "RD": 1, "IN": 1, "T1": 6, "T2": 6, "BIF": 12, "HX": 72, "IX": 64, "SLf": 64, "NT1": 1, "NT2": 1, "ST": 512, "OF": 16, "FM": 16, "UI": 1},
+    B16: {"oneb": 128, "GBb": 128, "GBK": 128, "nUS": 128, "IDb": 128, "IDK": 128, "nIDb": 128, "ID2b": 128, "ID3b": 128, "nIDBb": 128, "nB02": 128,
+          "it0": 128, "it1": 128, "IT2": 128, "ib": 64, "SLh": 64, "SLi": 64, "SEL": 2048, "WSA": 2048, "WSB": 2048, "FL": 512, "M2C": 512, "XG": S, "A0": S, "A1": S, "A2": S,
+          "FIT": 64, "CS": 64, "JK": 384, "JL": 576, "XH": 512, "SPQ": 112, "STQ": 208, "INVb": 96, "KL": 576, "EA": 384, "EB": 384, "TA": 768, "GQ": 112, "PG": 96, "PN": 96,
+          "TG": 192, "TN": 192, "F1": 64, "F2": 64, "F3": 64, "SG0": 512, "SG1": 512, "SG2": 512, "N1": 512, "N2": 512},
+    I32: {"pi": 1, "pi2": 1, "Ui": 64, "Um": 64, "UU": 64, "FQ": 64, "CA": 512, "KMi": 64, "PAR": 64, "MX": 64, "KD": 72, "XA": 6, "XI": 6, "VV": 6, "BII": 12},
+    U16: {"BQo": 6, "LO": 6, "UO": 6, "UO2": 6, "PO": 6, "TO": 12, "KIu": 12, "ROu": 6, "SQ": 6, "IXu": 64, "FX": 64},
+}
+_AT, SCRATCH = {}, {n: ("sbuf", [128, c], d) for n, (c, d) in _OWN.items()}
+for _d, _n in ((F32, "SF"), (B16, "SB"), (I32, "SJ"), (U16, "SU")):
+    _c = 0
+    for _k, _w in _PART[_d].items():
+        _AT[_k] = (_n, _c, _w)
+        _c += -(-_w // 16) * 16
+    SCRATCH[_n] = ("sbuf", [128, _c], _d)
+_PS = ["pA", "pB", "pM", "pN", "pK0", "pK1", "pD0", "pD1"]
+SCRATCH.update({n: ("psum", [128, 512], F32) for n in _PS})
+SEMAPHORES = ["sv", "ss", "st", "sg", "loc"] + ["a%s%d" % (k, r) for k in "ijpt" for r in range(RO)] + ["d%d" % k for k in range(30)]
+
+
+def _queues(g, T):
+    Q = {"v": g.vector, "s": g.scalar, "t": g.tensor, "g": g, "y": g.sync}
+    ENG = {"v": "sv", "s": "ss", "t": "st", "g": "sg"}
+    cnt, seen, acc, no = {}, {q: {} for q in Q}, {}, [0, 0]
+
+    def A(n, a=0, b=None, s=1, rows=None):
+        m, off, w = _AT[n] if n in _AT else (n, 0, T[n].shape[1])
+        b = w if b is None else b
+        a, b, t = a + off, b + off, T[m]
+        if rows is not None:
+            ap = t[rows, a:b]
+        elif s < 0:
+            ap = t[:, ::-1]
+        elif s > 1:
+            ap = t[:, a:b:s]
+        else:
+            ap = t[:, a:b]
+        return (ap, ((m, a, b, abs(s)),), ())
+
+    def X(ap):
+        return (ap, (), ())
+
+    def IND(win, off):
+        return (win[0].indirect(off[0]), win[1], off[1])
+
+    def need(q, outs, ins, chain=False):
+        deps = []
+        for w, regs in ((True, outs), (False, ins)):
+            for (n, a, b, s) in regs:
+                ps = n in _PS
+                for rec in acc.get(n, ()):
+                    rw, rq, sem, val, ra, rb, rs, clk, k = rec
+                    if not (w or rw or (ps and rq != q)):
+                        continue
+                    if not (ps and rq != q):
+                        if b <= ra or rb <= a or (s == rs and s > 1 and (a - ra) % s):
+                            continue
+                        if rq == q and chain and w:
+                            continue
+                    deps.append((k, sem, val, clk))
+        deps.sort(key=lambda d: -d[0])
+        for k, sem, val, clk in deps:
+            if seen[q].get(sem, 0) >= val:
+                continue
+            Q[q].wait_ge(T.sem[sem], val)
+            for s2, v2 in clk.items():
+                if seen[q].get(s2, 0) < v2:
+                    seen[q][s2] = v2
+            seen[q][sem] = max(val, seen[q].get(sem, 0))
+
+    def note(q, sem, val, clk, outs, ins):
+        no[0] += 1
+        for w, regs in ((True, outs), (False, ins)):
+            for (n, a, b, s) in regs:
+                old = acc.get(n, [])
+                if w and s == 1:
+                    old = [x for x in old if not (a <= x[4] and x[5] <= b)]
+                old.append((w, q, sem, val, a, b, s, clk, no[0]))
+                acc[n] = old
+
+    def split(outs, ins):
+        o = [x for p in outs for x in p[1]]
+        i = [x for p in outs for x in p[2]] + [x for p in ins if isinstance(p, tuple) for x in p[1] + p[2]]
+        return o, i
+
+    def run(q, outs, ins, call, chain=False):
+        o, i = split(outs, ins)
+        need(q, o, i, chain)
+        sem = ENG[q]
+        cnt[sem] = cnt.get(sem, 0) + 1
+        call().then_inc(T.sem[sem], 1)
+        clk = dict(seen[q])
+        clk[sem] = cnt[sem]
+        note(q, sem, cnt[sem], clk, o, i)
+
+    def v(x):
+        return x[0] if isinstance(x, tuple) else x
+
+    V, SC, TE = g.vector, g.scalar, g.tensor
+
+    def TT(o, a, b, op):
+        run("v", [o], [a, b], lambda: V.tensor_tensor(out=o[0], in0=a[0], in1=b[0], op=op))
+
+    def TS(o, a, s1, s2, op0, op1=None):
+        if op1 is None:
+            run("v", [o], [a, s1], lambda: V.tensor_scalar(out=o[0], in0=a[0], scalar1=v(s1), scalar2=None, op0=op0))
+        else:
+            run("v", [o], [a, s1, s2], lambda: V.tensor_scalar(out=o[0], in0=a[0], scalar1=v(s1), scalar2=v(s2), op0=op0, op1=op1))
+
+    def TC(o, a):
+        run("v", [o], [a], lambda: V.tensor_copy(out=o[0], in_=a[0]))
+
+    def MS(o, c):
+        run("v", [o], [], lambda: V.memset(o[0], c))
+
+    def RED(o, a, op):
+        run("v", [o], [a], lambda: V.tensor_reduce(out=o[0], in_=a[0], axis=AxisListType.X, op=op))
+
+    def SCAN(o, a, b, init, op0, op1):
+        run("v", [o], [a, b, init], lambda: V.tensor_tensor_scan(out=o[0], data0=a[0], data1=b[0], initial=v(init), op0=op0, op1=op1))
+
+    def ACT(o, a, f, bias=0.0, scale=1.0, acc=None):
+        if acc is None:
+            run("s", [o], [a, bias, scale], lambda: SC.activation(out=o[0], in_=a[0], func=f, bias=v(bias), scale=v(scale)))
+        else:
+            run("s", [o, acc], [a, bias, scale], lambda: SC.activation(out=o[0], in_=a[0], func=f, bias=v(bias), scale=v(scale), accum_out=acc[0]))
+
+    def MM(o, l, r, start, stop):
+        run("t", [o], [l, r], lambda: TE.matmul(o[0], l[0], r[0], start=start, stop=stop), not start)
+
+    def IOTA(o, pat, base, cm):
+        run("g", [o], [], lambda: g.iota(o[0], pat, base, cm, allow_small_or_imprecise_dtypes=True))
+
+    def AFF(o, a, pat, op, base, cm):
+        run("g", [o], [a], lambda: g.affine_select(o[0], a[0], pat, op, 0.0, base, cm))
+
+    def DMA(q, o, a):
+        os_, is_ = split([o], [a])
+        need(q, os_, is_)
+        sem = "d%d" % no[1]
+        no[1] += 1
+        Q[q].dma_start(o[0], a[0]).then_inc(T.sem[sem], 16)
+        cnt[sem] = 16
+        clk = dict(seen[q])
+        clk[sem] = 16
+        note("dma", sem, 16, clk, os_, is_)
+
+    def SEND(srcs, engines, call):
+        o, i = split([], srcs)
+        need("g", o, i)
+        call()
+        cnt["loc"] = cnt.get("loc", 0) + engines
+        note("rem", "loc", cnt["loc"], {}, o, i)
+
+    def LAND(dst, sem, val):
+        cnt[sem] = val
+        note("rem", sem, val, {sem: val}, list(dst[1]), [])
+
+    def END():
+        for sem in cnt:
+            if max(seen[q].get(sem, 0) for q in Q) < cnt[sem]:
+                g.wait_ge(T.sem[sem], cnt[sem])
+
+    return A, X, IND, TT, TS, TC, MS, RED, SCAN, ACT, MM, IOTA, AFF, DMA, SEND, LAND, END
+
+
+def rank_program(g, core, T, topo):
+    rank = T.rank_of(core)
+    if rank is None:
+        return
+    A, XT, IND, TT, TS, TC, MS, RED, SCAN, ACT, MM, IOTA, AFF, DMA, SEND, LAND, END = _queues(g, T)
+    CP, RL = AF.Copy, AF.Relu
+    q6 = (15, 96, 16)
+
+    DMA("y", A("G0", 0, S), XT(T.gd[:, :]))
+    DMA("s", A("wti"), XT(T.wt[:, :]))
+    DMA("s", A("kmi"), XT(T.km[:, :]))
+    DMA("s", A("thi"), XT(T.th[:, :]))
+    DMA("s", A("X", W // 2, W), XT(T.xs[:, W // 2:W]))
+    DMA("y", A("X", 0, W // 2), XT(T.xs[:, 0:W // 2]))
+    DMA("y", A("X0"), XT(T.xs[0::16, :]))
+
+    MS(A("one"), 1.0)
+    MS(A("oneb"), 1.0)
+    IOTA(A("pi"), [[0, 1]], 0, 1)
+    AFF(A("GBt"), A("one"), [[-16, 8], [0, 16]], O.is_ge, 0, 1)
+    AFF(A("GB"), A("GBt"), [[16, 8], [0, 16]], O.is_ge, 15, -1)
+    AFF(A("ID"), A("GB"), [[-1, 128]], O.is_equal, 0, 1)
+    MS(A("WSA"), 0.0)
+    for n, c in enumerate((-4080.0, 383.0 * BIG, 255.0, -1.0, 97.0)):
+        MS(A("CB", n, n + 1), c)
+    TS(A("pi2"), A("pi"), 15, None, O.bitwise_and)
+    TC(A("PI"), A("pi2"))
+    TC(A("wtf"), A("wti"))
+    TC(A("kmf"), A("kmi"))
+    TS(A("gwA"), A("GB", 0, 128, 16), A("wtf", 0, 1), None, O.mult)
+    MS(A("SEL"), 0.0)
+
+    def spread(dst, src, step):
+        for h in range(8):
+            ACT(A(dst, 16 * h, 16 * h + 129 * 15 + 1, 129), A("oneb", 0, 16), CP, scale=A(src, step * h, step * h + 1))
+    spread("WSA", "gwA", 1)
+
+    def lists(r):
+        G, WS = "G%d" % (r % 2), ("WSA", "WSB")[r % 2]
+        for i in range(16):
+            MM(A("pA", 0, 64), A(WS, 128 * i, 128 * i + 128), A(G, i, S, 16), i == 0, i == 15)
+        TC(A("Ui"), A("pA", 0, 64))
+        TS(A("Um"), A("Ui"), 4095, None, O.bitwise_and)
+        TC(A("Uf"), A("Um"))
+        for m in range(M):
+            ACT(A(("pB", "pM")[m // 4], 64 * (m % 4), 64 * (m % 4) + 64), A("Uf"), CP, scale=A("kmf", m, m + 1))
+        TT(A("UU"), A("Um"), A("Um"), O.mult)
+        TS(A("FQ"), A("UU"), 5, None, O.arith_shift_right)
+        for h in range(2):
+            for m in range(4 * h, 4 * h + 4):
+                TT(A("CA", 64 * m, 64 * m + 64), A(("pB", "pM")[h], 64 * (m % 4), 64 * (m % 4) + 64), A("FQ"), O.add)
+            TS(A("C", 256 * h, 256 * h + 256), A("CA", 256 * h, 256 * h + 256), W - 1, None, O.bitwise_and)
+            TC(A("OFF", 256 * h, 256 * h + 256), A("C", 256 * h, 256 * h + 256))
+            if h == 0 and r:
+                ACT(A("XG"), IND(A("X"), A("OFF", 0, 64)), CP)
+                ACT(A("XH"), IND(A("X"), A("OFF", 96, 128)), CP)
+
+    KB4 = ("pK0", "pK1", "pN", "pM")
+
+    def scores(r):
+        G = "G%d" % (r % 2)
+        for h in range(2):
+            MM(A("pD%d" % h), A("IDb"), A("XG", 512 * h, 512 * h + 512), True, False)
+            MM(A("pD%d" % h), A("IDb"), A(G, 512 * h, 512 * h + 512), False, True)
+        MM(A("pA"), A("IDb"), A("XH"), True, False)
+        MM(A("pA"), A("IDb"), A(G, 512, S), False, True)
+
+        def flag(h):
+            TS(A("FL", 256 * h, 256 * h + 256), A("C", 256 * h, 256 * h + 256), W - 96, None, O.is_ge)
+
+        def keys(m):
+            k = KB4[m % 4]
+            for i in range(16):
+                MM(A(k, 0, 64), A("SEL", 128 * i, 128 * i + 128), A("A%d" % (m % 3), i, S, 16), i == 0, False)
+            MM(A(k, 0, 64), A("IDb"), A("FL", 64 * m, 64 * m + 64), False, m == 0)
+            if m:
+                MM(A(k, 0, 64), A("IDb"), A("M2C", 64 * m, 64 * m + 64), False, True)
+
+        def least(m):
+            if m == 0:
+                TC(A("KM"), A(KB4[0], 0, 64))
+            elif m > 0:
+                TT(A("KM"), A(KB4[m % 4], 0, 64), A("KM"), O.min)
+        for h in range(2):
+            ACT(A("A0", 512 * h, 512 * h + 512), A("pD%d" % h), AF.Abs, bias=A("CB", 0, 1), scale=16.0)
+        ACT(A("A1", 512, S), A("pA"), AF.Abs, bias=A("CB", 0, 1), scale=16.0)
+        for m in range(1, M):
+            for h in range(2 if m == M - 1 else 1):
+                n = S // 2 if m in (1, M - 1) else S
+                a, b = n * h, n * h + n
+                TT(A("D%d" % (m % 3), a, b), IND(A("X"), A("OFF", 64 * m + a // 16, 64 * m + b // 16)), A(G, a, b), O.add)
+                ACT(A("A%d" % (m % 3), a, b), A("D%d" % (m % 3), a, b), AF.Abs, bias=A("CB", 0, 1), scale=16.0)
+            if m == 5 and r == 0:
+                ACT(A("NO"), A("X0"), RL, bias=A("CB", 1, 2), scale=-2 * BIG)
+            if m == 1:
+                flag(0)
+                keys(0)
+            if m == 3:
+                flag(1)
+            keys(m)
+            least(m - 3)
+        least(M - 3)
+        least(M - 2)
+        utable(0)
+        if r:
+            TC(IND(A("FW"), A("ROu")), A("ZR"))
+        least(M - 1)
+
+    def wrap(dst, src, tmp):
+        TT(A(tmp), src, A("MW"), O.mult)
+        SCAN(A(dst), A("RST"), A(tmp), 0.0, O.mult, O.add)
+
+    def utable(k):
+        if k == 0:
+            SCAN(A("UL", s=-1), A("NO", s=-1), A("PL", s=-1), float(W + 1), O.min, O.max)
+            TS(A("OF"), A("I16"), A("UL", 0, 1), None, O.mult)
+            MM(A("pD0", 0, 16), A("GB"), A("OF"), True, True)
+        elif k == 1:
+            TT(A("FM"), A("pD0", 0, 16), A("LM"), O.max)
+        elif k == 2:
+            RED(A("UI"), A("FM"), O.min)
+        else:
+            TS(A("U2"), A("UL"), A("UI"), None, O.min)
+            DMA("y", A("FW", 0, W, rows=slice(0, 128, 16)), A("U2"))
+
+    lists(0)
+    IOTA(A("QM"), [[0, 6], [1, 16]], 0, 0)
+    AFF(A("B0"), A("GB"), [[-16, 8], [0, 16]], O.is_equal, 0, 1)
+    AFF(A("USf"), A("GB"), [[-1, 128]], O.is_gt, 0, 1)
+    IOTA(A("PL0"), [[1, 512]], 2, 0)
+    IOTA(A("QB0"), [[16, 6]], 0, 0)
+    IOTA(A("BI"), [[1, 64]], 0, 0)
+    IOTA(A("i16"), [[1, 16]], 0, 0)
+    IOTA(A("it0"), [[0, 8], [1, 16]], 1, 0)
+    for n, c, base in (("Q0", 96, 0), ("Q1", 96, 1), ("QT", 96, W + CAP + 1), ("ib", 64, 0)):
+        IOTA(A(n), [[1, c]], base, 0)
+    IOTA(A("SLh"), [[16, 64]], 0, 0)
+    IOTA(A("M2C"), [[2, 8], [0, 64]], 0, 0)
+    IOTA(A("FW"), [[0, FWW]], 0, 0)
+    for n, c, base in (("KD", 72, 0), ("PW", 72, -1), ("LWn", 72, 0), ("HX", 72, 0), ("ZR", 96, 0), ("NEG", 512, -1), ("WSB", 2048, 0), ("SI0", 8, 0), ("SI1", 8, 0), ("SI2", 8, 0)):
+        IOTA(A(n), [[0, c]], base, 0)
+    for n, a, b in (("GQ", 96, 112), ("SPQ", 96, 112), ("STQ", 192, 208)):
+        IOTA(A(n, a, b), [[0, 16]], 0, 0)
+    spread("SEL", "GB", 16)
+    for n, a, c in (("IDb", "ID", 1.0), ("GBb", "GB", 1.0), ("nUS", "USf", -1.0), ("GB32", "GB", 32.0), ("GB8", "GB", 8.0), ("IDB", "ID", BIG)):
+        ACT(A(n), A(a), CP, scale=c)
+    ACT(A("XG"), IND(A("X"), A("OFF", 0, 64)), CP)
+    ACT(A("XH"), IND(A("X"), A("OFF", 96, 128)), CP)
+    TS(A("th16"), A("thi"), 16.0, None, O.mult)
+    TS(A("P512"), A("PI"), 512.0, None, O.mult)
+    TS(A("P513"), A("PI"), 512.0, 1.0, O.mult, O.add)
+    TS(A("P5K"), A("P513"), 10000.0, None, O.mult)
+    TS(A("PL"), A("PL0"), A("P512"), None, O.add)
+    TS(A("MW"), A("QM"), A("PI"), None, O.is_equal)
+    TS(A("NMW"), A("MW"), -1.0, None, O.mult)
+    TS(A("RST"), A("QM"), 0.0, None, O.is_gt)
+    TS(A("QB"), A("QB0"), A("PI"), 0.5, O.add, O.add)
+    TS(A("QBK"), A("QB"), -97.0, None, O.add)
+    TS(A("CB", 5, 6), A("PI"), 1.0 / 1024, None, O.mult)
+    TS(A("BI"), A("BI"), 1.0 / 32, A("CB", 5, 6), O.mult, O.add)
+    TS(A("I16"), A("i16"), A("PI"), None, O.is_equal)
+    TS(A("LM"), A("i16"), A("PI"), BIG, O.is_le, O.mult)
+    TS(A("SLi"), A("oneb", 0, 64), A("PI"), None, O.mult)
+    TS(A("SLf"), A("SLh"), A("PI"), None, O.add)
+    TT(A("it1"), A("it0"), A("GB"), O.mult)
+    TS(A("IT2"), A("it1"), -1.0, None, O.add)
+    TS(A("gwB"), A("GB", 0, 128, 16), A("wtf", 1, 2), None, O.mult)
+    TS(A("gwA"), A("GB", 0, 128, 16), A("wtf", 2, 3), None, O.mult)
+
+    near, far = T.cores[rank ^ 1], T.cores[rank ^ 2]
+
+    def to(dst, eng, sem, src, out):
+        rid, pid = topo.addr(dst)[0:2]
+        return RemoteDMATransfer(dst_ids=[DstId(rid=rid, pnc=pid)], dma_engine_mask=sum(1 << e for e in eng), remote_sem=T.sem[sem], src=src[0], dst=out[0])
+    en, ef = topo.engines(core, near), topo.engines(core, far)
+    hn = len(en) // 2
+
+    for r in range(RO):
+        last = r == RO - 1
+        G, H = "G%d" % (r % 2), "G%d" % ((r + 1) % 2)
+        SI, SP, STn, RI, RJ, Z, SG = ("%s%d" % (n, r) for n in ("SI", "SP", "ST", "RI", "RJ", "Z", "SG"))
+        if r:
+            lists(r)
+        scores(r)
+        if r == 0:
+            for n, a, c in (("nB02", "B0", -2.0), ("nIDBb", "ID", -BIG), ("nIDb", "ID", -1.0), ("GBK", "GB", BIG), ("IDK", "ID", BIG),
+                            ("ID2b", "ID", 2.0), ("ID3b", "ID", 3.0)):
+                ACT(A(n), A(a), CP, scale=c)
+        TC(A("KMi"), A("KM"))
+        TS(A("F0"), A("KM"), A("th16"), None, O.is_lt)
+        utable(1)
+        TS(A("PAR"), A("KMi"), 1, None, O.bitwise_and)
+        TS(A("MX"), A("KMi"), 14, None, O.bitwise_and)
+        TT(A("FIT"), A("F0"), A("PAR"), O.is_gt)
+        utable(2)
+        TS(A("KD", 0, 64), A("KMi"), 65520, None, O.bitwise_and)
+        SCAN(A("CS"), A("one", 0, 64), A("FIT"), 0.0, O.mult, O.add)
+        MM(A("pB", 0, 64), A("GBb"), A("CS"), True, True)
+        MM(A("pM", 0, 64), A("GBb"), A("CS"), True, False)
+        MM(A("pM", 0, 64), A("nUS"), A("FIT"), False, True)
+        MM(A("pN", 0, 64), A("GBb"), A("CS"), True, True)
+        for a in range(6):
+            ACT(A("JK", 64 * a, 64 * a + 64), A("pB", 0, 64), AF.Sign, bias=A("QB", a, a + 1), scale=-1.0, acc=A("BQ", a, a + 1))
+        if last:
+            MM(A("pK1"), A("IDb"), A("SG1"), True, False)
+            MM(A("pK1"), A("nIDb"), A("SG0"), False, True)
+            ACT(A("N1"), A("pK1"), RL)
+        if not last:
+            spread(("WSB", "WSA")[r], ("gwB", "gwA")[r], 1)
+        utable(3)
+        TT(A("LWn", 0, 64), A("MX"), A("BI"), O.add)
+        TT(A("PW", 0, 64), A("pM", 0, 64), A("FIT"), O.mult)
+        TS(A("INVb"), A("Q0"), A("pN", 63, 64), None, O.is_ge)
+        TS(A("INV"), A("INVb"), 2.0 ** -14, None, O.add)
+        TS(A("BQo"), A("BQ"), 0.5, 32.0, O.mult, O.add)
+        TT(A("OH"), IND(A("PW"), A("BQo")), A("Q1"), O.is_equal)
+        TT(A("LG"), IND(A("LWn"), A("BQo")), A("OH"), O.mult)
+        MM(A("pA", 0, 96), A("GB32"), A("LG"), True, True)
+        TT(A("KG"), IND(A("KD"), A("BQo")), A("OH"), O.mult)
+        MM(A("pK0", 0, 96), A("GB8"), A("KG"), True, False)
+        MM(A("pK0", 0, 96), A("ID"), A("Q0"), False, True)
+        TS(A("T1"), A("BQ"), 8.0, 608.0, O.mult, O.add)
+        wrap("SL", A("pA", 0, 96), "WL")
+        TC(A("LO"), A("SL", *q6))
+        TT(A("WK"), A("pK0", 0, 96), A("NMW"), O.mult)
+        TT(A("CG"), IND(A("C"), A("LO")), A("OH"), O.mult)
+        MM(A("pA", 0, 96), A("GB"), A("CG"), True, False)
+        MM(A("pA", 0, 96), A("IDB"), A("INV"), False, True)
+        SCAN(A("SK"), A("RST"), A("WK"), 0.0, O.mult, O.add)
+        for a in range(6):
+            ACT(A("SGN", 96 * a, 96 * a + 96), A("pK0", 0, 96), AF.Sign, bias=A("SK", 16 * a + 15, 16 * a + 16))
+        TS(A("XA"), A("SL", *q6), 32.0, None, O.mult)
+        wrap("SC", A("pA", 0, 96), "WC")
+        for a in range(6):
+            ACT(A("KB", 96 * a, 96 * a + 96), A("SGN", 96 * a, 96 * a + 96), CP, scale=A("SC", 16 * a + 15, 16 * a + 16))
+        TS(A("UO"), A("SC", *q6), 15.0, W - 1.0, O.add, O.min)
+        TS(A("XI"), A("XA"), 2047, None, O.bitwise_and)
+        TC(A("EG"), IND(A("FW"), A("UO")))
+        MM(A("pM", 0, 96), A("B0"), A("EG"), True, True)
+        TT(A("T2"), A("XI"), A("T1"), O.subtract)
+        TS(A("PO"), A("SC", *q6), 9.0, W - 1.0, O.add, O.min)
+
+        def same(a):
+            TT(A("KL", 96 * a, 96 * a + 96), A("KB", 96 * a, 96 * a + 96), A("pA", 0, 96), O.is_equal)
+            MM(A("pK1", 0, 96), A("GBK"), A("KL", 96 * a, 96 * a + 96), a == 0, False)
+        TS(A("SQ"), A("T2"), 96.0, None, O.add)
+        TS(A("C6"), A("SC", *q6), -1.0, W - 1.0, O.add, O.min)
+        wrap("S1", A("pM", 0, 96), "W1")
+        TS(A("UO2"), A("S1", *q6), 6.0, W - 1.0, O.add, O.min)
+        TC(A("EG2"), IND(A("FW"), A("UO2")))
+        MM(A("pN", 0, 96), A("B0"), A("EG2"), True, True)
+        ACT(A("PG"), IND(A("X"), A("PO")), CP)
+        ACT(A("PN"), A("PG"), RL, scale=-1.0)
+        MM(A("pD0", 0, 96), A("nIDb"), A("PG"), True, False)
+        MM(A("pD0", 0, 96), A("nB02"), A("PN"), False, True)
+        for a in range(4):
+            same(a)
+        TT(A("W2"), A("pN", 0, 96), A("MW"), O.mult)
+        same(4)
+        SCAN(A("S2"), A("RST"), A("W2"), 0.0, O.mult, O.add)
+        same(5)
+        MM(A("pK1", 0, 96), A("IDK"), A("INVb"), False, True)
+        TS(A("TO", 0, 6), A("S1", *q6), -2.0, None, O.add)
+        TS(A("TO", 6, 12), A("S2", *q6), -2.0, None, O.add)
+        ACT(A("CR"), A("pA", 0, 96), CP)
+        ACT(A("M1"), A("CR"), RL, bias=A("P5K"), scale=-10000.0)
+        ACT(A("SPQ", 0, 96), A("pD0", 0, 96), RL, bias=A("CB", 2, 3))
+        ACT(A("TG"), IND(A("X"), A("TO")), CP)
+        ACT(A("TN"), A("TG"), RL, scale=-1.0)
+        MM(A("pD1", 0, 192), A("nIDb"), A("TG"), True, False)
+        MM(A("pD1", 0, 192), A("nB02"), A("TN"), False, True)
+        TT(A("NCQ"), A("pK1", 0, 96), A("QT"), O.min)
+        TS(A("CUT"), A("NCQ"), 0.5, None, O.is_lt)
+        SCAN(A("RK"), A("one", 0, 96), A("CUT"), -97.0, O.mult, O.add)
+        ACT(A(SI, 0, 1), A("RK", 95, 96), AF.Identity, bias=A("CB", 4, 5))
+        ACT(A(SI, 7, 8), A("RK", 95, 96), AF.Identity, bias=A("CB", 3, 4), scale=-1.0)
+        SEND([A(SI)], 2 * hn, lambda: g.remote_dma_fused([to(near, en[:hn], "ai%d" % r, A(SI), A(RI)), to(far, ef[hn:], "aj%d" % r, A(SI), A(RJ))], local_sem=T.sem["loc"]))
+        for a in range(6):
+            ACT(A("JL", 96 * a, 96 * a + 96), A("RK"), AF.Sign, bias=A("QBK", a, a + 1), scale=-1.0, acc=A("BK", a, a + 1))
+        ACT(A("STQ", 0, 192), A("pD1", 0, 192), RL, bias=A("CB", 2, 3))
+        TT(A("CD"), A("NCQ"), A("RK"), O.add)
+        TT(A("LEN"), A("pN", 0, 96), A("CR"), O.subtract)
+        TT(A("WD"), A("CD"), A("MW"), O.mult)
+        SCAN(A("SD"), A("RST"), A("WD"), 0.0, O.mult, O.add)
+        TT(A("R6"), A("C6"), A("SD", *q6), O.max)
+        TT(A("VV"), A("T2"), A("SD", *q6), O.subtract)
+        TS(A("KIu", 0, 6), A("BK"), 0.5, 48.0, O.mult, O.add)
+        TS(A("KIu", 6, 12), A("BK"), 0.5, 144.0, O.mult, O.add)
+        ACT(A(SP), IND(A("SPQ"), A("KIu", 0, 6)), CP)
+        SEND([A(SP)], len(en), lambda: g.remote_dma_fused([to(near, en, "ap%d" % r, A(SP), A(Z, 0, 96))], local_sem=T.sem["loc"]))
+        ACT(A(STn), IND(A("STQ"), A("KIu")), CP)
+        SEND([A(STn)], len(ef), lambda: g.remote_dma_fused([to(far, ef, "at%d" % r, A(STn), A(Z, 96, 288))], local_sem=T.sem["loc"]))
+        ACT(A("GQ", 0, 96), IND(A(G, 0, S), A("SQ")), CP)
+        ACT(A(G, S, S + CAP), IND(A("GQ"), A("KIu", 0, 6)), CP)
+        TC(A("ROu"), A("R6"))
+        TS(A("BII", 0, 6), A("VV"), 16383, 4, O.bitwise_and, O.arith_shift_right)
+        TS(A("BII", 6, 12), A("VV"), 15, None, O.bitwise_and)
+        LAND(A(RI), "ai%d" % r, hn)
+        LAND(A(RJ), "aj%d" % r, len(ef) - hn)
+        LAND(A(Z, 0, 96), "ap%d" % r, len(en))
+        LAND(A(Z, 96, 288), "at%d" % r, len(ef))
+        TC(IND(A("FW"), A("ROu")), A("LEN"))
+        DMA("y", A("LW"), A("FW", 0, W, rows=slice(1, 128, 16)))
+        TC(A("BIF"), A("BII"))
+        for a in range(6):
+            ACT(A("EA", 64 * a, 64 * a + 64), A("ib"), AF.Abs, bias=A("BIF", a, a + 1), scale=-1.0)
+        ACT(A("EB"), A("EA"), RL, bias=A("one", 0, 1), scale=-1.0)
+        for a in range(6):
+            TS(A("TA", 128 * a, 128 * a + 128), A("IT2"), A("BIF", 6 + a, 7 + a), None, O.is_ge)
+            if a == 1:
+                TT(A("M2"), A("pN", 0, 96), A("M1"), O.min)
+            if a == 3:
+                RED(A("RD"), A("M2"), O.max)
+        TS(A("IN"), A("RD"), A("P512"), 0.0, O.subtract, O.max)
+        for a in range(6):
+            MM(A("pB", 0, 64), A("GBb"), A("EB", 64 * a, 64 * a + 64), a == 0, a == 5)
+        MM(A("pA", 0, 64), A("IDb"), A("SLh"), True, False)
+        MM(A("pA", 0, 64), A("IDb"), A("SLi"), False, False)
+        for a in range(6):
+            MM(A("pA", 0, 64), A("TA", 128 * a, 128 * a + 128), A("EB", 64 * a, 64 * a + 64), False, a == 5)
+        SCAN(A("HX", 1, 65), A("one", 0, 64), A("pB", 0, 64), 0.0, O.mult, O.add)
+        TT(A("IX"), A("pA", 0, 64), A("HX", 0, 64), O.add)
+        TC(A("IXu"), A("IX"))
+        ACT(A(Z, 288, 288 + S), IND(A(G, 0, S + CAP), A("IXu")), CP)
+        TT(A("NT1"), A(RI, 0, 1), A(RJ, 0, 1), O.add)
+        TS(A("F1"), A("SLf"), A(RI, 0, 1), A(RI, 7, 8), O.is_ge, O.mult)
+        TT(A("NT2"), A("NT1"), A(RJ, 0, 1), O.add)
+        TS(A("F2"), A("SLf"), A("NT1"), A(RJ, 7, 8), O.is_ge, O.mult)
+        TS(A("F3"), A("SLf"), A("NT2"), A(RJ, 7, 8), O.is_ge, O.mult)
+        SCAN(A("ST"), A("NEG"), A("LW"), A("IN"), O.add, O.max)
+        ACT(A(SG), A("ST"), AF.Sign)
+        for k, n in enumerate(("SLh", "SLi", "F1", "F2", "F3")):
+            MM(A("pM", 0, 64), A("IDb"), A(n), k == 0, k == 4)
+        if not last:
+            MM(A("pK0"), A("IDb"), A("X0"), True, False)
+            MM(A("pK0"), A("nIDBb"), A(SG), False, True)
+        TC(A("FX"), A("pM", 0, 64))
+        TC(A(H, 0, S // 2), IND(A(Z), A("FX", 0, 32)))
+        ACT(A(H, S // 2, S), IND(A(Z), A("FX", 32, 64)), CP)
+        if last:
+            DMA("y", XT(T.yg[:, :]), A(H, 0, S))
+        else:
+            TC(A("X0"), A("pK0"))
+            ACT(A("NO"), A("X0"), RL, bias=A("CB", 1, 2), scale=-2 * BIG)
+            DMA("y", A("X", 0, W, rows=slice(0, 128, 16)), A("X0"))
+        if last:
+            MM(A("pK1"), A("IDb"), A(SG), True, False)
+            MM(A("pK1"), A("nIDb"), A("SG0"), False, False)
+            MM(A("pK1"), A("nIDb"), A("N1"), False, True)
+            ACT(A("N2"), A("pK1"), RL)
+            MM(A("pD0"), A("IDb"), A("SG0"), True, False)
+            MM(A("pD0"), A("ID2b"), A("N1"), False, False)
+            MM(A("pD0"), A("ID3b"), A("N2"), False, True)
+            ACT(A("YC"), A("pD0"), CP)
+            DMA("s", XT(T.yc[:, :]), A("YC"))
+    END()

@@ -3,28 +3,31 @@ from concourse.mybir import AluOpType as O, ActivationFunctionType as AF, AxisLi
 
 W, S, M, CAP, RO = 8192, 1024, 8, 96, 3
 BIG = 16384.0
-FWW = W + 2 * CAP
+FWW = W + 112
+ARR = 3 * CAP
+FAR = 2.0 ** 20
 
 F32, B16, I32, U16 = "float32", "bfloat16", "int32", "uint16"
 _OWN = {
-    "X": (W, B16), "FW": (FWW, F32), "G0": (S + CAP, B16), "G1": (S + CAP, B16), "X0": (512, B16),
-    "wti": (3, I32), "kmi": (8, I32), "thi": (1, I32), "LW": (512, F32), "U2": (512, F32), "YC": (512, F32),
-    "UL": (512, F32), "NO": (512, F32), "PL": (512, F32), "D0": (S, F32), "D1": (S, F32), "D2": (S, F32), "C": (512, I32), "OFF": (512, U16),
+    "X": (W, B16), "FW": (FWW, F32), "GI": (S, B16), "G0": (S + CAP, B16), "G1": (S + CAP, B16), "YG": (S, B16),
+    "wti": (3, I32), "kmi": (8, I32), "thi": (1, I32), "LW": (512, F32), "U2": (512, F32), "YC": (512, F32), "XF": (512, F32),
+    "UL": (512, F32), "C": (512, I32), "OFF": (512, U16),
 }
 for _r in range(RO):
-    _OWN.update({"SI%d" % _r: (8, F32), "SP%d" % _r: (96, B16), "ST%d" % _r: (192, B16), "RI%d" % _r: (8, F32), "RJ%d" % _r: (8, F32), "Z%d" % _r: (288 + S, B16)})
+    _OWN.update({"X0%d" % _r: (512, B16), "RK%d" % _r: (96, F32), "SP%d" % _r: (96, B16), "ST%d" % _r: (192, B16), "RI%d" % _r: (8, F32), "RJ%d" % _r: (8, F32),
+                 "Z%d" % _r: (ARR + S, B16)})
 _PART = {
-    F32: {"wtf": 3, "kmf": 8, "th16": 1, "one": 128, "GB": 128, "GBt": 128, "GB8": 128, "GB32": 128, "B0": 128, "ID": 128, "IDB": 128, "USf": 128,
-          "PI": 1, "P512": 1, "P513": 1, "P5K": 1, "CB": 16, "QM": 96, "MW": 96, "RST": 96, "Q0": 96, "Q1": 96, "QT": 96, "NMW": 96, "BI": 64, "QB0": 6, "QB": 6, "QBK": 6, "BK": 6,
-          "i16": 16, "I16": 16, "LM": 16, "PL0": 512, "NEG": 512, "gwA": 8, "gwB": 8, "Uf": 64, "KM": 64, "F0": 64, "PW": 72, "LWn": 72, "BQ": 6, "OH": 96,
-          "LG": 96, "KG": 96, "WL": 96, "SL": 96, "INV": 96, "CG": 96, "WK": 96, "SK": 96, "WC": 96, "SC": 96, "EG": 96, "EG2": 96, "W1": 96, "S1": 96,
-          "W2": 96, "S2": 96, "KB": 576, "SGN": 576, "C6": 6, "R6": 6, "CR": 96, "CUT": 96, "NCQ": 96, "RK": 96, "CD": 96, "WD": 96, "SD": 96, "LEN": 96, "ZR": 96,
-          "M1": 96, "M2": 96, "RD": 1, "IN": 1, "T1": 6, "T2": 6, "BIF": 12, "HX": 72, "IX": 64, "SLf": 64, "NT1": 1, "NT2": 1, "ST": 512, "OF": 16, "FM": 16, "UI": 1},
-    B16: {"oneb": 128, "GBb": 128, "GBK": 128, "nUS": 128, "IDb": 128, "IDK": 128, "nIDb": 128, "ID2b": 128, "ID3b": 128, "nIDBb": 128, "nB02": 128,
-          "it0": 128, "it1": 128, "IT2": 128, "ib": 64, "SLh": 64, "SLi": 64, "SEL": 2048, "WSA": 2048, "WSB": 2048, "FL": 512, "M2C": 512, "XG": S, "A0": S, "A1": S, "A2": S,
-          "FIT": 64, "CS": 64, "JK": 384, "JL": 576, "XH": 512, "SPQ": 112, "STQ": 208, "INVb": 96, "KL": 576, "EA": 384, "EB": 384, "TA": 768, "GQ": 112, "PG": 96, "PN": 96,
-          "TG": 192, "TN": 192, "F1": 64, "F2": 64, "F3": 64, "SG0": 512, "SG1": 512, "SG2": 512, "N1": 512, "N2": 512},
-    I32: {"pi": 1, "pi2": 1, "Ui": 64, "Um": 64, "UU": 64, "FQ": 64, "CA": 512, "KMi": 64, "PAR": 64, "MX": 64, "KD": 72, "XA": 6, "XI": 6, "VV": 6, "BII": 12},
+    F32: {"wtf": 3, "kmf": 8, "th16": 1, "one": 128, "GB": 128, "GBt": 128, "nGB": 128, "nGB8": 128, "GB32": 128, "B0": 128, "ID": 128, "USf": 128, "LSf": 128,
+          "PI": 1, "P512": 1, "P513": 1, "P5K": 1, "PIN": 1, "LS1": 1, "LB1": 1, "CB": 16, "CW3": 3, "QM": 96, "MW": 96, "RSB": 96, "DMP": 96, "Q0": 96, "Q1": 96, "BI": 64, "QB0": 6, "QB": 6,
+          "BK": 6, "i16": 16, "I16": 16, "LM": 16, "PL0": 512, "PL": 512, "NO": 512, "Uf": 64, "KM": 64, "F0": 64, "PW": 72, "LWn": 72, "BQ": 6, "OH": 96,
+          "LG": 96, "KG": 96, "SL": 96, "CG": 96, "SK": 96, "SC": 96, "EG": 96, "EG2": 96, "S1": 96, "S2": 96, "KB": 576, "SGN": 576, "R6": 96, "CUT": 96, "LEN": 96,
+          "M1": 96, "M20": 97, "M21": 97, "M22": 97, "M23": 97, "IN": 1, "T1": 6, "T2": 6, "VV": 6, "VR": 6, "SLf": 64, "NT": 2, "NM": 2, "STT": 512, "OF": 16, "FM": 16, "UI": 1},
+    B16: {"oneb": 128, "GBb": 128, "GBK": 128, "nUS": 128, "LSK": 128, "IDb": 128, "IDh": 128, "IDK": 128, "nIDb": 128, "nB02": 128, "TSL": 144, "T32": 144, "Tn16": 144,
+          "WS0": 144, "WS1": 144, "WS2": 144, "it0": 128, "ITH": 128, "ROW": 65, "SLh": 64, "SLi": 64, "FL": 512, "M2C": 512, "MK": 96, "Q0b": 96, "C8K": 512, "N4": 512, "TWO": 512,
+          "XG0": S, "XG1": S, "AB0": S, "AB1": S, "D0": S, "D1": 2 * S, "R0": S, "R1": 2 * S,
+          "FIT": 64, "CS": 64, "JK": 384, "JL": 576, "SPQ": 112, "STQ": 208, "INV": 96, "KL": 576, "CW": 11, "LE": 390, "EQ": 390, "TA": 768, "GQ": 112, "PG": 96, "PN": 96,
+          "TG": 192, "TN": 192, "F1": 18, "F2": 18, "F3": 18, "SG0": 512, "SG1": 512},
+    I32: {"pi": 1, "pi2": 1, "Ui": 64, "Um": 64, "UU": 64, "FQ": 64, "CA": 512, "KMi": 64, "PAR": 64, "MX": 64, "KD": 72, "XA": 6, "XI": 6},
     U16: {"BQo": 6, "LO": 6, "UO": 6, "UO2": 6, "PO": 6, "TO": 12, "KIu": 12, "ROu": 6, "SQ": 6, "IXu": 64, "FX": 64},
 }
 _AT, SCRATCH = {}, {n: ("sbuf", [128, c], d) for n, (c, d) in _OWN.items()}
@@ -38,11 +41,19 @@ _PS = ["pA", "pB", "pM", "pN", "pK0", "pK1", "pD0", "pD1"]
 SCRATCH.update({n: ("psum", [128, 512], F32) for n in _PS})
 SEMAPHORES = ["sv", "ss", "st", "sg", "loc"] + ["a%s%d" % (k, r) for k in "ijpt" for r in range(RO)] + ["d%d" % k for k in range(30)]
 
+CUT_AT = 240
+BY_S = [(0, 64, "pN", 0), (64, 128, "pN", 64), (128, 192, "pK1", 64), (192, CUT_AT, "pM", 0)]
+BY_V = [(320, 384, "pK0", 0), (384, 448, "pK1", 0), (448, 512, "pB", 0), (CUT_AT, 320, "pA", 0)]
+_C = {"cy": 0.95, "gath": 1.5, "scat": 3.5, "pe": 0.48, "hop": 110.0, "own": 90.0, "dma": 2000.0, "rem": 2800.0, "passes": 6, "vlate": 1000.0}
+_ORDER = []
+
 
 def _queues(g, T):
     Q = {"v": g.vector, "s": g.scalar, "t": g.tensor, "g": g, "y": g.sync}
     ENG = {"v": "sv", "s": "ss", "t": "st", "g": "sg"}
-    cnt, seen, acc, no = {}, {q: {} for q in Q}, {}, [0, 0]
+    cnt, seen, acc, no, ops = {}, {q: {} for q in Q}, {}, [0, 0], []
+    lines = {}
+    cy = _C["cy"]
 
     def A(n, a=0, b=None, s=1, rows=None):
         m, off, w = _AT[n] if n in _AT else (n, 0, T[n].shape[1])
@@ -51,34 +62,43 @@ def _queues(g, T):
         if rows is not None:
             ap = t[rows, a:b]
         elif s < 0:
-            ap = t[:, ::-1]
+            ap = t[:, ::-1] if a == 0 and b == t.shape[1] else t[:, b - 1:a - 1:-1]
         elif s > 1:
             ap = t[:, a:b:s]
         else:
             ap = t[:, a:b]
-        return (ap, ((m, a, b, abs(s)),), ())
+        return (ap, ((m, a, b, abs(s)),), (), -(-(b - a) // abs(s)), SCRATCH[m][2], 0)
 
     def X(ap):
-        return (ap, (), ())
+        return (ap, (), (), 0, None, 0)
 
     def IND(win, off):
-        return (win[0].indirect(off[0]), win[1], off[1])
+        return (win[0].indirect(off[0]), win[1], off[1], 16 * off[3], win[4], 1)
 
-    def need(q, outs, ins, chain=False):
-        deps = []
+    def meets(w, q, reg, rec, chain):
+        n, a, b, s = reg
+        rw, rq, ra, rb, rs = rec[0:5]
+        ps = n in _PS and rq != q
+        if not (w or rw or ps):
+            return False
+        if not ps:
+            if b <= ra or rb <= a or (s == rs and s > 1 and (a - ra) % s):
+                return False
+            if rq == q and chain and w:
+                return False
+        return True
+
+    def keep(book, q, outs, ins, *what):
         for w, regs in ((True, outs), (False, ins)):
             for (n, a, b, s) in regs:
-                ps = n in _PS
-                for rec in acc.get(n, ()):
-                    rw, rq, sem, val, ra, rb, rs, clk, k = rec
-                    if not (w or rw or (ps and rq != q)):
-                        continue
-                    if not (ps and rq != q):
-                        if b <= ra or rb <= a or (s == rs and s > 1 and (a - ra) % s):
-                            continue
-                        if rq == q and chain and w:
-                            continue
-                    deps.append((k, sem, val, clk))
+                old = book.get(n, [])
+                if w and s == 1:
+                    old = [x for x in old if not (a <= x[2] and x[3] <= b)]
+                old.append((w, q, a, b, s) + what)
+                book[n] = old
+
+    def need(q, outs, ins, chain=False):
+        deps = [rec[5:] for w, regs in ((True, outs), (False, ins)) for reg in regs for rec in acc.get(reg[0], ()) if meets(w, q, reg, rec, chain)]
         deps.sort(key=lambda d: -d[0])
         for k, sem, val, clk in deps:
             if seen[q].get(sem, 0) >= val:
@@ -91,115 +111,211 @@ def _queues(g, T):
 
     def note(q, sem, val, clk, outs, ins):
         no[0] += 1
-        for w, regs in ((True, outs), (False, ins)):
-            for (n, a, b, s) in regs:
-                old = acc.get(n, [])
-                if w and s == 1:
-                    old = [x for x in old if not (a <= x[4] and x[5] <= b)]
-                old.append((w, q, sem, val, a, b, s, clk, no[0]))
-                acc[n] = old
+        keep(acc, q, outs, ins, no[0], sem, val, clk)
 
     def split(outs, ins):
         o = [x for p in outs for x in p[1]]
         i = [x for p in outs for x in p[2]] + [x for p in ins if isinstance(p, tuple) for x in p[1] + p[2]]
         return o, i
 
-    def run(q, outs, ins, call, chain=False):
+    def add(q, as_q, o, i, emit, busy, lat, chain=False, after=()):
+        ops.append((q, as_q, o, i, emit, busy, lat, chain, list(after)))
+        return len(ops) - 1
+
+    def LINE(name):
+        if name in lines:
+            ops[-1][8].append(lines[name])
+        lines[name] = len(ops) - 1
+
+    def run(q, outs, ins, call, busy, chain=False):
         o, i = split(outs, ins)
-        need(q, o, i, chain)
-        sem = ENG[q]
-        cnt[sem] = cnt.get(sem, 0) + 1
-        call().then_inc(T.sem[sem], 1)
-        clk = dict(seen[q])
-        clk[sem] = cnt[sem]
-        note(q, sem, cnt[sem], clk, o, i)
+
+        def emit():
+            need(q, o, i, chain)
+            sem = ENG[q]
+            cnt[sem] = cnt.get(sem, 0) + 1
+            call().then_inc(T.sem[sem], 1)
+            clk = dict(seen[q])
+            clk[sem] = cnt[sem]
+            note(q, sem, cnt[sem], clk, o, i)
+        return add(q, q, o, i, emit, busy, 0.0, chain)
 
     def v(x):
         return x[0] if isinstance(x, tuple) else x
 
+    def vlen(o, *ins, tt=False):
+        if o[5]:
+            return 50 + cy * _C["scat"] * o[3]
+        if ins and ins[0][5]:
+            return 50 + cy * _C["gath"] * o[3]
+        r = 0.5 if all(x[4] in (B16, U16) for x in (o,) + ins) else 1.0
+        if tt and all(x[1][0][0] not in _PS for x in ins):
+            r *= 2
+        return cy * max(64, r * max(x[3] for x in (o,) + ins))
+
     V, SC, TE = g.vector, g.scalar, g.tensor
 
     def TT(o, a, b, op):
-        run("v", [o], [a, b], lambda: V.tensor_tensor(out=o[0], in0=a[0], in1=b[0], op=op))
+        run("v", [o], [a, b], lambda: V.tensor_tensor(out=o[0], in0=a[0], in1=b[0], op=op), vlen(o, a, b, tt=True))
 
     def TS(o, a, s1, s2, op0, op1=None):
         if op1 is None:
-            run("v", [o], [a, s1], lambda: V.tensor_scalar(out=o[0], in0=a[0], scalar1=v(s1), scalar2=None, op0=op0))
+            run("v", [o], [a, s1], lambda: V.tensor_scalar(out=o[0], in0=a[0], scalar1=v(s1), scalar2=None, op0=op0), vlen(o, a))
         else:
-            run("v", [o], [a, s1, s2], lambda: V.tensor_scalar(out=o[0], in0=a[0], scalar1=v(s1), scalar2=v(s2), op0=op0, op1=op1))
+            run("v", [o], [a, s1, s2], lambda: V.tensor_scalar(out=o[0], in0=a[0], scalar1=v(s1), scalar2=v(s2), op0=op0, op1=op1), vlen(o, a))
 
     def TC(o, a):
-        run("v", [o], [a], lambda: V.tensor_copy(out=o[0], in_=a[0]))
+        run("v", [o], [a], lambda: V.tensor_copy(out=o[0], in_=a[0]), vlen(o, a))
 
     def MS(o, c):
-        run("v", [o], [], lambda: V.memset(o[0], c))
+        run("v", [o], [], lambda: V.memset(o[0], c), vlen(o))
 
     def RED(o, a, op):
-        run("v", [o], [a], lambda: V.tensor_reduce(out=o[0], in_=a[0], axis=AxisListType.X, op=op))
+        run("v", [o], [a], lambda: V.tensor_reduce(out=o[0], in_=a[0], axis=AxisListType.X, op=op), cy * max(64, a[3]))
 
     def SCAN(o, a, b, init, op0, op1):
-        run("v", [o], [a, b, init], lambda: V.tensor_tensor_scan(out=o[0], data0=a[0], data1=b[0], initial=v(init), op0=op0, op1=op1))
+        run("v", [o], [a, b, init], lambda: V.tensor_tensor_scan(out=o[0], data0=a[0], data1=b[0], initial=v(init), op0=op0, op1=op1), vlen(o, a, b))
 
     def ACT(o, a, f, bias=0.0, scale=1.0, acc=None):
+        n = 65 + cy * _C["gath"] * o[3] if a[5] else 30 + cy * max(64, o[3])
         if acc is None:
-            run("s", [o], [a, bias, scale], lambda: SC.activation(out=o[0], in_=a[0], func=f, bias=v(bias), scale=v(scale)))
+            run("s", [o], [a, bias, scale], lambda: SC.activation(out=o[0], in_=a[0], func=f, bias=v(bias), scale=v(scale)), n)
         else:
-            run("s", [o, acc], [a, bias, scale], lambda: SC.activation(out=o[0], in_=a[0], func=f, bias=v(bias), scale=v(scale), accum_out=acc[0]))
+            run("s", [o, acc], [a, bias, scale], lambda: SC.activation(out=o[0], in_=a[0], func=f, bias=v(bias), scale=v(scale), accum_out=acc[0]), n + 20)
 
     def MM(o, l, r, start, stop):
-        run("t", [o], [l, r], lambda: TE.matmul(o[0], l[0], r[0], start=start, stop=stop), not start)
+        run("t", [o], [l, r], lambda: TE.matmul(o[0], l[0], r[0], start=start, stop=stop), 5 + _C["pe"] * max(64, r[3]) * (4 if r[4] == F32 else 1), not start)
+
+    def MMS(o, *pairs, start=True, stop=True):
+        for k, (l, r) in enumerate(pairs):
+            MM(o, l, r, start and k == 0, stop and k == len(pairs) - 1)
+        part = ops[-len(pairs):]
+        del ops[-len(pairs):]
+
+        def emit():
+            for op in part:
+                op[4]()
+        add("t", "t", part[0][2], [x for op in part for x in op[3]], emit, sum(op[5] for op in part), 0.0, not start)
 
     def IOTA(o, pat, base, cm):
-        run("g", [o], [], lambda: g.iota(o[0], pat, base, cm, allow_small_or_imprecise_dtypes=True))
+        run("g", [o], [], lambda: g.iota(o[0], pat, base, cm, allow_small_or_imprecise_dtypes=True), 130 + 2 * cy * o[3])
 
     def AFF(o, a, pat, op, base, cm):
-        run("g", [o], [a], lambda: g.affine_select(o[0], a[0], pat, op, 0.0, base, cm))
+        run("g", [o], [a], lambda: g.affine_select(o[0], a[0], pat, op, 0.0, base, cm), 170 + 2 * cy * o[3])
 
-    def DMA(q, o, a):
+    def DMA(q, o, a, lat=0.0, after=()):
         os_, is_ = split([o], [a])
-        need(q, os_, is_)
-        sem = "d%d" % no[1]
-        no[1] += 1
-        Q[q].dma_start(o[0], a[0]).then_inc(T.sem[sem], 16)
-        cnt[sem] = 16
-        clk = dict(seen[q])
-        clk[sem] = 16
-        note("dma", sem, 16, clk, os_, is_)
+
+        def emit():
+            need(q, os_, is_)
+            sem = "d%d" % no[1]
+            no[1] += 1
+            Q[q].dma_start(o[0], a[0]).then_inc(T.sem[sem], 16)
+            cnt[sem] = 16
+            clk = dict(seen[q])
+            clk[sem] = 16
+            note("dma", sem, 16, clk, os_, is_)
+        return add(q, "dma", os_, is_, emit, 60.0, _C["dma"] + lat, False, after)
 
     def SEND(srcs, engines, call):
         o, i = split([], srcs)
-        need("g", o, i)
-        call()
-        cnt["loc"] = cnt.get("loc", 0) + engines
-        note("rem", "loc", cnt["loc"], {}, o, i)
 
-    def LAND(dst, sem, val):
-        cnt[sem] = val
-        note("rem", sem, val, {sem: val}, list(dst[1]), [])
+        def emit():
+            need("g", o, i)
+            call()
+            cnt["loc"] = cnt.get("loc", 0) + engines
+            note("rem", "loc", cnt["loc"], {}, o, i)
+        return add("g", "rem", o, i, emit, 400.0, 0.0)
+
+    def LAND(dst, sem, val, sent):
+        def emit():
+            cnt[sem] = val
+            note("rem", sem, val, {sem: val}, list(dst[1]), [])
+        add(None, "rem", list(dst[1]), [], emit, 0.0, _C["rem"], False, (sent,))
+
+    def order():
+        n, book, bank = len(ops), {}, {}
+        pre, suc = [{} for _ in range(n)], [[] for _ in range(n)]
+        for k, (q, aq, o, i, emit, busy, lat, chain, after) in enumerate(ops):
+            for w, regs in ((True, o), (False, i)):
+                for reg in regs:
+                    for rec in book.get(reg[0], ()):
+                        if meets(w, aq if aq != "dma" else q, reg, rec, chain):
+                            j = rec[5]
+                            pre[k][j] = ops[j][6] + (_C["own"] if ops[j][0] == q else _C["hop"])
+            if q == "t":
+                b = o[0][0]
+                if b in bank:
+                    pre[k].setdefault(bank[b], 0.0)
+                bank[b] = k
+            for j in after:
+                pre[k].setdefault(j, 0.0)
+            pre[k].pop(k, None)
+            keep(book, aq, o, i, k)
+            for j in pre[k]:
+                suc[j].append(k)
+        tail = [0.0] * n
+        for k in range(n - 1, -1, -1):
+            tail[k] = ops[k][5] + max([ops[k][6]] + [pre[j][k] + tail[j] for j in suc[k]])
+        back = [{j: pre[j][k] for j in suc[k]} for k in range(n)]
+
+        def place(seq, before, first):
+            start, slots = [0.0] * n, {q: [] for q in Q}
+            for k in seq:
+                q, busy = ops[k][0], ops[k][5]
+                t = max([first[k]] + [start[j] + ops[j][5] + d for j, d in before[k].items()])
+                if q is not None:
+                    sl = slots[q]
+                    at, hi = 0, len(sl)
+                    while at < hi:
+                        mid = (at + hi) // 2
+                        if sl[mid][0] < t:
+                            at = mid + 1
+                        else:
+                            hi = mid
+                    while at < len(sl) and max(t, sl[at - 1][1] if at else 0.0) + busy > sl[at][0]:
+                        at += 1
+                    t = max(t, sl[at - 1][1] if at else 0.0)
+                    sl.insert(at, (t, t + busy))
+                start[k] = t
+            return start
+        seq, best = sorted(range(n), key=lambda k: (-tail[k], k)), None
+        for it in range(_C["passes"]):
+            start = place(seq, pre, [0.0] * n)
+            span = max(start[k] + ops[k][5] + ops[k][6] for k in range(n))
+            if best is None or span < best[0]:
+                best = (span, sorted(range(n), key=lambda k: (start[k], k)))
+            late = place(sorted(range(n), key=lambda k: (-start[k] - ops[k][5], -k)), back, [op[6] for op in ops])
+            seq = sorted(range(n), key=lambda k: (-late[k] - ops[k][5], k))
+        return best[1]
 
     def END():
+        if not _ORDER:
+            _ORDER.extend(order())
+        for k in _ORDER:
+            ops[k][4]()
         for sem in cnt:
             if max(seen[q].get(sem, 0) for q in Q) < cnt[sem]:
                 g.wait_ge(T.sem[sem], cnt[sem])
 
-    return A, X, IND, TT, TS, TC, MS, RED, SCAN, ACT, MM, IOTA, AFF, DMA, SEND, LAND, END
+    return A, X, IND, TT, TS, TC, MS, RED, SCAN, ACT, MM, MMS, IOTA, AFF, DMA, SEND, LAND, LINE, END
 
 
 def rank_program(g, core, T, topo):
     rank = T.rank_of(core)
     if rank is None:
         return
-    A, XT, IND, TT, TS, TC, MS, RED, SCAN, ACT, MM, IOTA, AFF, DMA, SEND, LAND, END = _queues(g, T)
-    CP, RL = AF.Copy, AF.Relu
+    A, XT, IND, TT, TS, TC, MS, RED, SCAN, ACT, MM, MMS, IOTA, AFF, DMA, SEND, LAND, LINE, END = _queues(g, T)
+    CP, RL, IDN = AF.Copy, AF.Relu, AF.Identity
     q6 = (15, 96, 16)
 
-    DMA("y", A("G0", 0, S), XT(T.gd[:, :]))
-    DMA("s", A("wti"), XT(T.wt[:, :]))
-    DMA("s", A("kmi"), XT(T.km[:, :]))
-    DMA("s", A("thi"), XT(T.th[:, :]))
-    DMA("s", A("X", W // 2, W), XT(T.xs[:, W // 2:W]))
-    DMA("y", A("X", 0, W // 2), XT(T.xs[:, 0:W // 2]))
-    DMA("y", A("X0"), XT(T.xs[0::16, :]))
+    d0 = DMA("y", A("GI"), XT(T.gd[:, :]), 800)
+    d1 = DMA("s", A("wti"), XT(T.wt[:, :]))
+    d1 = DMA("s", A("kmi"), XT(T.km[:, :]), 200, [d1])
+    d1 = DMA("s", A("thi"), XT(T.th[:, :]), 400, [d1])
+    d0 = DMA("y", A("X00"), XT(T.xs[0::16, :]), 1400, [d0])
+    DMA("s", A("X", W // 2, W), XT(T.xs[:, W // 2:W]), 7500, [d1])
+    DMA("y", A("X", 0, W // 2), XT(T.xs[:, 0:W // 2]), 7500, [d0])
 
     MS(A("one"), 1.0)
     MS(A("oneb"), 1.0)
@@ -207,152 +323,186 @@ def rank_program(g, core, T, topo):
     AFF(A("GBt"), A("one"), [[-16, 8], [0, 16]], O.is_ge, 0, 1)
     AFF(A("GB"), A("GBt"), [[16, 8], [0, 16]], O.is_ge, 15, -1)
     AFF(A("ID"), A("GB"), [[-1, 128]], O.is_equal, 0, 1)
-    MS(A("WSA"), 0.0)
-    for n, c in enumerate((-4080.0, 383.0 * BIG, 255.0, -1.0, 97.0)):
+    for n, c in enumerate((0.5, 383.0 * BIG, 255.0)):
         MS(A("CB", n, n + 1), c)
     TS(A("pi2"), A("pi"), 15, None, O.bitwise_and)
     TC(A("PI"), A("pi2"))
     TC(A("wtf"), A("wti"))
     TC(A("kmf"), A("kmi"))
-    TS(A("gwA"), A("GB", 0, 128, 16), A("wtf", 0, 1), None, O.mult)
-    MS(A("SEL"), 0.0)
-
-    def spread(dst, src, step):
-        for h in range(8):
-            ACT(A(dst, 16 * h, 16 * h + 129 * 15 + 1, 129), A("oneb", 0, 16), CP, scale=A(src, step * h, step * h + 1))
-    spread("WSA", "gwA", 1)
-
-    def lists(r):
-        G, WS = "G%d" % (r % 2), ("WSA", "WSB")[r % 2]
-        for i in range(16):
-            MM(A("pA", 0, 64), A(WS, 128 * i, 128 * i + 128), A(G, i, S, 16), i == 0, i == 15)
-        TC(A("Ui"), A("pA", 0, 64))
-        TS(A("Um"), A("Ui"), 4095, None, O.bitwise_and)
-        TC(A("Uf"), A("Um"))
-        for m in range(M):
-            ACT(A(("pB", "pM")[m // 4], 64 * (m % 4), 64 * (m % 4) + 64), A("Uf"), CP, scale=A("kmf", m, m + 1))
-        TT(A("UU"), A("Um"), A("Um"), O.mult)
-        TS(A("FQ"), A("UU"), 5, None, O.arith_shift_right)
-        for h in range(2):
-            for m in range(4 * h, 4 * h + 4):
-                TT(A("CA", 64 * m, 64 * m + 64), A(("pB", "pM")[h], 64 * (m % 4), 64 * (m % 4) + 64), A("FQ"), O.add)
-            TS(A("C", 256 * h, 256 * h + 256), A("CA", 256 * h, 256 * h + 256), W - 1, None, O.bitwise_and)
-            TC(A("OFF", 256 * h, 256 * h + 256), A("C", 256 * h, 256 * h + 256))
-            if h == 0 and r:
-                ACT(A("XG"), IND(A("X"), A("OFF", 0, 64)), CP)
-                ACT(A("XH"), IND(A("X"), A("OFF", 96, 128)), CP)
-
-    KB4 = ("pK0", "pK1", "pN", "pM")
-
-    def scores(r):
-        G = "G%d" % (r % 2)
-        for h in range(2):
-            MM(A("pD%d" % h), A("IDb"), A("XG", 512 * h, 512 * h + 512), True, False)
-            MM(A("pD%d" % h), A("IDb"), A(G, 512 * h, 512 * h + 512), False, True)
-        MM(A("pA"), A("IDb"), A("XH"), True, False)
-        MM(A("pA"), A("IDb"), A(G, 512, S), False, True)
-
-        def flag(h):
-            TS(A("FL", 256 * h, 256 * h + 256), A("C", 256 * h, 256 * h + 256), W - 96, None, O.is_ge)
-
-        def keys(m):
-            k = KB4[m % 4]
-            for i in range(16):
-                MM(A(k, 0, 64), A("SEL", 128 * i, 128 * i + 128), A("A%d" % (m % 3), i, S, 16), i == 0, False)
-            MM(A(k, 0, 64), A("IDb"), A("FL", 64 * m, 64 * m + 64), False, m == 0)
-            if m:
-                MM(A(k, 0, 64), A("IDb"), A("M2C", 64 * m, 64 * m + 64), False, True)
-
-        def least(m):
-            if m == 0:
-                TC(A("KM"), A(KB4[0], 0, 64))
-            elif m > 0:
-                TT(A("KM"), A(KB4[m % 4], 0, 64), A("KM"), O.min)
-        for h in range(2):
-            ACT(A("A0", 512 * h, 512 * h + 512), A("pD%d" % h), AF.Abs, bias=A("CB", 0, 1), scale=16.0)
-        ACT(A("A1", 512, S), A("pA"), AF.Abs, bias=A("CB", 0, 1), scale=16.0)
-        for m in range(1, M):
-            for h in range(2 if m == M - 1 else 1):
-                n = S // 2 if m in (1, M - 1) else S
-                a, b = n * h, n * h + n
-                TT(A("D%d" % (m % 3), a, b), IND(A("X"), A("OFF", 64 * m + a // 16, 64 * m + b // 16)), A(G, a, b), O.add)
-                ACT(A("A%d" % (m % 3), a, b), A("D%d" % (m % 3), a, b), AF.Abs, bias=A("CB", 0, 1), scale=16.0)
-            if m == 5 and r == 0:
-                ACT(A("NO"), A("X0"), RL, bias=A("CB", 1, 2), scale=-2 * BIG)
-            if m == 1:
-                flag(0)
-                keys(0)
-            if m == 3:
-                flag(1)
-            keys(m)
-            least(m - 3)
-        least(M - 3)
-        least(M - 2)
-        utable(0)
-        if r:
-            TC(IND(A("FW"), A("ROu")), A("ZR"))
-        least(M - 1)
-
-    def wrap(dst, src, tmp):
-        TT(A(tmp), src, A("MW"), O.mult)
-        SCAN(A(dst), A("RST"), A(tmp), 0.0, O.mult, O.add)
-
-    def utable(k):
-        if k == 0:
-            SCAN(A("UL", s=-1), A("NO", s=-1), A("PL", s=-1), float(W + 1), O.min, O.max)
-            TS(A("OF"), A("I16"), A("UL", 0, 1), None, O.mult)
-            MM(A("pD0", 0, 16), A("GB"), A("OF"), True, True)
-        elif k == 1:
-            TT(A("FM"), A("pD0", 0, 16), A("LM"), O.max)
-        elif k == 2:
-            RED(A("UI"), A("FM"), O.min)
-        else:
-            TS(A("U2"), A("UL"), A("UI"), None, O.min)
-            DMA("y", A("FW", 0, W, rows=slice(0, 128, 16)), A("U2"))
-
-    lists(0)
+    MS(A("TSL"), 0.0)
+    TC(A("TSL", 15, 128, 16), A("GB", 0, 128, 16))
+    for r in range(RO):
+        TS(A("WS%d" % r), A("TSL"), A("wtf", r, r + 1), -1.0, O.mult, O.mult)
+    ACT(A("T32"), A("TSL"), CP, scale=32.0)
+    ACT(A("Tn16"), A("TSL"), CP, scale=-16.0)
+    MMS(A("pN", 0, 3), (A("GB"), A("wtf")))
+    TS(A("CW3"), A("pN", 0, 3), 255.0, None, O.mult)
+    TS(A("G0", 0, S), A("GI"), -1.0, 255.0, O.mult, O.add)
     IOTA(A("QM"), [[0, 6], [1, 16]], 0, 0)
     AFF(A("B0"), A("GB"), [[-16, 8], [0, 16]], O.is_equal, 0, 1)
     AFF(A("USf"), A("GB"), [[-1, 128]], O.is_gt, 0, 1)
+    AFF(A("LSf"), A("GB"), [[1, 128]], O.is_gt, 0, -1)
     IOTA(A("PL0"), [[1, 512]], 2, 0)
     IOTA(A("QB0"), [[16, 6]], 0, 0)
     IOTA(A("BI"), [[1, 64]], 0, 0)
     IOTA(A("i16"), [[1, 16]], 0, 0)
-    IOTA(A("it0"), [[0, 8], [1, 16]], 1, 0)
-    for n, c, base in (("Q0", 96, 0), ("Q1", 96, 1), ("QT", 96, W + CAP + 1), ("ib", 64, 0)):
+    IOTA(A("it0"), [[0, 8], [1, 16]], 0, 0)
+    for n, c, base in (("Q0", 96, 0), ("Q1", 96, 1), ("Q0b", 96, 0)):
         IOTA(A(n), [[1, c]], base, 0)
+    IOTA(A("ROW"), [[16, 65]], -8, 0)
     IOTA(A("SLh"), [[16, 64]], 0, 0)
     IOTA(A("M2C"), [[2, 8], [0, 64]], 0, 0)
-    IOTA(A("FW"), [[0, FWW]], 0, 0)
-    for n, c, base in (("KD", 72, 0), ("PW", 72, -1), ("LWn", 72, 0), ("HX", 72, 0), ("ZR", 96, 0), ("NEG", 512, -1), ("WSB", 2048, 0), ("SI0", 8, 0), ("SI1", 8, 0), ("SI2", 8, 0)):
+    for a in range(0, FWW, FWW // 8):
+        IOTA(A("FW", a, a + FWW // 8), [[0, FWW // 8]], 0, 0)
+    for n, c, base in (("KD", 72, 0), ("PW", 72, -1), ("LWn", 72, 0), ("C8K", 512, W), ("N4", 512, -4), ("TWO", 512, 2), ("CW", 11, 0), ("RSB", 96, -2 ** 22), ("DMP", 96, -1)):
         IOTA(A(n), [[0, c]], base, 0)
-    for n, a, b in (("GQ", 96, 112), ("SPQ", 96, 112), ("STQ", 192, 208)):
-        IOTA(A(n, a, b), [[0, 16]], 0, 0)
-    spread("SEL", "GB", 16)
-    for n, a, c in (("IDb", "ID", 1.0), ("GBb", "GB", 1.0), ("nUS", "USf", -1.0), ("GB32", "GB", 32.0), ("GB8", "GB", 8.0), ("IDB", "ID", BIG)):
+    for n, a, b in (("GQ", 96, 112), ("SPQ", 96, 112), ("STQ", 192, 208), ("G0", S, S + CAP), ("G1", S, S + CAP)):
+        IOTA(A(n, a, b), [[0, b - a]], 0, 0)
+    for n, a, c in (("IDb", "ID", 1.0), ("nIDb", "ID", -1.0), ("GBb", "GB", 1.0), ("nUS", "USf", -1.0), ("GB32", "GB", 32.0), ("nGB8", "GB", -8.0), ("nGB", "GB", -1.0),
+                    ("nB02", "B0", -2.0), ("GBK", "GB", BIG), ("IDK", "ID", BIG), ("IDh", "ID", 0.5)):
         ACT(A(n), A(a), CP, scale=c)
-    ACT(A("XG"), IND(A("X"), A("OFF", 0, 64)), CP)
-    ACT(A("XH"), IND(A("X"), A("OFF", 96, 128)), CP)
+    TS(A("GBt"), A("ID"), 4096.0, None, O.mult)
+    TT(A("LSK"), A("GBt"), A("LSf"), O.add)
     TS(A("th16"), A("thi"), 16.0, None, O.mult)
     TS(A("P512"), A("PI"), 512.0, None, O.mult)
     TS(A("P513"), A("PI"), 512.0, 1.0, O.mult, O.add)
+    TS(A("PIN"), A("PI"), 512.0, 0.4375, O.mult, O.add)
     TS(A("P5K"), A("P513"), 10000.0, None, O.mult)
+    TC(A("M20", 96, 97), A("P513"))
+    TS(A("CB", 4, 5), A("PI"), 2.0, None, O.is_equal)
+    TS(A("LS1"), A("CB", 4, 5), W + 4.0, -float(W), O.mult, O.add)
+    TS(A("LB1"), A("CB", 4, 5), -4.0 - (2 * W - 4608), 2.0 * W - 4608, O.mult, O.add)
     TS(A("PL"), A("PL0"), A("P512"), None, O.add)
-    TS(A("MW"), A("QM"), A("PI"), None, O.is_equal)
-    TS(A("NMW"), A("MW"), -1.0, None, O.mult)
-    TS(A("RST"), A("QM"), 0.0, None, O.is_gt)
+    TS(A("MK"), A("QM"), A("PI"), FAR, O.not_equal, O.mult)
+    MS(A("RSB", 0, 96, 16), 2 * FAR)
+    TS(A("DMP", 0, 96, 16), A("QB0"), A("PI"), W + 1.0, O.add, O.add)
     TS(A("QB"), A("QB0"), A("PI"), 0.5, O.add, O.add)
-    TS(A("QBK"), A("QB"), -97.0, None, O.add)
     TS(A("CB", 5, 6), A("PI"), 1.0 / 1024, None, O.mult)
     TS(A("BI"), A("BI"), 1.0 / 32, A("CB", 5, 6), O.mult, O.add)
     TS(A("I16"), A("i16"), A("PI"), None, O.is_equal)
     TS(A("LM"), A("i16"), A("PI"), BIG, O.is_le, O.mult)
     TS(A("SLi"), A("oneb", 0, 64), A("PI"), None, O.mult)
     TS(A("SLf"), A("SLh"), A("PI"), None, O.add)
-    TT(A("it1"), A("it0"), A("GB"), O.mult)
-    TS(A("IT2"), A("it1"), -1.0, None, O.add)
-    TS(A("gwB"), A("GB", 0, 128, 16), A("wtf", 1, 2), None, O.mult)
-    TS(A("gwA"), A("GB", 0, 128, 16), A("wtf", 2, 3), None, O.mult)
+    TS(A("GBt"), A("GB"), 8192.0, -8192.0 - 7.5, O.mult, O.add)
+    TT(A("ITH"), A("GBt"), A("it0"), O.add)
+    TC(A("XF"), A("X00"))
+    DMA("y", A("FW", 1, W + 1, rows=slice(1, 128, 16)), A("XF"), 500)
+
+    def sel(n, i):
+        return A(n, 15 - i, 143 - i)
+
+    def lists(r):
+        G = "G%d" % (r % 2)
+        MMS(A("pA", 0, 64), *[(sel("WS%d" % r, i), A(G, i, S, 16)) for i in range(16)])
+        TS(A("Ui"), A("pA", 0, 64), A("CW3", r, r + 1), None, O.add)
+        TS(A("Um"), A("Ui"), 4095, None, O.bitwise_and)
+        TC(A("Uf"), A("Um"))
+        TT(A("UU"), A("Um"), A("Um"), O.mult)
+        TS(A("FQ"), A("UU"), 5, None, O.arith_shift_right)
+        banks = {0: ("pB", 0), 1: ("pM", 0), 2: ("pM", 1), 3: ("pM", 2), 4: ("pN", 0), 5: ("pN", 1), 6: ("pK0", 0), 7: ("pK0", 1)}
+        for m in range(M):
+            ACT(A(banks[m][0], 64 * banks[m][1], 64 * banks[m][1] + 64), A("Uf"), CP, scale=A("kmf", m, m + 1))
+            LINE("s")
+
+        def sums(m):
+            TT(A("CA", 64 * m, 64 * m + 64), A(banks[m][0], 64 * banks[m][1], 64 * banks[m][1] + 64), A("FQ"), O.add)
+
+        def rest(a, b):
+            TS(A("C", 64 * a, 64 * b), A("CA", 64 * a, 64 * b), W - 1, None, O.bitwise_and)
+
+        def offs(a, b):
+            TC(A("OFF", 64 * a, 64 * b), A("C", 64 * a, 64 * b))
+
+        def flag(a, b):
+            TS(A("FL", 64 * a, 64 * b), A("OFF", 64 * a, 64 * b), W - 96.0, None, O.is_ge)
+        for f, *args in ((sums, 0), (rest, 0, 1), (offs, 0, 1), (sums, 1), (sums, 2), (sums, 3), (sums, 4), (sums, 5), (sums, 6), (sums, 7), (rest, 4, 8),
+                         (rest, 1, 4), (offs, 4, 8), (offs, 1, 4), (flag, 4, 8), (flag, 0, 4)):
+            f(*args)
+            LINE("v")
+
+    def scores(r):
+        G = "G%d" % (r % 2)
+        left = [M] * 64
+
+        held = {}
+
+        def opens(u, D):
+            a, b, bank, at = u
+            MMS(A(bank, at, at + b - a), (A("IDb"), A("M2C", a, b)), (A("IDb"), A("FL", a, b)),
+                *[(sel("Tn16", i), A(D, i, 16 * (b - a), 16)) for i in range(16 if D else 0)], stop=False)
+
+        def closes(u, R):
+            a, b, bank, at = u
+            MMS(A(bank, at, at + b - a), *[(sel("T32", i), A(R, i, 16 * (b - a), 16)) for i in range(16)], start=False)
+            held.setdefault(bank, []).append(u)
+            if len(held[bank]) < sum(1 for x in BY_S + BY_V if x[2] == bank):
+                return
+            for a, b, bank, at in held[bank]:
+                c = a
+                while c < b:
+                    e = c + 1
+                    while e < b and e % 64 and left[e % 64] == left[c % 64]:
+                        e += 1
+                    key, c0, c1 = A(bank, at + c - a, at + e - a), c % 64, c % 64 + e - c
+                    if left[c0] == M:
+                        TS(A("KM", c0, c1), key, FAR, None, O.min)
+                    else:
+                        TT(A("KMi" if left[c0] == 1 else "KM", c0, c1), key, A("KM", c0, c1), O.min)
+                    for x in range(c0, c1):
+                        left[x] -= 1
+                    c = e
+
+        def v_get(k, u):
+            cut = [u[0]] + [c for c in range(u[0] + 1, u[1]) if c % 64 == 0] + [u[1]]
+            for a, b in zip(cut, cut[1:]):
+                TT(A("D%d" % (k % 2), 16 * (a - u[0]), 16 * (b - u[0])), IND(A("X"), A("OFF", a, b)), A(G, 16 * (a % 64), 16 * (a % 64 + b - a)), O.subtract)
+                LINE("v")
+            opens(u, "D%d" % (k % 2))
+
+        def v_cut(k, u):
+            n = 16 * (u[1] - u[0])
+            TS(A("R%d" % (k % 2), 0, n), A("D%d" % (k % 2), 0, n), 0.0, None, O.max)
+            LINE("v")
+            closes(u, "R%d" % (k % 2))
+
+        def s_get(k, j, u, h, e):
+            xg = A("XG%d" % (k % 2), 16 * (h - u[0]), 16 * (e - u[0]))
+            ACT(xg, IND(A("X"), A("OFF", h, e)), CP)
+            LINE("s")
+            MMS(A("pD%d" % (j % 2), 0, 16 * (e - h)), (A("nIDb"), A(G, 16 * (h % 64), 16 * (h % 64 + e - h))), (A("IDb"), xg))
+
+        def s_cut(k, j, u, h, e):
+            ACT(A("AB%d" % (k % 2), 16 * (h - u[0]), 16 * (e - u[0])), A("pD%d" % (j % 2), 0, 16 * (e - h)), AF.Abs, scale=0.5)
+            LINE("s")
+            if e == u[1]:
+                opens(u, None)
+                closes(u, "AB%d" % (k % 2))
+        steps = []
+        halves = [(k, u, h, min(u[1], h + 32)) for k, u in enumerate(BY_S) for h in range(u[0], u[1], 32)]
+        for q, t, gets, cuts in (("v", _C["vlate"], [(v_get, (k, u), 24 * (u[1] - u[0])) for k, u in enumerate(BY_V)], [(v_cut, (k, u), 8 * (u[1] - u[0])) for k, u in enumerate(BY_V)]),
+                                 ("s", 0.0, [(s_get, (k, j, u, h, e), 24 * (e - h)) for j, (k, u, h, e) in enumerate(halves)],
+                                  [(s_cut, (k, j, u, h, e), 16 * (e - h)) for j, (k, u, h, e) in enumerate(halves)])):
+            line = gets[:1] + [x for pair in zip(gets[1:], cuts) for x in pair] + cuts[-1:]
+            if q == "v":
+                line[-3:-1] = line[-2:-4:-1]
+            for f, args, n in line:
+                t += n
+                steps.append((t, len(steps), f, args))
+        for t, k, f, args in sorted(steps, key=lambda x: x[:2]):
+            f(*args)
+
+    def own(dst, bank):
+        SCAN(A(dst), A("RSB"), A(bank, 0, 96), 0.0, O.max, O.min)
+
+    def utable(r):
+        ACT(A("NO"), A("X0%d" % r), RL, bias=A("CB", 1, 2), scale=-2 * BIG)
+        SCAN(A("UL", s=-1), A("NO", s=-1), A("PL", s=-1), float(W + 1), O.min, O.max)
+        TS(A("OF"), A("I16"), A("UL", 0, 1), None, O.mult)
+        MMS(A("pK0", 128, 144), (A("GB"), A("OF")))
+        TT(A("FM"), A("pK0", 128, 144), A("LM"), O.max)
+        RED(A("UI"), A("FM"), O.min)
+        TS(A("U2"), A("UL"), A("UI"), None, O.min)
+        DMA("y", A("FW", 0, W, rows=slice(0, 128, 16)), A("U2"), 500)
 
     near, far = T.cores[rank ^ 1], T.cores[rank ^ 2]
 
@@ -361,183 +511,164 @@ def rank_program(g, core, T, topo):
         return RemoteDMATransfer(dst_ids=[DstId(rid=rid, pnc=pid)], dma_engine_mask=sum(1 << e for e in eng), remote_sem=T.sem[sem], src=src[0], dst=out[0])
     en, ef = topo.engines(core, near), topo.engines(core, far)
     hn = len(en) // 2
+    mk = (A("IDb"), A("MK"))
 
-    for r in range(RO):
+    def one_round(r):
         last = r == RO - 1
-        G, H = "G%d" % (r % 2), "G%d" % ((r + 1) % 2)
-        SI, SP, STn, RI, RJ, Z, SG = ("%s%d" % (n, r) for n in ("SI", "SP", "ST", "RI", "RJ", "Z", "SG"))
-        if r:
-            lists(r)
+        G, H = "G%d" % (r % 2), "YG" if last else "G%d" % ((r + 1) % 2)
+        RK, SP, STn, RI, RJ, Z, M2, M3 = ("%s%d" % (n, k) for n, k in (("RK", r), ("SP", r), ("ST", r), ("RI", r), ("RJ", r), ("Z", r), ("M2", r), ("M2", r + 1)))
+        lists(r)
         scores(r)
-        if r == 0:
-            for n, a, c in (("nB02", "B0", -2.0), ("nIDBb", "ID", -BIG), ("nIDb", "ID", -1.0), ("GBK", "GB", BIG), ("IDK", "ID", BIG),
-                            ("ID2b", "ID", 2.0), ("ID3b", "ID", 3.0)):
-                ACT(A(n), A(a), CP, scale=c)
-        TC(A("KMi"), A("KM"))
-        TS(A("F0"), A("KM"), A("th16"), None, O.is_lt)
-        utable(1)
+        utable(r)
         TS(A("PAR"), A("KMi"), 1, None, O.bitwise_and)
-        TS(A("MX"), A("KMi"), 14, None, O.bitwise_and)
+        TS(A("F0"), A("KMi"), A("th16"), None, O.is_lt)
         TT(A("FIT"), A("F0"), A("PAR"), O.is_gt)
-        utable(2)
-        TS(A("KD", 0, 64), A("KMi"), 65520, None, O.bitwise_and)
-        SCAN(A("CS"), A("one", 0, 64), A("FIT"), 0.0, O.mult, O.add)
-        MM(A("pB", 0, 64), A("GBb"), A("CS"), True, True)
-        MM(A("pM", 0, 64), A("GBb"), A("CS"), True, False)
-        MM(A("pM", 0, 64), A("nUS"), A("FIT"), False, True)
-        MM(A("pN", 0, 64), A("GBb"), A("CS"), True, True)
+        SCAN(A("CS"), A("oneb", 0, 64), A("FIT"), 0.0, O.mult, O.add)
+        MMS(A("pB", 0, 64), (A("GBb"), A("CS")))
+        MMS(A("pM", 0, 64), (A("GBb"), A("CS")), (A("nUS"), A("FIT")))
+        MMS(A("pM", 64, 66), (A("GBb"), A("CS", 62, 64)))
         for a in range(6):
             ACT(A("JK", 64 * a, 64 * a + 64), A("pB", 0, 64), AF.Sign, bias=A("QB", a, a + 1), scale=-1.0, acc=A("BQ", a, a + 1))
-        if last:
-            MM(A("pK1"), A("IDb"), A("SG1"), True, False)
-            MM(A("pK1"), A("nIDb"), A("SG0"), False, True)
-            ACT(A("N1"), A("pK1"), RL)
-        if not last:
-            spread(("WSB", "WSA")[r], ("gwB", "gwA")[r], 1)
-        utable(3)
+        TS(A("MX"), A("KMi"), 14, None, O.bitwise_and)
+        TS(A("KD", 0, 64), A("KMi"), 65520, None, O.bitwise_and)
         TT(A("LWn", 0, 64), A("MX"), A("BI"), O.add)
         TT(A("PW", 0, 64), A("pM", 0, 64), A("FIT"), O.mult)
-        TS(A("INVb"), A("Q0"), A("pN", 63, 64), None, O.is_ge)
-        TS(A("INV"), A("INVb"), 2.0 ** -14, None, O.add)
+        TS(A("INV"), A("Q0"), A("pM", 65, 66), 2.0 ** -14, O.is_ge, O.add)
+        inv = (A("IDK"), A("INV"))
         TS(A("BQo"), A("BQ"), 0.5, 32.0, O.mult, O.add)
         TT(A("OH"), IND(A("PW"), A("BQo")), A("Q1"), O.is_equal)
         TT(A("LG"), IND(A("LWn"), A("BQo")), A("OH"), O.mult)
-        MM(A("pA", 0, 96), A("GB32"), A("LG"), True, True)
+        MMS(A("pA", 0, 96), mk, (A("GB32"), A("LG")))
         TT(A("KG"), IND(A("KD"), A("BQo")), A("OH"), O.mult)
-        MM(A("pK0", 0, 96), A("GB8"), A("KG"), True, False)
-        MM(A("pK0", 0, 96), A("ID"), A("Q0"), False, True)
-        TS(A("T1"), A("BQ"), 8.0, 608.0, O.mult, O.add)
-        wrap("SL", A("pA", 0, 96), "WL")
+        own("SL", "pA")
         TC(A("LO"), A("SL", *q6))
-        TT(A("WK"), A("pK0", 0, 96), A("NMW"), O.mult)
+        MMS(A("pK0", 0, 96), mk, (A("nIDb"), A("Q0b")), (A("nGB8"), A("KG")))
+        MMS(A("pK1", 0, 96), (A("nIDb"), A("Q0b")), (A("nGB8"), A("KG")))
         TT(A("CG"), IND(A("C"), A("LO")), A("OH"), O.mult)
-        MM(A("pA", 0, 96), A("GB"), A("CG"), True, False)
-        MM(A("pA", 0, 96), A("IDB"), A("INV"), False, True)
-        SCAN(A("SK"), A("RST"), A("WK"), 0.0, O.mult, O.add)
+        MMS(A("pA", 0, 96), mk, inv, (A("GB"), A("CG")))
+        MMS(A("pB", 0, 96), inv, (A("GB"), A("CG")))
+        own("SK", "pK0")
         for a in range(6):
-            ACT(A("SGN", 96 * a, 96 * a + 96), A("pK0", 0, 96), AF.Sign, bias=A("SK", 16 * a + 15, 16 * a + 16))
-        TS(A("XA"), A("SL", *q6), 32.0, None, O.mult)
-        wrap("SC", A("pA", 0, 96), "WC")
+            ACT(A("SGN", 96 * a, 96 * a + 96), A("pK1", 0, 96), AF.Sign, bias=A("SK", 16 * a + 15, 16 * a + 16), scale=-1.0)
+        own("SC", "pA")
         for a in range(6):
             ACT(A("KB", 96 * a, 96 * a + 96), A("SGN", 96 * a, 96 * a + 96), CP, scale=A("SC", 16 * a + 15, 16 * a + 16))
         TS(A("UO"), A("SC", *q6), 15.0, W - 1.0, O.add, O.min)
-        TS(A("XI"), A("XA"), 2047, None, O.bitwise_and)
         TC(A("EG"), IND(A("FW"), A("UO")))
-        MM(A("pM", 0, 96), A("B0"), A("EG"), True, True)
-        TT(A("T2"), A("XI"), A("T1"), O.subtract)
-        TS(A("PO"), A("SC", *q6), 9.0, W - 1.0, O.add, O.min)
-
-        def same(a):
-            TT(A("KL", 96 * a, 96 * a + 96), A("KB", 96 * a, 96 * a + 96), A("pA", 0, 96), O.is_equal)
-            MM(A("pK1", 0, 96), A("GBK"), A("KL", 96 * a, 96 * a + 96), a == 0, False)
-        TS(A("SQ"), A("T2"), 96.0, None, O.add)
-        TS(A("C6"), A("SC", *q6), -1.0, W - 1.0, O.add, O.min)
-        wrap("S1", A("pM", 0, 96), "W1")
+        MMS(A("pM", 0, 96), mk, (A("B0"), A("EG")))
+        own("S1", "pM")
         TS(A("UO2"), A("S1", *q6), 6.0, W - 1.0, O.add, O.min)
         TC(A("EG2"), IND(A("FW"), A("UO2")))
-        MM(A("pN", 0, 96), A("B0"), A("EG2"), True, True)
-        ACT(A("PG"), IND(A("X"), A("PO")), CP)
-        ACT(A("PN"), A("PG"), RL, scale=-1.0)
-        MM(A("pD0", 0, 96), A("nIDb"), A("PG"), True, False)
-        MM(A("pD0", 0, 96), A("nB02"), A("PN"), False, True)
-        for a in range(4):
-            same(a)
-        TT(A("W2"), A("pN", 0, 96), A("MW"), O.mult)
-        same(4)
-        SCAN(A("S2"), A("RST"), A("W2"), 0.0, O.mult, O.add)
-        same(5)
-        MM(A("pK1", 0, 96), A("IDK"), A("INVb"), False, True)
+        MMS(A("pN", 0, 96), mk, (A("B0"), A("EG2")))
+        own("S2", "pN")
         TS(A("TO", 0, 6), A("S1", *q6), -2.0, None, O.add)
         TS(A("TO", 6, 12), A("S2", *q6), -2.0, None, O.add)
-        ACT(A("CR"), A("pA", 0, 96), CP)
-        ACT(A("M1"), A("CR"), RL, bias=A("P5K"), scale=-10000.0)
+        TS(A("PO"), A("SC", *q6), 9.0, W - 1.0, O.add, O.min)
+        ACT(A("PG"), IND(A("X"), A("PO")), CP)
+        ACT(A("PN"), A("PG"), RL, scale=-1.0)
+        MMS(A("pD0", 0, 96), (A("nIDb"), A("PG")), (A("nB02"), A("PN")))
         ACT(A("SPQ", 0, 96), A("pD0", 0, 96), RL, bias=A("CB", 2, 3))
+        MMS(A("pD0", 96, 192), (A("nGB"), A("CG")), (A("B0"), A("EG2")))
+        ACT(A("LEN"), A("pD0", 96, 192), IDN, bias=A("LB1"), scale=A("LS1"))
+        MMS(A("pM", 96, 192), (A("B0"), A("EG2")))
         ACT(A("TG"), IND(A("X"), A("TO")), CP)
         ACT(A("TN"), A("TG"), RL, scale=-1.0)
-        MM(A("pD1", 0, 192), A("nIDb"), A("TG"), True, False)
-        MM(A("pD1", 0, 192), A("nB02"), A("TN"), False, True)
-        TT(A("NCQ"), A("pK1", 0, 96), A("QT"), O.min)
-        TS(A("CUT"), A("NCQ"), 0.5, None, O.is_lt)
-        SCAN(A("RK"), A("one", 0, 96), A("CUT"), -97.0, O.mult, O.add)
-        ACT(A(SI, 0, 1), A("RK", 95, 96), AF.Identity, bias=A("CB", 4, 5))
-        ACT(A(SI, 7, 8), A("RK", 95, 96), AF.Identity, bias=A("CB", 3, 4), scale=-1.0)
-        SEND([A(SI)], 2 * hn, lambda: g.remote_dma_fused([to(near, en[:hn], "ai%d" % r, A(SI), A(RI)), to(far, ef[hn:], "aj%d" % r, A(SI), A(RJ))], local_sem=T.sem["loc"]))
-        for a in range(6):
-            ACT(A("JL", 96 * a, 96 * a + 96), A("RK"), AF.Sign, bias=A("QBK", a, a + 1), scale=-1.0, acc=A("BK", a, a + 1))
+        MMS(A("pD1", 0, 192), (A("nIDb"), A("TG")), (A("nB02"), A("TN")))
         ACT(A("STQ", 0, 192), A("pD1", 0, 192), RL, bias=A("CB", 2, 3))
-        TT(A("CD"), A("NCQ"), A("RK"), O.add)
-        TT(A("LEN"), A("pN", 0, 96), A("CR"), O.subtract)
-        TT(A("WD"), A("CD"), A("MW"), O.mult)
-        SCAN(A("SD"), A("RST"), A("WD"), 0.0, O.mult, O.add)
-        TT(A("R6"), A("C6"), A("SD", *q6), O.max)
-        TT(A("VV"), A("T2"), A("SD", *q6), O.subtract)
+        TS(A("T1"), A("BQ"), 8.0, 512.0 - 4088.5, O.mult, O.add)
+        TS(A("XA"), A("SL", *q6), 32.0, None, O.mult)
+        TS(A("XI"), A("XA"), 2047, None, O.bitwise_and)
+        TT(A("T2"), A("XI"), A("T1"), O.subtract)
+        TS(A("SQ"), A("T2"), -4088.5, None, O.add)
+        ACT(A("GQ", 0, 96), IND(A(G, 0, S), A("SQ")), CP)
+        MM(A("pK0", 0, 96), *mk, True, False)
+        MM(A("pK0", 0, 96), *inv, False, False)
+        MM(A("pK0", 0, 96), A("GB"), A("CG"), False, False)
+        MM(A("pK1", 0, 96), *inv, True, False)
+        for a in range(6):
+            TT(A("KL", 96 * a, 96 * a + 96), A("KB", 96 * a, 96 * a + 96), A("pB", 0, 96), O.is_equal)
+            MM(A("pK1", 0, 96), A("GBK"), A("KL", 96 * a, 96 * a + 96), False, a == 5)
+            MM(A("pK0", 0, 96), A("GBK"), A("KL", 96 * a, 96 * a + 96), False, a == 5)
+        TS(A("CUT"), A("pK1", 0, 96), 1.5, None, O.is_lt)
+        SCAN(A(RK), A("one", 0, 96), A("CUT"), 0.0, O.mult, O.add)
+        cnts = A(RK, 88, 96)
+        k = SEND([cnts], 2 * hn, lambda: g.remote_dma_fused([to(near, en[:hn], "ai%d" % r, cnts, A(RI)), to(far, ef[hn:], "aj%d" % r, cnts, A(RJ))], local_sem=T.sem["loc"]))
+        LAND(A(RI), "ai%d" % r, hn, k)
+        LAND(A(RJ), "aj%d" % r, len(ef) - hn, k)
+        for a in range(6):
+            ACT(A("JL", 96 * a, 96 * a + 96), A(RK), AF.Sign, bias=A("QB", a, a + 1), scale=-1.0, acc=A("BK", a, a + 1))
         TS(A("KIu", 0, 6), A("BK"), 0.5, 48.0, O.mult, O.add)
         TS(A("KIu", 6, 12), A("BK"), 0.5, 144.0, O.mult, O.add)
         ACT(A(SP), IND(A("SPQ"), A("KIu", 0, 6)), CP)
-        SEND([A(SP)], len(en), lambda: g.remote_dma_fused([to(near, en, "ap%d" % r, A(SP), A(Z, 0, 96))], local_sem=T.sem["loc"]))
+        k = SEND([A(SP)], len(en), lambda: g.remote_dma_fused([to(near, en, "ap%d" % r, A(SP), A(Z, 0, 96))], local_sem=T.sem["loc"]))
+        LAND(A(Z, 0, 96), "ap%d" % r, len(en), k)
         ACT(A(STn), IND(A("STQ"), A("KIu")), CP)
-        SEND([A(STn)], len(ef), lambda: g.remote_dma_fused([to(far, ef, "at%d" % r, A(STn), A(Z, 96, 288))], local_sem=T.sem["loc"]))
-        ACT(A("GQ", 0, 96), IND(A(G, 0, S), A("SQ")), CP)
+        k = SEND([A(STn)], len(ef), lambda: g.remote_dma_fused([to(far, ef, "at%d" % r, A(STn), A(Z, 96, ARR))], local_sem=T.sem["loc"]))
+        LAND(A(Z, 96, ARR), "at%d" % r, len(ef), k)
         ACT(A(G, S, S + CAP), IND(A("GQ"), A("KIu", 0, 6)), CP)
-        TC(A("ROu"), A("R6"))
-        TS(A("BII", 0, 6), A("VV"), 16383, 4, O.bitwise_and, O.arith_shift_right)
-        TS(A("BII", 6, 12), A("VV"), 15, None, O.bitwise_and)
-        LAND(A(RI), "ai%d" % r, hn)
-        LAND(A(RJ), "aj%d" % r, len(ef) - hn)
-        LAND(A(Z, 0, 96), "ap%d" % r, len(en))
-        LAND(A(Z, 96, 288), "at%d" % r, len(ef))
+        SCAN(A("R6"), A("DMP"), A("pK0", 0, 96), 0.0, O.max, O.min)
+        TC(A("ROu"), A("R6", *q6))
         TC(IND(A("FW"), A("ROu")), A("LEN"))
-        DMA("y", A("LW"), A("FW", 0, W, rows=slice(1, 128, 16)))
-        TC(A("BIF"), A("BII"))
-        for a in range(6):
-            ACT(A("EA", 64 * a, 64 * a + 64), A("ib"), AF.Abs, bias=A("BIF", a, a + 1), scale=-1.0)
-        ACT(A("EB"), A("EA"), RL, bias=A("one", 0, 1), scale=-1.0)
-        for a in range(6):
-            TS(A("TA", 128 * a, 128 * a + 128), A("IT2"), A("BIF", 6 + a, 7 + a), None, O.is_ge)
-            if a == 1:
-                TT(A("M2"), A("pN", 0, 96), A("M1"), O.min)
-            if a == 3:
-                RED(A("RD"), A("M2"), O.max)
-        TS(A("IN"), A("RD"), A("P512"), 0.0, O.subtract, O.max)
-        for a in range(6):
-            MM(A("pB", 0, 64), A("GBb"), A("EB", 64 * a, 64 * a + 64), a == 0, a == 5)
-        MM(A("pA", 0, 64), A("IDb"), A("SLh"), True, False)
-        MM(A("pA", 0, 64), A("IDb"), A("SLi"), False, False)
-        for a in range(6):
-            MM(A("pA", 0, 64), A("TA", 128 * a, 128 * a + 128), A("EB", 64 * a, 64 * a + 64), False, a == 5)
-        SCAN(A("HX", 1, 65), A("one", 0, 64), A("pB", 0, 64), 0.0, O.mult, O.add)
-        TT(A("IX"), A("pA", 0, 64), A("HX", 0, 64), O.add)
-        TC(A("IXu"), A("IX"))
-        ACT(A(Z, 288, 288 + S), IND(A(G, 0, S + CAP), A("IXu")), CP)
-        TT(A("NT1"), A(RI, 0, 1), A(RJ, 0, 1), O.add)
-        TS(A("F1"), A("SLf"), A(RI, 0, 1), A(RI, 7, 8), O.is_ge, O.mult)
-        TT(A("NT2"), A("NT1"), A(RJ, 0, 1), O.add)
-        TS(A("F2"), A("SLf"), A("NT1"), A(RJ, 7, 8), O.is_ge, O.mult)
-        TS(A("F3"), A("SLf"), A("NT2"), A(RJ, 7, 8), O.is_ge, O.mult)
-        SCAN(A("ST"), A("NEG"), A("LW"), A("IN"), O.add, O.max)
-        ACT(A(SG), A("ST"), AF.Sign)
-        for k, n in enumerate(("SLh", "SLi", "F1", "F2", "F3")):
-            MM(A("pM", 0, 64), A("IDb"), A(n), k == 0, k == 4)
-        if not last:
-            MM(A("pK0"), A("IDb"), A("X0"), True, False)
-            MM(A("pK0"), A("nIDBb"), A(SG), False, True)
-        TC(A("FX"), A("pM", 0, 64))
-        TC(A(H, 0, S // 2), IND(A(Z), A("FX", 0, 32)))
-        ACT(A(H, S // 2, S), IND(A(Z), A("FX", 32, 64)), CP)
+        DMA("y", A("LW"), A("FW", 1, W + 1, rows=slice(2 if last else 1, 128, 16)), 800)
+        ACT(A("M1"), A("pB", 0, 96), RL, bias=A("P5K"), scale=-10000.0)
+        TT(A(M2, 0, 96), A("pM", 96, 192), A("M1"), O.min)
+        RED(A(M3, 96, 97), A(M2), O.max)
         if last:
-            DMA("y", XT(T.yg[:, :]), A(H, 0, S))
+            TS(A("IN"), A(M3, 96, 97), A("P512"), 4.0, O.subtract, O.mult)
+            for k in range(2):
+                ACT(A("SG%d" % k), A("X0%d" % (k + 1)), AF.Sign, bias=A("CB", 0, 1))
+            MMS(A("pD1"), (A("IDb"), A("TWO")), (A("IDh"), A("SG0")), (A("IDh"), A("SG1")))
+            SCAN(A("STT"), A("N4"), A("LW"), A("IN"), O.add, O.max)
+            TT(A("YC"), A("STT"), A("pD1"), O.min)
+            DMA("s", XT(T.yc[:, :]), A("YC"), 800)
         else:
-            TC(A("X0"), A("pK0"))
-            ACT(A("NO"), A("X0"), RL, bias=A("CB", 1, 2), scale=-2 * BIG)
-            DMA("y", A("X", 0, W, rows=slice(0, 128, 16)), A("X0"))
+            X1 = "X0%d" % (r + 1)
+            TS(A("IN"), A(M3, 96, 97), A("PIN"), -float(W), O.subtract, O.mult)
+            SCAN(A(X1), A("C8K"), A("LW"), A("IN"), O.add, O.min)
+            DMA("y", A("X", 0, W, rows=slice(0, 128, 16)), A(X1), 400)
+        TS(A("CW", 5, 11), A("R6", *q6), W + 0.5, None, O.is_lt)
+        MMS(A("pN", 0, 6), (A("LSK"), A("CW", 5, 11)), *[(A("GBb"), A("CW", 5 - s, 11 - s)) for s in range(1, 6)])
+        TT(A("VV"), A("T2"), A("pN", 0, 6), O.subtract)
+        TS(A("VR"), A("VV"), 1.5 * 2 ** 27, -1.5 * 2 ** 27, O.add, O.add)
+        for a in range(6):
+            TS(A("LE", 65 * a, 65 * a + 65), A("ROW"), A("VV", a, a + 1), None, O.is_ge)
+        TT(A("EQ", 0, 389), A("LE", 1, 390), A("LE", 0, 389), O.subtract)
+        for a in range(6):
+            TS(A("TA", 128 * a, 128 * a + 128), A("ITH"), A("VR", a, a + 1), A("VV", a, a + 1), O.add, O.is_ge)
+        MMS(A("pA", 0, 64), (A("IDb"), A("SLh")), (A("IDb"), A("SLi")), *([(A("GBb"), A("LE", 65 * a, 65 * a + 64)) for a in range(6)]
+                                                                         + [(A("TA", 128 * a, 128 * a + 128), A("EQ", 65 * a, 65 * a + 64)) for a in range(6)]))
+        TC(A("IXu"), A("pA", 0, 64))
+
+        def turn(q, out, win, off, flip):
+            if q == "v" and flip:
+                TS(out, IND(win, off), -1.0, 255.0, O.mult, O.add)
+            elif q == "v":
+                TC(out, IND(win, off))
+            elif flip:
+                ACT(out, IND(win, off), IDN, bias=A("CB", 2, 3), scale=-1.0)
+            else:
+                ACT(out, IND(win, off), CP)
+        turn("v", A(Z, ARR, ARR + 512), A(G), A("IXu", 0, 32), True)
+        turn("s", A(Z, ARR + 512, ARR + S), A(G), A("IXu", 32, 64), True)
+        n1, n2 = A(RI, 7, 8), A(RJ, 7, 8)
+        TT(A("NT", 0, 1), n1, n2, O.add)
+        TT(A("NT", 1, 2), A("NT", 0, 1), n2, O.add)
+        TS(A("FX", 18, 64), A("SLf", 18, 64), A("NT", 1, 2), None, O.subtract)
+        turn("v", A(H, ARR, 640), A(Z, ARR, ARR + S), A("FX", 18, 40), not last)
+        turn("s", A(H, 640, S), A(Z, ARR, ARR + S), A("FX", 40, 64), not last)
+        TS(A("NM", 0, 1), n1, -1.0, float(CAP), O.mult, O.add)
+        TS(A("NM", 1, 2), n2, -1.0, float(CAP), O.mult, O.add)
+        TS(A("F1"), A("SLf", 0, 18), n1, A("NM", 0, 1), O.is_ge, O.mult)
+        TS(A("F2"), A("SLf", 0, 18), A("NT", 0, 1), A("NM", 1, 2), O.is_ge, O.mult)
+        TS(A("F3"), A("SLf", 0, 18), A("NT", 1, 2), A("NM", 1, 2), O.is_ge, O.mult)
+        MMS(A("pB", 0, 18), *[(A("IDb"), A(n, 0, 18)) for n in ("SLh", "SLi", "F1", "F2", "F3")])
+        TC(A("FX", 0, 18), A("pB", 0, 18))
+        turn("v", A(H, 0, 160), A(Z), A("FX", 0, 10), not last)
+        turn("s", A(H, 160, ARR), A(Z), A("FX", 10, 18), not last)
         if last:
-            MM(A("pK1"), A("IDb"), A(SG), True, False)
-            MM(A("pK1"), A("nIDb"), A("SG0"), False, False)
-            MM(A("pK1"), A("nIDb"), A("N1"), False, True)
-            ACT(A("N2"), A("pK1"), RL)
-            MM(A("pD0"), A("IDb"), A("SG0"), True, False)
-            MM(A("pD0"), A("ID2b"), A("N1"), False, False)
-            MM(A("pD0"), A("ID3b"), A("N2"), False, True)
-            ACT(A("YC"), A("pD0"), CP)
-            DMA("s", XT(T.yc[:, :]), A("YC"))
+            DMA("y", XT(T.yg[:, ARR:S]), A(H, ARR, S), 500)
+            DMA("y", XT(T.yg[:, 0:ARR]), A(H, 0, ARR), 300)
+
+    for r in range(RO):
+        one_round(r)
     END()

@@ -1,3 +1,4 @@
+import numpy as np
 from concourse.bass import DstId, RemoteDMATransfer
 from concourse.mybir import AluOpType as O, ActivationFunctionType as AF, AxisListType
 
@@ -5,9 +6,10 @@ W, S, M, CAP, RO = 8192, 1024, 8, 96, 3
 BIG = 16384.0
 FWW = W + 112
 ARR = 3 * CAP
+STEP = 2.0 ** 18
 FAR = 2.0 ** 20
 
-F32, B16, I32, U16 = "float32", "bfloat16", "int32", "uint16"
+F32, B16, F16, I32, U16 = "float32", "bfloat16", "float16", "int32", "uint16"
 _OWN = {
     "X": (W, B16), "FW": (FWW, F32), "GI": (S, B16), "G0": (S + CAP, B16), "G1": (S + CAP, B16), "YG": (S, B16),
     "wti": (3, I32), "kmi": (8, I32), "thi": (1, I32), "LW": (512, F32), "U2": (512, F32), "YC": (512, F32), "XF": (512, F32),
@@ -17,21 +19,22 @@ for _r in range(RO):
     _OWN.update({"X0%d" % _r: (512, B16), "RK%d" % _r: (96, F32), "SP%d" % _r: (96, B16), "ST%d" % _r: (192, B16), "RI%d" % _r: (8, F32), "RJ%d" % _r: (8, F32),
                  "Z%d" % _r: (ARR + S, B16)})
 _PART = {
-    F32: {"wtf": 3, "kmf": 8, "th16": 1, "one": 128, "GB": 128, "GBt": 128, "nGB": 128, "nGB8": 128, "GB32": 128, "B0": 128, "ID": 128, "USf": 128, "LSf": 128,
+    F32: {"wtf": 3, "kmf": 8, "th16": 1, "one": 128, "GB": 128, "GBt": 128, "nGB": 128, "nGB8": 128, "SI": 96, "B0": 128, "ID": 128, "USf": 128, "LSf": 128,
           "PI": 1, "P512": 1, "P513": 1, "P5K": 1, "PIN": 1, "LS1": 1, "LB1": 1, "CB": 16, "CW3": 3, "QM": 96, "MW": 96, "RSB": 96, "DMP": 96, "Q0": 96, "Q1": 96, "BI": 64, "QB0": 6, "QB": 6,
-          "BK": 6, "i16": 16, "I16": 16, "LM": 16, "PL0": 512, "PL": 512, "NO": 512, "Uf": 64, "KM": 64, "F0": 64, "PW": 72, "LWn": 72, "BQ": 6, "OH": 96,
-          "LG": 96, "KG": 96, "SL": 96, "CG": 96, "SK": 96, "SC": 96, "EG": 96, "EG2": 96, "S1": 96, "S2": 96, "KB": 576, "SGN": 576, "R6": 96, "CUT": 96, "LEN": 96,
+          "BK": 6, "i16": 16, "I16": 16, "LM": 16, "PL0": 512, "PL": 512, "NO": 512, "Uf": 64, "KM": 64, "KT": 128, "F0": 64, "PW": 72, "LWn": 72, "BQ": 6,
+          "KG": 96, "SL": 96, "CG": 96, "SK": 96, "SC": 96, "EG": 96, "EG2": 96, "S1": 96, "S2": 96, "KB": 576, "SGN": 576, "R6": 96, "CUT": 96, "LEN": 96,
           "M1": 96, "M20": 97, "M21": 97, "M22": 97, "M23": 97, "IN": 1, "T1": 6, "T2": 6, "VV": 6, "VR": 6, "SLf": 64, "NT": 2, "NM": 2, "STT": 512, "OF": 16, "FM": 16, "UI": 1},
-    B16: {"oneb": 128, "GBb": 128, "GBK": 128, "nUS": 128, "LSK": 128, "IDb": 128, "IDh": 128, "IDK": 128, "nIDb": 128, "nB02": 128, "TSL": 144, "T32": 144, "Tn16": 144,
+    B16: {"oneb": 128, "GBb": 128, "GBK": 128, "nUS": 128, "LSK": 128, "IDb": 128, "IDh": 128, "IDK": 128, "nIDb": 128, "IDE": 128, "B0e": 128, "C23": 192, "RS6": 576, "JV": 576, "RS4": 384, "JW": 384, "OH": 96, "GBi": 128, "TSL": 144, "T32": 144, "Tn16": 144,
           "WS0": 144, "WS1": 144, "WS2": 144, "it0": 128, "ITH": 128, "ROW": 65, "SLh": 64, "SLi": 64, "FL": 512, "M2C": 512, "MK": 96, "Q0b": 96, "C8K": 512, "N4": 512, "TWO": 512,
-          "XG0": S, "XG1": S, "AB0": S, "AB1": S, "D0": S, "D1": 2 * S, "R0": S, "R1": 2 * S,
+          "DD": M * S, "RR": M * S,
           "FIT": 64, "CS": 64, "JK": 384, "JL": 576, "SPQ": 112, "STQ": 208, "INV": 96, "KL": 576, "CW": 11, "LE": 390, "EQ": 390, "TA": 768, "GQ": 112, "PG": 96, "PN": 96,
           "TG": 192, "TN": 192, "F1": 18, "F2": 18, "F3": 18, "SG0": 512, "SG1": 512},
-    I32: {"pi": 1, "pi2": 1, "Ui": 64, "Um": 64, "UU": 64, "FQ": 64, "CA": 512, "KMi": 64, "PAR": 64, "MX": 64, "KD": 72, "XA": 6, "XI": 6},
+    I32: {"pi": 1, "pi2": 1, "Ui": 64, "Um": 64, "UU": 64, "FQ": 64, "CA": 512, "KMi": 64, "PAR": 64, "MX": 64, "KD": 72},
+    F16: {"GB32": 128, "LG": 96},
     U16: {"BQo": 6, "LO": 6, "UO": 6, "UO2": 6, "PO": 6, "TO": 12, "KIu": 12, "ROu": 6, "SQ": 6, "IXu": 64, "FX": 64},
 }
 _AT, SCRATCH = {}, {n: ("sbuf", [128, c], d) for n, (c, d) in _OWN.items()}
-for _d, _n in ((F32, "SF"), (B16, "SB"), (I32, "SJ"), (U16, "SU")):
+for _d, _n in ((F32, "SF"), (B16, "SB"), (I32, "SJ"), (U16, "SU"), (F16, "SH")):
     _c = 0
     for _k, _w in _PART[_d].items():
         _AT[_k] = (_n, _c, _w)
@@ -41,10 +44,13 @@ _PS = ["pA", "pB", "pM", "pN", "pK0", "pK1", "pD0", "pD1"]
 SCRATCH.update({n: ("psum", [128, 512], F32) for n in _PS})
 SEMAPHORES = ["sv", "ss", "st", "sg", "loc"] + ["a%s%d" % (k, r) for k in "ijpt" for r in range(RO)] + ["d%d" % k for k in range(30)]
 
-CUT_AT = 240
-BY_S = [(0, 64, "pN", 0), (64, 128, "pN", 64), (128, 192, "pK1", 64), (192, CUT_AT, "pM", 0)]
-BY_V = [(320, 384, "pK0", 0), (384, 448, "pK1", 0), (448, 512, "pB", 0), (CUT_AT, 320, "pA", 0)]
-_C = {"cy": 0.95, "gath": 1.5, "scat": 3.5, "pe": 0.48, "hop": 110.0, "own": 90.0, "dma": 2000.0, "rem": 2800.0, "passes": 6, "vlate": 1000.0}
+CUT_AT = 204
+UNITS = [(0, 64, "pK1", 0), (64, 192, "pN", 0), (192, 256, "pM", 0), (256, 320, "pA", 0), (320, 448, "pK0", 0), (448, 512, "pB", 0)]
+LINE_V = [("get", 448, 512), ("get", 320, 384), ("get", 384, 448), ("cut", 448, 512), ("cut", 320, 448), ("get", CUT_AT, 256), ("get", 256, 288), ("get", 288, 320)]
+LINE_S = [("get", 0, 32), ("get", 32, 64), ("cut", 0, 32), ("get", 64, 96), ("cut", 32, 64), ("get", 96, 128), ("cut", 64, 96), ("get", 128, 160), ("cut", 96, 128),
+          ("get", 160, 192), ("cut", 128, 160), ("get", 192, CUT_AT), ("cut", 160, 192), ("cut", 192, CUT_AT), ("cut", CUT_AT, 256), ("cut", 256, 288), ("cut", 288, 320)]
+_C = {"cy": np.array([0.88, 1.15, 0.92, 0.85]), "gath": np.array([1.56, 1.95, 1.1, 1.56]), "scat": np.array([3.8, 5.0, 2.0, 3.8]), "pe": np.array([0.45, 0.58, 0.47, 0.43]),
+      "far": np.array([1.0, 1.2, 1.0, 0.6]), "rfar": np.array([1.0, 1.3, 1.4, 0.7]), "hop": 150.0, "own": 120.0, "dma": 1800.0, "rem": 2800.0, "soon": 1.0, "u2s": 0, "o1": 32, "o2": 40, "ks": 4, "js": 4, "spv": 0, "passes": 4, "shakes": 0, "swaps": 4000, "heat": 30.0, "seed": 1, "weigh": 0.4, "vlate": 1000.0}
 _ORDER = []
 
 
@@ -67,7 +73,7 @@ def _queues(g, T):
             ap = t[:, a:b:s]
         else:
             ap = t[:, a:b]
-        return (ap, ((m, a, b, abs(s)),), (), -(-(b - a) // abs(s)), SCRATCH[m][2], 0)
+        return (ap, ((m, a, b, abs(s) if rows is None else -rows.start - 1),), (), -(-(b - a) // abs(s)), SCRATCH[m][2], 0)
 
     def X(ap):
         return (ap, (), (), 0, None, 0)
@@ -82,7 +88,7 @@ def _queues(g, T):
         if not (w or rw or ps):
             return False
         if not ps:
-            if b <= ra or rb <= a or (s == rs and s > 1 and (a - ra) % s):
+            if b <= ra or rb <= a or (s == rs and s > 1 and (a - ra) % s) or (s < 0 and rs < 0 and s != rs):
                 return False
             if rq == q and chain and w:
                 return False
@@ -187,21 +193,23 @@ def _queues(g, T):
         run("t", [o], [l, r], lambda: TE.matmul(o[0], l[0], r[0], start=start, stop=stop), 5 + _C["pe"] * max(64, r[3]) * (4 if r[4] == F32 else 1), not start)
 
     def MMS(o, *pairs, start=True, stop=True):
-        for k, (l, r) in enumerate(pairs):
-            MM(o, l, r, start and k == 0, stop and k == len(pairs) - 1)
+        for k, (l, r, *part) in enumerate(pairs):
+            MM(part[0] if part else o, l, r, start and k == 0, stop and k == len(pairs) - 1)
         part = ops[-len(pairs):]
         del ops[-len(pairs):]
 
         def emit():
             for op in part:
                 op[4]()
-        add("t", "t", part[0][2], [x for op in part for x in op[3]], emit, sum(op[5] for op in part), 0.0, not start)
+        add("t", "t", list(o[1]), [x for op in part for x in op[3]], emit, sum(op[5] for op in part), 0.0, not start)
 
     def IOTA(o, pat, base, cm):
         run("g", [o], [], lambda: g.iota(o[0], pat, base, cm, allow_small_or_imprecise_dtypes=True), 130 + 2 * cy * o[3])
+        LINE("g")
 
     def AFF(o, a, pat, op, base, cm):
         run("g", [o], [a], lambda: g.affine_select(o[0], a[0], pat, op, 0.0, base, cm), 170 + 2 * cy * o[3])
+        LINE("g")
 
     def DMA(q, o, a, lat=0.0, after=()):
         os_, is_ = split([o], [a])
@@ -254,39 +262,164 @@ def _queues(g, T):
             keep(book, aq, o, i, k)
             for j in pre[k]:
                 suc[j].append(k)
-        tail = [0.0] * n
-        for k in range(n - 1, -1, -1):
-            tail[k] = ops[k][5] + max([ops[k][6]] + [pre[j][k] + tail[j] for j in suc[k]])
-        back = [{j: pre[j][k] for j in suc[k]} for k in range(n)]
+        busy = [[float((op[5] + 0 * cy)[x]) for op in ops] for x in range(len(cy))]
+        lat, on, b0 = [op[6] for op in ops], [op[0] for op in ops], busy[0]
+        fore = [[(j, d) for j, d in p.items() if not any(j in pre[x] and pre[x][j] + p[x] >= d for x in p)] for p in pre]
+        fores = [[[(j, d + (lat[j] * (float(_C["far" if on[j] else "rfar"][x]) - 1) if d else 0.0)) for j, d in p] for p in fore] for x in range(len(cy))]
+        back = [[] for _ in range(n)]
+        for k in range(n):
+            for j, d in fore[k]:
+                back[j].append((k, d))
 
         def place(seq, before, first):
-            start, slots = [0.0] * n, {q: [] for q in Q}
+            start, end, slots = [0.0] * n, [0.0] * n, {q: [(-1.0, 0.0)] for q in Q}
             for k in seq:
-                q, busy = ops[k][0], ops[k][5]
-                t = max([first[k]] + [start[j] + ops[j][5] + d for j, d in before[k].items()])
-                if q is not None:
-                    sl = slots[q]
-                    at, hi = 0, len(sl)
-                    while at < hi:
-                        mid = (at + hi) // 2
-                        if sl[mid][0] < t:
-                            at = mid + 1
-                        else:
-                            hi = mid
-                    while at < len(sl) and max(t, sl[at - 1][1] if at else 0.0) + busy > sl[at][0]:
-                        at += 1
-                    t = max(t, sl[at - 1][1] if at else 0.0)
-                    sl.insert(at, (t, t + busy))
-                start[k] = t
+                t = first[k]
+                for j, d in before[k]:
+                    if end[j] + d > t:
+                        t = end[j] + d
+                if on[k] is not None:
+                    sl = slots[on[k]]
+                    at = len(sl)
+                    if sl[-1][1] > t:
+                        at, hi = 1, len(sl)
+                        while at < hi:
+                            mid = (at + hi) // 2
+                            if sl[mid][0] < t:
+                                at = mid + 1
+                            else:
+                                hi = mid
+                        while at < len(sl) and max(t, sl[at - 1][1]) + b0[k] > sl[at][0]:
+                            at += 1
+                        t = max(t, sl[at - 1][1])
+                    sl.insert(at, (t, t + b0[k]))
+                start[k], end[k] = t, t + b0[k]
             return start
+
+        def eager(key, ahead):
+            start, ready, wait = [0.0] * n, [0.0] * n, [len(p) for p in fore]
+            free, open_ = {q: 0.0 for q in list(Q) + [None]}, {q: [] for q in list(Q) + [None]}
+            for k in range(n):
+                if not wait[k]:
+                    open_[on[k]].append(k)
+            for _ in range(n):
+                t, q = min((max(free[q], min(ready[k] for k in ks)), str(q)) for q, ks in open_.items() if ks)
+                q = None if q == "None" else q
+                k = min((k for k in open_[q] if ready[k] <= t + ahead), key=lambda k: key[k])
+                open_[q].remove(k)
+                start[k] = max(t, ready[k])
+                end = start[k] + b0[k]
+                if q:
+                    free[q] = end
+                for j, d in back[k]:
+                    ready[j] = max(ready[j], end + d)
+                    wait[j] -= 1
+                    if not wait[j]:
+                        open_[on[j]].append(j)
+            return start
+
+        def span(start):
+            seq = sorted(range(n), key=lambda k: (start[k], k))
+            total = max(start[k] + b0[k] + lat[k] for k in seq)
+            for b in busy[1:]:
+                end, free = [0.0] * n, {q: 0.0 for q in Q}
+                free[None] = 0.0
+                for k in seq:
+                    t = free[on[k]] if on[k] else 0.0
+                    for j, d in fore[k]:
+                        if end[j] + d > t:
+                            t = end[j] + d
+                    end[k] = free[on[k]] = t + b[k]
+                total += _C["weigh"] * max(end[k] + lat[k] for k in seq)
+            return total, seq, start
+        tail, zero = [0.0] * n, [0.0] * n
+        for k in range(n - 1, -1, -1):
+            tail[k] = b0[k] + max([lat[k]] + [d + tail[j] for j, d in back[k]])
         seq, best = sorted(range(n), key=lambda k: (-tail[k], k)), None
         for it in range(_C["passes"]):
-            start = place(seq, pre, [0.0] * n)
-            span = max(start[k] + ops[k][5] + ops[k][6] for k in range(n))
-            if best is None or span < best[0]:
-                best = (span, sorted(range(n), key=lambda k: (start[k], k)))
-            late = place(sorted(range(n), key=lambda k: (-start[k] - ops[k][5], -k)), back, [op[6] for op in ops])
-            seq = sorted(range(n), key=lambda k: (-late[k] - ops[k][5], k))
+            now = span(place(seq, fore, zero))
+            best = now if best is None or now[0] < best[0] else best
+            late = place(sorted(range(n), key=lambda k: (-now[2][k] - b0[k], -k)), back, lat)
+            seq = sorted(range(n), key=lambda k: (-late[k] - b0[k], k))
+            for ahead in (0.0, 100.0, 250.0):
+                now = span(eager([-late[k] - b0[k] for k in range(n)], ahead))
+                best = now if now[0] < best[0] else best
+        rng = np.random.default_rng(_C["seed"])
+        for it in range(_C["shakes"]):
+            t0, width, key = rng.random() * max(best[2]), rng.choice([300.0, 1000.0, 3000.0]), list(best[2])
+            noise = rng.random(n) * width
+            for k in range(n):
+                if t0 - 3000 < key[k] < t0 + 3000:
+                    key[k] += noise[k]
+                for j, d in fore[k]:
+                    if key[j] >= key[k]:
+                        key[k] = key[j] + 1e-3
+            now = span(place(sorted(range(n), key=lambda k: key[k]), fore, zero))
+            best = now if now[0] <= best[0] else best
+
+        def walk(seq, b, fore, at, old):
+            end, why, last = list(old[0]), list(old[1]), {q: -1 for q in Q}
+            for k in seq[:at]:
+                last[on[k]] = k
+            for k in seq[at:]:
+                q, t, w = on[k], 0.0, -1
+                if q:
+                    w = last[q]
+                    t = end[w] if w >= 0 else 0.0
+                    last[q] = k
+                    w = -2 - w
+                for j, d in fore[k]:
+                    if end[j] + d > t:
+                        t, w = end[j] + d, j
+                end[k], why[k] = t + b[k], w
+            k = max(ends, key=lambda k: end[k] + lat[k])
+            total, stood = end[k] + lat[k] + _C["soon"] * sum(end) / n, []
+            while k != -1:
+                w = why[k]
+                if w < -1:
+                    w = -2 - w
+                    stood.append((w, k))
+                k = w
+            return total, stood, (end, why)
+
+        def judge(seq, at, old):
+            res = [walk(seq, b, f, at, o) for b, f, o in zip(busy, fores, old)]
+            return res[0][0] + _C["weigh"] * sum(x[0] for x in res[1:]), seq, [p for x in res for p in x[1]], [x[2] for x in res]
+        ends = [k for k in range(n) if not suc[k]]
+        best = now = judge(best[1], 0, [([0.0] * n, [-1] * n)] * len(busy))
+        for it in range(_C["swaps"]):
+            a, b = now[2][int(rng.integers(len(now[2])))]
+            seq = now[1]
+            i, j = seq.index(a), seq.index(b)
+            if rng.random() < 0.5:
+                for _ in range(int(rng.integers(3))):
+                    i = max([x for x in range(max(0, i - 40), i) if on[seq[x]] == on[a]] + [-1])
+                    if i < 0:
+                        break
+                if i < 0:
+                    continue
+                go, part = {b}, seq[i:j + 1]
+                for k in part[::-1]:
+                    if k in go:
+                        go.update(pre[k])
+                if a in go:
+                    continue
+                part = [k for k in part if k in go] + [k for k in part if k not in go]
+            else:
+                for _ in range(int(rng.integers(8)) - 2):
+                    j = min([x for x in range(j + 1, min(n, j + 40)) if on[seq[x]] == on[a]] + [j + 40, n - 1])
+                go, part = {a}, seq[i:j + 1]
+                for k in part:
+                    if k in go:
+                        go.update(suc[k])
+                if b in go:
+                    continue
+                part = [k for k in part if k not in go] + [k for k in part if k in go]
+            new = judge(seq[:i] + part + seq[j + 1:], i, now[3])
+            if new[0] <= now[0] - _C["heat"] * (1 - it / _C["swaps"]) * np.log(1 - rng.random()):
+                now = new
+                best = now if now[0] < best[0] else best
+        _C["span"] = best[0]
         return best[1]
 
     def END():
@@ -323,7 +456,7 @@ def rank_program(g, core, T, topo):
     AFF(A("GBt"), A("one"), [[-16, 8], [0, 16]], O.is_ge, 0, 1)
     AFF(A("GB"), A("GBt"), [[16, 8], [0, 16]], O.is_ge, 15, -1)
     AFF(A("ID"), A("GB"), [[-1, 128]], O.is_equal, 0, 1)
-    for n, c in enumerate((0.5, 383.0 * BIG, 255.0)):
+    for n, c in enumerate((0.5, 383.0 * BIG, 255.0, 2.0 ** 23 + 255)):
         MS(A("CB", n, n + 1), c)
     TS(A("pi2"), A("pi"), 15, None, O.bitwise_and)
     TC(A("PI"), A("pi2"))
@@ -332,7 +465,7 @@ def rank_program(g, core, T, topo):
     MS(A("TSL"), 0.0)
     TC(A("TSL", 15, 128, 16), A("GB", 0, 128, 16))
     for r in range(RO):
-        TS(A("WS%d" % r), A("TSL"), A("wtf", r, r + 1), -1.0, O.mult, O.mult)
+        TS(A("WS%d" % r), A("TSL"), A("wtf", r, r + 1), -1.0 if r else 1.0, O.mult, O.mult)
     ACT(A("T32"), A("TSL"), CP, scale=32.0)
     ACT(A("Tn16"), A("TSL"), CP, scale=-16.0)
     MMS(A("pN", 0, 3), (A("GB"), A("wtf")))
@@ -352,33 +485,44 @@ def rank_program(g, core, T, topo):
     IOTA(A("ROW"), [[16, 65]], -8, 0)
     IOTA(A("SLh"), [[16, 64]], 0, 0)
     IOTA(A("M2C"), [[2, 8], [0, 64]], 0, 0)
-    for a in range(0, FWW, FWW // 8):
-        IOTA(A("FW", a, a + FWW // 8), [[0, FWW // 8]], 0, 0)
-    for n, c, base in (("KD", 72, 0), ("PW", 72, -1), ("LWn", 72, 0), ("C8K", 512, W), ("N4", 512, -4), ("TWO", 512, 2), ("CW", 11, 0), ("RSB", 96, -2 ** 22), ("DMP", 96, -1)):
-        IOTA(A(n), [[0, c]], base, 0)
+    for n, c in (("KD", 0), ("PW", -1.0), ("LWn", 0.0), ("C8K", STEP), ("C23", 2.0 ** 23), ("N4", -4.0), ("TWO", 2.0), ("CW", 0.0), ("RSB", -4 * FAR), ("DMP", -1.0), ("U2", 0.0)):
+        MS(A(n), c)
     for n, a, b in (("GQ", 96, 112), ("SPQ", 96, 112), ("STQ", 192, 208), ("G0", S, S + CAP), ("G1", S, S + CAP)):
-        IOTA(A(n, a, b), [[0, b - a]], 0, 0)
-    for n, a, c in (("IDb", "ID", 1.0), ("nIDb", "ID", -1.0), ("GBb", "GB", 1.0), ("nUS", "USf", -1.0), ("GB32", "GB", 32.0), ("nGB8", "GB", -8.0), ("nGB", "GB", -1.0),
-                    ("nB02", "B0", -2.0), ("GBK", "GB", BIG), ("IDK", "ID", BIG), ("IDh", "ID", 0.5)):
+        MS(A(n, a, b), 0.0)
+    for a in range(0, 4096, 512):
+        ACT(A("FW", a, a + 512), A("U2"), CP)
+    for a in range(4096, FWW, 526):
+        IOTA(A("FW", a, a + 526), [[0, 526]], 0, 0)
+    for n, a, c in (("IDb", "ID", 1.0), ("nIDb", "ID", -1.0), ("GBb", "GB", 1.0), ("nUS", "USf", -1.0), ("nGB8", "GB", -8.0), ("nGB", "GB", -1.0),
+                    ("GBK", "GB", BIG), ("IDK", "ID", BIG), ("IDh", "ID", 0.5)):
         ACT(A(n), A(a), CP, scale=c)
     TS(A("GBt"), A("ID"), 4096.0, None, O.mult)
     TT(A("LSK"), A("GBt"), A("LSf"), O.add)
     TS(A("th16"), A("thi"), 16.0, None, O.mult)
     TS(A("P512"), A("PI"), 512.0, None, O.mult)
     TS(A("P513"), A("PI"), 512.0, 1.0, O.mult, O.add)
-    TS(A("PIN"), A("PI"), 512.0, 0.4375, O.mult, O.add)
+    TS(A("PIN"), A("PI"), 512.0, 0.25, O.mult, O.add)
     TS(A("P5K"), A("P513"), 10000.0, None, O.mult)
     TC(A("M20", 96, 97), A("P513"))
     TS(A("CB", 4, 5), A("PI"), 2.0, None, O.is_equal)
-    TS(A("LS1"), A("CB", 4, 5), W + 4.0, -float(W), O.mult, O.add)
-    TS(A("LB1"), A("CB", 4, 5), -4.0 - (2 * W - 4608), 2.0 * W - 4608, O.mult, O.add)
+    TS(A("LS1"), A("CB", 4, 5), STEP + 4.0, -STEP, O.mult, O.add)
+    TS(A("LB1"), A("CB", 4, 5), -4.0 - 1.25 * STEP, 1.25 * STEP, O.mult, O.add)
+    TS(A("B0e"), A("B0"), 2.0 ** -9, None, O.mult)
+    TT(A("IDE"), A("B0e"), A("ID"), O.max)
     TS(A("PL"), A("PL0"), A("P512"), None, O.add)
     TS(A("MK"), A("QM"), A("PI"), FAR, O.not_equal, O.mult)
     MS(A("RSB", 0, 96, 16), 2 * FAR)
+    if _C["js"] < 6:
+        MS(A("RS6"), 1.0)
+        MS(A("RS6", 0, 576, 96), 0.0)
     TS(A("DMP", 0, 96, 16), A("QB0"), A("PI"), W + 1.0, O.add, O.add)
     TS(A("QB"), A("QB0"), A("PI"), 0.5, O.add, O.add)
-    TS(A("CB", 5, 6), A("PI"), 1.0 / 1024, None, O.mult)
-    TS(A("BI"), A("BI"), 1.0 / 32, A("CB", 5, 6), O.mult, O.add)
+    TS(A("BI"), A("BI"), 1.0 / 32, None, O.mult)
+    TS(A("GBi"), A("GB"), A("PI"), None, O.mult)
+    TS(A("GB32"), A("GB"), 32.0, None, O.mult)
+    if _C["ks"] < 6:
+        MS(A("RS4"), 1.0)
+        MS(A("RS4", 0, 384, 64), 0.0)
     TS(A("I16"), A("i16"), A("PI"), None, O.is_equal)
     TS(A("LM"), A("i16"), A("PI"), BIG, O.is_le, O.mult)
     TS(A("SLi"), A("oneb", 0, 64), A("PI"), None, O.mult)
@@ -392,9 +536,9 @@ def rank_program(g, core, T, topo):
         return A(n, 15 - i, 143 - i)
 
     def lists(r):
-        G = "G%d" % (r % 2)
+        G = "G%d" % (r % 2) if r else "GI"
         MMS(A("pA", 0, 64), *[(sel("WS%d" % r, i), A(G, i, S, 16)) for i in range(16)])
-        TS(A("Ui"), A("pA", 0, 64), A("CW3", r, r + 1), None, O.add)
+        TS(A("Ui"), A("pA", 0, 64), A("CW3", r, r + 1) if r else 0.0, None, O.add)
         TS(A("Um"), A("Ui"), 4095, None, O.bitwise_and)
         TC(A("Uf"), A("Um"))
         TT(A("UU"), A("Um"), A("Um"), O.mult)
@@ -424,27 +568,51 @@ def rank_program(g, core, T, topo):
         G = "G%d" % (r % 2)
         left = [M] * 64
 
-        held = {}
+        held, pairs = {}, [0, sum(1 for u in UNITS if u[1] - u[0] == 128)]
+
+        def rows(u, src, by, stop):
+            a, b, bank, at = u
+            if b - a == 128:
+                MMS(A(bank, at, at + 128), *[(A(src, 16 * a + i, 16 * b, 16), A(by, 15, 128, 16), A(bank, at + i, at + 128, 16)) for i in range(16)], start=False, stop=stop)
+            else:
+                MMS(A(bank, at, at + b - a), *[(sel(by, i), A(src, 16 * a + i, 16 * b, 16)) for i in range(16)], start=False, stop=stop)
 
         def opens(u, D):
             a, b, bank, at = u
-            MMS(A(bank, at, at + b - a), (A("IDb"), A("M2C", a, b)), (A("IDb"), A("FL", a, b)),
-                *[(sel("Tn16", i), A(D, i, 16 * (b - a), 16)) for i in range(16 if D else 0)], stop=False)
+            if b - a == 128:
+                MMS(A(bank, at, at + 128), (A("M2C", a, b), A("IDb")), (A("FL", a, b), A("IDb")), stop=False)
+            else:
+                MMS(A(bank, at, at + b - a), (A("IDb"), A("M2C", a, b)), (A("IDb"), A("FL", a, b)), stop=False)
+            if D:
+                rows(u, "DD", "Tn16", False)
 
-        def closes(u, R):
+        def closes(u):
             a, b, bank, at = u
-            MMS(A(bank, at, at + b - a), *[(sel("T32", i), A(R, i, 16 * (b - a), 16)) for i in range(16)], start=False)
-            held.setdefault(bank, []).append(u)
-            if len(held[bank]) < sum(1 for x in BY_S + BY_V if x[2] == bank):
+            rows(u, "RR", "T32", True)
+            if b - a == 128:
+                pairs[0] += 1
+                if pairs[0] == 1:
+                    TS(A("KT"), A(bank, at, at + 128), FAR, None, O.min)
+                else:
+                    TT(A("KT"), A(bank, at, at + 128), A("KT"), O.min)
+                if pairs[0] < pairs[1]:
+                    return
+                for x in range(64):
+                    left[x] -= 2 * pairs[1] - 2
+                at += 128
+                MMS(A(bank, at, at + 128), (A("KT"), A("ID")))
+            held.setdefault(bank, []).append((a, b, bank, at))
+            if len(held[bank]) < sum(1 for x in UNITS if x[2] == bank):
                 return
             for a, b, bank, at in held[bank]:
                 c = a
                 while c < b:
                     e = c + 1
-                    while e < b and e % 64 and left[e % 64] == left[c % 64]:
+                    while e < b and e % 64 and (left[e % 64] == 1) == (left[c % 64] == 1) and (e % 64 in held) == (c % 64 in held):
                         e += 1
                     key, c0, c1 = A(bank, at + c - a, at + e - a), c % 64, c % 64 + e - c
-                    if left[c0] == M:
+                    if c0 not in held:
+                        held.update({x: 1 for x in range(c0, c1)})
                         TS(A("KM", c0, c1), key, FAR, None, O.min)
                     else:
                         TT(A("KMi" if left[c0] == 1 else "KM", c0, c1), key, A("KM", c0, c1), O.min)
@@ -452,44 +620,36 @@ def rank_program(g, core, T, topo):
                         left[x] -= 1
                     c = e
 
-        def v_get(k, u):
-            cut = [u[0]] + [c for c in range(u[0] + 1, u[1]) if c % 64 == 0] + [u[1]]
-            for a, b in zip(cut, cut[1:]):
-                TT(A("D%d" % (k % 2), 16 * (a - u[0]), 16 * (b - u[0])), IND(A("X"), A("OFF", a, b)), A(G, 16 * (a % 64), 16 * (a % 64 + b - a)), O.subtract)
-                LINE("v")
-            opens(u, "D%d" % (k % 2))
-
-        def v_cut(k, u):
-            n = 16 * (u[1] - u[0])
-            TS(A("R%d" % (k % 2), 0, n), A("D%d" % (k % 2), 0, n), 0.0, None, O.max)
-            LINE("v")
-            closes(u, "R%d" % (k % 2))
-
-        def s_get(k, j, u, h, e):
-            xg = A("XG%d" % (k % 2), 16 * (h - u[0]), 16 * (e - u[0]))
-            ACT(xg, IND(A("X"), A("OFF", h, e)), CP)
-            LINE("s")
-            MMS(A("pD%d" % (j % 2), 0, 16 * (e - h)), (A("nIDb"), A(G, 16 * (h % 64), 16 * (h % 64 + e - h))), (A("IDb"), xg))
-
-        def s_cut(k, j, u, h, e):
-            ACT(A("AB%d" % (k % 2), 16 * (h - u[0]), 16 * (e - u[0])), A("pD%d" % (j % 2), 0, 16 * (e - h)), AF.Abs, scale=0.5)
-            LINE("s")
-            if e == u[1]:
-                opens(u, None)
-                closes(u, "AB%d" % (k % 2))
-        steps = []
-        halves = [(k, u, h, min(u[1], h + 32)) for k, u in enumerate(BY_S) for h in range(u[0], u[1], 32)]
-        for q, t, gets, cuts in (("v", _C["vlate"], [(v_get, (k, u), 24 * (u[1] - u[0])) for k, u in enumerate(BY_V)], [(v_cut, (k, u), 8 * (u[1] - u[0])) for k, u in enumerate(BY_V)]),
-                                 ("s", 0.0, [(s_get, (k, j, u, h, e), 24 * (e - h)) for j, (k, u, h, e) in enumerate(halves)],
-                                  [(s_cut, (k, j, u, h, e), 16 * (e - h)) for j, (k, u, h, e) in enumerate(halves)])):
-            line = gets[:1] + [x for pair in zip(gets[1:], cuts) for x in pair] + cuts[-1:]
-            if q == "v":
-                line[-3:-1] = line[-2:-4:-1]
-            for f, args, n in line:
-                t += n
-                steps.append((t, len(steps), f, args))
-        for t, k, f, args in sorted(steps, key=lambda x: x[:2]):
-            f(*args)
+        got, done, where, by_v = set(), set(), {}, {c for k, a, b in LINE_V if k == "cut" for c in range(a, b)}
+        t, at = {"v": _C["vlate"], "s": 0.0}, {"v": 0, "s": 0}
+        while at["v"] < len(LINE_V) or at["s"] < len(LINE_S):
+            can = [q for q, line in (("v", LINE_V), ("s", LINE_S)) if at[q] < len(line) and (line[at[q]][0] == "get" or got.issuperset(range(*line[at[q]][1:])))]
+            q = min(can, key=lambda q: t[q])
+            k, a, b = (LINE_V if q == "v" else LINE_S)[at[q]]
+            at[q] += 1
+            t[q] += (b - a) * (24 if k == "get" else 8 if q == "v" else 16)
+            d, mine = A("DD", 16 * a, 16 * b), k == "get" and A(G, 16 * (a % 64), 16 * (a % 64 + b - a))
+            if k == "get" and q == "v":
+                TT(d, IND(A("X"), A("OFF", a, b)), mine, O.subtract)
+            elif k == "get":
+                ACT(d, IND(A("X"), A("OFF", a, b)), CP)
+            elif q == "v":
+                TS(A("RR", 16 * a, 16 * b), d, 0.0, None, O.max)
+            else:
+                ACT(A("RR", 16 * a, 16 * b), where.get(a, d), AF.Abs, scale=0.5)
+            LINE(q)
+            if k == "get" and q == "s":
+                where[a] = A("pD%d" % (len(where) % 2), 0, 16 * (b - a))
+                MMS(where[a], (A("nIDb"), mine), (A("IDb"), d))
+            for u in UNITS:
+                if u[0] < b and a < u[1]:
+                    if k == "get" and u[0] in by_v and (got | set(range(a, b))).issuperset(range(u[0], u[1])):
+                        opens(u, True)
+                    if k == "cut" and (done | set(range(a, b))).issuperset(range(u[0], u[1])):
+                        if u[0] not in by_v:
+                            opens(u, False)
+                        closes(u)
+            (got if k == "get" else done).update(range(a, b))
 
     def own(dst, bank):
         SCAN(A(dst), A("RSB"), A(bank, 0, 96), 0.0, O.max, O.min)
@@ -498,10 +658,14 @@ def rank_program(g, core, T, topo):
         ACT(A("NO"), A("X0%d" % r), RL, bias=A("CB", 1, 2), scale=-2 * BIG)
         SCAN(A("UL", s=-1), A("NO", s=-1), A("PL", s=-1), float(W + 1), O.min, O.max)
         TS(A("OF"), A("I16"), A("UL", 0, 1), None, O.mult)
-        MMS(A("pK0", 128, 144), (A("GB"), A("OF")))
-        TT(A("FM"), A("pK0", 128, 144), A("LM"), O.max)
+        MMS(A("pA", 256, 272), (A("GB"), A("OF")))
+        TT(A("FM"), A("pA", 256, 272), A("LM"), O.max)
         RED(A("UI"), A("FM"), O.min)
-        TS(A("U2"), A("UL"), A("UI"), None, O.min)
+        if _C["u2s"] and r:
+            ACT(A("NO"), A("UL"), RL, bias=A("UI"), scale=-1.0)
+            ACT(A("U2"), A("NO"), IDN, bias=A("UI"), scale=-1.0)
+        else:
+            TS(A("U2"), A("UL"), A("UI"), None, O.min)
         DMA("y", A("FW", 0, W, rows=slice(0, 128, 16)), A("U2"), 500)
 
     near, far = T.cores[rank ^ 1], T.cores[rank ^ 2]
@@ -518,35 +682,49 @@ def rank_program(g, core, T, topo):
         G, H = "G%d" % (r % 2), "YG" if last else "G%d" % ((r + 1) % 2)
         RK, SP, STn, RI, RJ, Z, M2, M3 = ("%s%d" % (n, k) for n, k in (("RK", r), ("SP", r), ("ST", r), ("RI", r), ("RJ", r), ("Z", r), ("M2", r), ("M2", r + 1)))
         lists(r)
-        scores(r)
         utable(r)
+        scores(r)
         TS(A("PAR"), A("KMi"), 1, None, O.bitwise_and)
         TS(A("F0"), A("KMi"), A("th16"), None, O.is_lt)
         TT(A("FIT"), A("F0"), A("PAR"), O.is_gt)
         SCAN(A("CS"), A("oneb", 0, 64), A("FIT"), 0.0, O.mult, O.add)
         MMS(A("pB", 0, 64), (A("GBb"), A("CS")))
         MMS(A("pM", 0, 64), (A("GBb"), A("CS")), (A("nUS"), A("FIT")))
-        MMS(A("pM", 64, 66), (A("GBb"), A("CS", 62, 64)))
-        for a in range(6):
+        MMS(A("pM", 64, 128), (A("GBb"), A("CS")))
+        ks = _C["ks"]
+        for a in range(ks):
             ACT(A("JK", 64 * a, 64 * a + 64), A("pB", 0, 64), AF.Sign, bias=A("QB", a, a + 1), scale=-1.0, acc=A("BQ", a, a + 1))
+        for a in range(ks, 6):
+            TS(A("JK", 64 * a, 64 * a + 64), A("pM", 64, 128), A("QB", a, a + 1), None, O.is_le)
+        TS(A("BQo", 0, ks), A("BQ", 0, ks), 0.5, 32.0, O.mult, O.add)
+        TS(A("T1", 0, ks), A("BQ", 0, ks), 8.0, 512.0 + 4088.5, O.mult, O.add)
+        if ks < 6:
+            SCAN(A("JW", 64 * ks, 384), A("RS4", 64 * ks, 384), A("JK", 64 * ks, 384), 0.0, O.mult, O.add)
+            TC(A("BQo", ks, 6), A("JW", 64 * ks + 63, 384, 64))
+            TS(A("T1", ks, 6), A("JW", 64 * ks + 63, 384, 64), 16.0, 4088.5, O.mult, O.add)
         TS(A("MX"), A("KMi"), 14, None, O.bitwise_and)
         TS(A("KD", 0, 64), A("KMi"), 65520, None, O.bitwise_and)
         TT(A("LWn", 0, 64), A("MX"), A("BI"), O.add)
         TT(A("PW", 0, 64), A("pM", 0, 64), A("FIT"), O.mult)
-        TS(A("INV"), A("Q0"), A("pM", 65, 66), 2.0 ** -14, O.is_ge, O.add)
+        TS(A("INV"), A("Q0"), A("pM", 127, 128), 2.0 ** -14, O.is_ge, O.add)
         inv = (A("IDK"), A("INV"))
-        TS(A("BQo"), A("BQ"), 0.5, 32.0, O.mult, O.add)
+
+        def two(o, early, late):
+            MMS(o, *early, stop=False)
+            MMS(o, *late, start=False)
         TT(A("OH"), IND(A("PW"), A("BQo")), A("Q1"), O.is_equal)
         TT(A("LG"), IND(A("LWn"), A("BQo")), A("OH"), O.mult)
-        MMS(A("pA", 0, 96), mk, (A("GB32"), A("LG")))
+        two(A("pA", 0, 96), [mk], [(A("GB32"), A("LG"))])
         TT(A("KG"), IND(A("KD"), A("BQo")), A("OH"), O.mult)
         own("SL", "pA")
         TC(A("LO"), A("SL", *q6))
-        MMS(A("pK0", 0, 96), mk, (A("nIDb"), A("Q0b")), (A("nGB8"), A("KG")))
-        MMS(A("pK1", 0, 96), (A("nIDb"), A("Q0b")), (A("nGB8"), A("KG")))
+        two(A("pN", 0, 96), [mk], [(A("GBi"), A("OH"))])
+        own("SI", "pN")
+        two(A("pK0", 0, 96), [mk, (A("nIDb"), A("Q0b"))], [(A("nGB8"), A("KG"))])
+        two(A("pK1", 0, 96), [(A("nIDb"), A("Q0b"))], [(A("nGB8"), A("KG"))])
         TT(A("CG"), IND(A("C"), A("LO")), A("OH"), O.mult)
-        MMS(A("pA", 0, 96), mk, inv, (A("GB"), A("CG")))
-        MMS(A("pB", 0, 96), inv, (A("GB"), A("CG")))
+        two(A("pA", 0, 96), [mk, inv], [(A("GB"), A("CG"))])
+        two(A("pB", 0, 96), [inv], [(A("GB"), A("CG"))])
         own("SK", "pK0")
         for a in range(6):
             ACT(A("SGN", 96 * a, 96 * a + 96), A("pK1", 0, 96), AF.Sign, bias=A("SK", 16 * a + 15, 16 * a + 16), scale=-1.0)
@@ -555,31 +733,26 @@ def rank_program(g, core, T, topo):
             ACT(A("KB", 96 * a, 96 * a + 96), A("SGN", 96 * a, 96 * a + 96), CP, scale=A("SC", 16 * a + 15, 16 * a + 16))
         TS(A("UO"), A("SC", *q6), 15.0, W - 1.0, O.add, O.min)
         TC(A("EG"), IND(A("FW"), A("UO")))
-        MMS(A("pM", 0, 96), mk, (A("B0"), A("EG")))
+        two(A("pM", 0, 96), [mk], [(A("B0"), A("EG"))])
         own("S1", "pM")
         TS(A("UO2"), A("S1", *q6), 6.0, W - 1.0, O.add, O.min)
         TC(A("EG2"), IND(A("FW"), A("UO2")))
-        MMS(A("pN", 0, 96), mk, (A("B0"), A("EG2")))
+        two(A("pN", 0, 96), [mk], [(A("B0"), A("EG2"))])
         own("S2", "pN")
         TS(A("TO", 0, 6), A("S1", *q6), -2.0, None, O.add)
         TS(A("TO", 6, 12), A("S2", *q6), -2.0, None, O.add)
         TS(A("PO"), A("SC", *q6), 9.0, W - 1.0, O.add, O.min)
-        ACT(A("PG"), IND(A("X"), A("PO")), CP)
-        ACT(A("PN"), A("PG"), RL, scale=-1.0)
-        MMS(A("pD0", 0, 96), (A("nIDb"), A("PG")), (A("nB02"), A("PN")))
-        ACT(A("SPQ", 0, 96), A("pD0", 0, 96), RL, bias=A("CB", 2, 3))
-        MMS(A("pD0", 96, 192), (A("nGB"), A("CG")), (A("B0"), A("EG2")))
+        ACT(A("PG"), IND(A("X"), A("PO")), AF.Abs)
+        two(A("pD0", 0, 96), [(A("IDb"), A("C23", 0, 96))], [(A("IDE"), A("PG"))])
+        ACT(A("SPQ", 0, 96), A("pD0", 0, 96), RL, bias=A("CB", 3, 4), scale=-1.0)
+        two(A("pD0", 96, 192), [(A("nGB"), A("CG"))], [(A("B0"), A("EG2"))])
         ACT(A("LEN"), A("pD0", 96, 192), IDN, bias=A("LB1"), scale=A("LS1"))
         MMS(A("pM", 96, 192), (A("B0"), A("EG2")))
-        ACT(A("TG"), IND(A("X"), A("TO")), CP)
-        ACT(A("TN"), A("TG"), RL, scale=-1.0)
-        MMS(A("pD1", 0, 192), (A("nIDb"), A("TG")), (A("nB02"), A("TN")))
-        ACT(A("STQ", 0, 192), A("pD1", 0, 192), RL, bias=A("CB", 2, 3))
-        TS(A("T1"), A("BQ"), 8.0, 512.0 - 4088.5, O.mult, O.add)
-        TS(A("XA"), A("SL", *q6), 32.0, None, O.mult)
-        TS(A("XI"), A("XA"), 2047, None, O.bitwise_and)
-        TT(A("T2"), A("XI"), A("T1"), O.subtract)
-        TS(A("SQ"), A("T2"), -4088.5, None, O.add)
+        ACT(A("TG"), IND(A("X"), A("TO")), AF.Abs)
+        two(A("pD1", 0, 192), [(A("IDb"), A("C23"))], [(A("IDE"), A("TG"))])
+        ACT(A("STQ", 0, 192), A("pD1", 0, 192), RL, bias=A("CB", 3, 4), scale=-1.0)
+        TT(A("T2"), A("SI", *q6), A("T1"), O.add)
+        TS(A("SQ"), A("T2"), -4088.5, S - 1.0, O.add, O.min)
         ACT(A("GQ", 0, 96), IND(A(G, 0, S), A("SQ")), CP)
         MM(A("pK0", 0, 96), *mk, True, False)
         MM(A("pK0", 0, 96), *inv, False, False)
@@ -595,11 +768,22 @@ def rank_program(g, core, T, topo):
         k = SEND([cnts], 2 * hn, lambda: g.remote_dma_fused([to(near, en[:hn], "ai%d" % r, cnts, A(RI)), to(far, ef[hn:], "aj%d" % r, cnts, A(RJ))], local_sem=T.sem["loc"]))
         LAND(A(RI), "ai%d" % r, hn, k)
         LAND(A(RJ), "aj%d" % r, len(ef) - hn, k)
-        for a in range(6):
+        js = _C["js"]
+        for a in range(js):
             ACT(A("JL", 96 * a, 96 * a + 96), A(RK), AF.Sign, bias=A("QB", a, a + 1), scale=-1.0, acc=A("BK", a, a + 1))
-        TS(A("KIu", 0, 6), A("BK"), 0.5, 48.0, O.mult, O.add)
-        TS(A("KIu", 6, 12), A("BK"), 0.5, 144.0, O.mult, O.add)
-        ACT(A(SP), IND(A("SPQ"), A("KIu", 0, 6)), CP)
+        for a in range(js, 6):
+            TS(A("JL", 96 * a, 96 * a + 96), A(RK), A("QB", a, a + 1), None, O.is_le)
+        if js:
+            TS(A("KIu", 0, js), A("BK", 0, js), 0.5, 48.0, O.mult, O.add)
+            TS(A("KIu", 6, 6 + js), A("BK", 0, js), 0.5, 144.0, O.mult, O.add)
+        if js < 6:
+            SCAN(A("JV", 96 * js, 576), A("RS6", 96 * js, 576), A("JL", 96 * js, 576), 0.0, O.mult, O.add)
+            TC(A("KIu", js, 6), A("JV", 96 * js + 95, 576, 96))
+            TS(A("KIu", 6 + js, 12), A("JV", 96 * js + 95, 576, 96), 96.0, None, O.add)
+        if _C["spv"]:
+            TC(A(SP), IND(A("SPQ"), A("KIu", 0, 6)))
+        else:
+            ACT(A(SP), IND(A("SPQ"), A("KIu", 0, 6)), CP)
         k = SEND([A(SP)], len(en), lambda: g.remote_dma_fused([to(near, en, "ap%d" % r, A(SP), A(Z, 0, 96))], local_sem=T.sem["loc"]))
         LAND(A(Z, 0, 96), "ap%d" % r, len(en), k)
         ACT(A(STn), IND(A("STQ"), A("KIu")), CP)
@@ -623,7 +807,7 @@ def rank_program(g, core, T, topo):
             DMA("s", XT(T.yc[:, :]), A("YC"), 800)
         else:
             X1 = "X0%d" % (r + 1)
-            TS(A("IN"), A(M3, 96, 97), A("PIN"), -float(W), O.subtract, O.mult)
+            TS(A("IN"), A(M3, 96, 97), A("PIN"), -STEP, O.subtract, O.mult)
             SCAN(A(X1), A("C8K"), A("LW"), A("IN"), O.add, O.min)
             DMA("y", A("X", 0, W, rows=slice(0, 128, 16)), A(X1), 400)
         TS(A("CW", 5, 11), A("R6", *q6), W + 0.5, None, O.is_lt)
@@ -648,16 +832,21 @@ def rank_program(g, core, T, topo):
                 ACT(out, IND(win, off), IDN, bias=A("CB", 2, 3), scale=-1.0)
             else:
                 ACT(out, IND(win, off), CP)
-        turn("v", A(Z, ARR, ARR + 512), A(G), A("IXu", 0, 32), True)
-        turn("s", A(Z, ARR + 512, ARR + S), A(G), A("IXu", 32, 64), True)
+        o1, o2 = _C["o1"], _C["o2"]
+        turn("v", A(Z, ARR, ARR + 16 * o1), A(G), A("IXu", 0, o1), True)
+        LINE("n")
+        turn("s", A(Z, ARR + 16 * o1, ARR + S), A(G), A("IXu", o1, 64), True)
         n1, n2 = A(RI, 7, 8), A(RJ, 7, 8)
         TT(A("NT", 0, 1), n1, n2, O.add)
+        LINE("n")
         TT(A("NT", 1, 2), A("NT", 0, 1), n2, O.add)
         TS(A("FX", 18, 64), A("SLf", 18, 64), A("NT", 1, 2), None, O.subtract)
-        turn("v", A(H, ARR, 640), A(Z, ARR, ARR + S), A("FX", 18, 40), not last)
-        turn("s", A(H, 640, S), A(Z, ARR, ARR + S), A("FX", 40, 64), not last)
+        turn("v", A(H, ARR, 16 * o2), A(Z, ARR, ARR + S), A("FX", 18, o2), not last)
+        turn("s", A(H, 16 * o2, S), A(Z, ARR, ARR + S), A("FX", o2, 64), not last)
         TS(A("NM", 0, 1), n1, -1.0, float(CAP), O.mult, O.add)
+        LINE("n")
         TS(A("NM", 1, 2), n2, -1.0, float(CAP), O.mult, O.add)
+        LINE("n")
         TS(A("F1"), A("SLf", 0, 18), n1, A("NM", 0, 1), O.is_ge, O.mult)
         TS(A("F2"), A("SLf", 0, 18), A("NT", 0, 1), A("NM", 1, 2), O.is_ge, O.mult)
         TS(A("F3"), A("SLf", 0, 18), A("NT", 1, 2), A("NM", 1, 2), O.is_ge, O.mult)

@@ -12,25 +12,25 @@ FAR = 2.0 ** 20
 F32, B16, F16, I32, U16 = "float32", "bfloat16", "float16", "int32", "uint16"
 _OWN = {
     "X": (W, B16), "FW": (FWW, F32), "GI": (S, B16), "G0": (S + CAP, B16), "G1": (S + CAP, B16), "YG": (S, B16),
-    "wti": (3, I32), "kmi": (8, I32), "thi": (1, I32), "LW": (512, F32), "U2": (512, F32), "YC": (512, F32), "XF": (512, F32),
-    "UL": (512, F32), "C": (512, I32), "OFF": (512, U16),
+    "wti": (3, I32), "kmi": (8, I32), "thi": (1, I32), "LW": (512, F32), "U2": (512, F32), "YC": (512, F32), "XF": (512, F32), "ZR": (512, F32),
+    "DD": (M * S, B16), "RR": (M * S, B16), "C": (512, I32), "OFF": (512, U16),
 }
 for _r in range(RO):
-    _OWN.update({"X0%d" % _r: (512, B16), "RK%d" % _r: (96, F32), "SP%d" % _r: (96, B16), "ST%d" % _r: (192, B16), "RI%d" % _r: (8, F32), "RJ%d" % _r: (8, F32),
-                 "Z%d" % _r: (ARR + S, B16)})
+    _OWN.update({"X0%d" % _r: (512, B16), "RK%d" % _r: (96, B16), "ST%d" % _r: (ARR, B16), "RI%d" % _r: (16, B16), "RJ%d" % _r: (16, B16),
+                 "Z%d" % _r: (ARR + CAP + S, B16)})
 _PART = {
     F32: {"wtf": 3, "kmf": 8, "th16": 1, "one": 128, "GB": 128, "GBt": 128, "nGB": 128, "nGB8": 128, "SI": 96, "B0": 128, "ID": 128, "USf": 128, "LSf": 128,
           "PI": 1, "P512": 1, "P513": 1, "P5K": 1, "PIN": 1, "LS1": 1, "LB1": 1, "CB": 16, "CW3": 3, "QM": 96, "MW": 96, "RSB": 96, "DMP": 96, "Q0": 96, "Q1": 96, "BI": 64, "QB0": 6, "QB": 6,
-          "BK": 6, "i16": 16, "I16": 16, "LM": 16, "PL0": 512, "PL": 512, "NO": 512, "Uf": 64, "KM": 64, "KT": 128, "F0": 64, "PW": 72, "LWn": 72, "BQ": 6,
-          "KG": 96, "SL": 96, "CG": 96, "SK": 96, "SC": 96, "EG": 96, "EG2": 96, "S1": 96, "S2": 96, "KB": 576, "SGN": 576, "R6": 96, "CUT": 96, "LEN": 96,
+          "BK": 6, "i16": 16, "I16": 16, "LM": 16, "PL0": 512, "LST": 1, "UF": 1, "B15f": 128, "Uf": 64, "KM": 64, "KT": 128, "F0": 64, "PW": 72, "LWn": 72, "BQ": 6,
+          "KG": 96, "SL": 96, "CG": 96, "SK": 96, "SC": 96, "EG": 96, "EG2": 96, "S1": 96, "S2": 96, "KB": 576, "SGN": 576, "R6": 96, "LEN": 96,
           "M1": 96, "M20": 97, "M21": 97, "M22": 97, "M23": 97, "IN": 1, "T1": 6, "T2": 6, "VV": 6, "VR": 6, "SLf": 64, "NT": 2, "NM": 2, "STT": 512, "OF": 16, "FM": 16, "UI": 1},
-    B16: {"oneb": 128, "GBb": 128, "GBK": 128, "nUS": 128, "LSK": 128, "IDb": 128, "IDh": 128, "IDK": 128, "nIDb": 128, "IDE": 128, "B0e": 128, "C23": 192, "RS6": 576, "JV": 576, "RS4": 384, "JW": 384, "OH": 96, "GBi": 128, "TSL": 144, "T32": 144, "Tn16": 144,
+    B16: {"oneb": 128, "GBb": 128, "GBK": 128, "nUS": 128, "LSK": 128, "IDb": 128, "IDh": 128, "IDK": 128, "nIDb": 128, "IDE": 128, "B0e": 128, "B15": 128, "NMb": 1, "CUT": 96, "NO": 512, "C23": 96, "RS6": 576, "JV": 576, "RS4": 384, "JW": 384, "OH": 96, "GBi": 128, "TSL": 144, "T32": 144, "Tn16": 144,
           "WS0": 144, "WS1": 144, "WS2": 144, "it0": 128, "ITH": 128, "ROW": 65, "SLh": 64, "SLi": 64, "FL": 512, "M2C": 512, "MK": 96, "Q0b": 96, "C8K": 512, "N4": 512, "TWO": 512,
-          "DD": M * S, "RR": M * S,
-          "FIT": 64, "CS": 64, "JK": 384, "JL": 576, "SPQ": 112, "STQ": 208, "INV": 96, "KL": 576, "CW": 11, "LE": 390, "EQ": 390, "TA": 768, "GQ": 112, "PG": 96, "PN": 96,
+
+          "FIT": 64, "CS": 64, "JK": 384, "JL": 576, "SPQ": 112, "STQ": 208, "INV": 96, "KL": 576, "CW": 11, "LE": 390, "EQ": 390, "EA": 384, "TA": 768, "GQ": 112, "PG": 96, "PN": 96,
           "TG": 192, "TN": 192, "F1": 18, "F2": 18, "F3": 18, "SG0": 512, "SG1": 512},
     I32: {"pi": 1, "pi2": 1, "Ui": 64, "Um": 64, "UU": 64, "FQ": 64, "CA": 512, "KMi": 64, "PAR": 64, "MX": 64, "KD": 72},
-    F16: {"GB32": 128, "LG": 96},
+    F16: {"GB32": 128, "LG": 96, "PL": 512, "UL": 512},
     U16: {"BQo": 6, "LO": 6, "UO": 6, "UO2": 6, "PO": 6, "TO": 12, "KIu": 12, "ROu": 6, "SQ": 6, "IXu": 64, "FX": 64},
 }
 _AT, SCRATCH = {}, {n: ("sbuf", [128, c], d) for n, (c, d) in _OWN.items()}
@@ -42,15 +42,18 @@ for _d, _n in ((F32, "SF"), (B16, "SB"), (I32, "SJ"), (U16, "SU"), (F16, "SH")):
     SCRATCH[_n] = ("sbuf", [128, _c], _d)
 _PS = ["pA", "pB", "pM", "pN", "pK0", "pK1", "pD0", "pD1"]
 SCRATCH.update({n: ("psum", [128, 512], F32) for n in _PS})
-SEMAPHORES = ["sv", "ss", "st", "sg", "loc"] + ["a%s%d" % (k, r) for k in "ijpt" for r in range(RO)] + ["d%d" % k for k in range(30)]
+SEMAPHORES = ["sv", "ss", "st", "sg", "loc"] + ["a%s%d" % (k, r) for k in "ijptu" for r in range(RO)] + ["d%d" % k for k in range(45)]
 
-CUT_AT = 204
-UNITS = [(0, 64, "pK1", 0), (64, 192, "pN", 0), (192, 256, "pM", 0), (256, 320, "pA", 0), (320, 448, "pK0", 0), (448, 512, "pB", 0)]
-LINE_V = [("get", 448, 512), ("get", 320, 384), ("get", 384, 448), ("cut", 448, 512), ("cut", 320, 448), ("get", CUT_AT, 256), ("get", 256, 288), ("get", 288, 320)]
+CUT_AT, CUTS = 204, (192, 208, 208)
+UNITS = [(0, 128, "pN", 0), (128, 192, "pK1", 0), (192, 256, "pM", 0), (256, 320, "pA", 0), (320, 448, "pK0", 0), (448, 512, "pB", 0)]
+LINE_V = [("get", 448, 512), ("tab", 1, 1), ("get", 320, 384), ("tab", 2, 2), ("get", 384, 448), ("tab", 3, 3), ("cut", 448, 512), ("cut", 320, 448), ("tab", 4, 4), ("get", CUT_AT, 256),
+          ("min", 0, 128), ("get", 256, 288), ("min", 320, 448), ("min", 448, 512), ("get", 288, 320), ("min", 128, 192), ("tab", 5, 5), ("min", -1, -1), ("min", 192, 256), ("min", 256, 320)]
 LINE_S = [("get", 0, 32), ("get", 32, 64), ("cut", 0, 32), ("get", 64, 96), ("cut", 32, 64), ("get", 96, 128), ("cut", 64, 96), ("get", 128, 160), ("cut", 96, 128),
           ("get", 160, 192), ("cut", 128, 160), ("get", 192, CUT_AT), ("cut", 160, 192), ("cut", 192, CUT_AT), ("cut", CUT_AT, 256), ("cut", 256, 288), ("cut", 288, 320)]
 _C = {"cy": np.array([0.88, 1.15, 0.92, 0.85]), "gath": np.array([1.56, 1.95, 1.1, 1.56]), "scat": np.array([3.8, 5.0, 2.0, 3.8]), "pe": np.array([0.45, 0.58, 0.47, 0.43]),
-      "far": np.array([1.0, 1.2, 1.0, 0.6]), "rfar": np.array([1.0, 1.3, 1.4, 0.7]), "hop": 150.0, "own": 120.0, "dma": 1800.0, "rem": 2800.0, "soon": 1.0, "u2s": 0, "o1": 32, "o2": 40, "ks": 4, "js": 4, "spv": 0, "passes": 4, "shakes": 0, "swaps": 4000, "heat": 30.0, "seed": 1, "weigh": 0.4, "vlate": 1000.0}
+      "far": np.array([1.0, 1.3, 1.2, 0.7]), "rfar": np.array([1.0, 1.4, 1.6, 0.7]), "hop": 200.0, "own": 170.0, "dma": 1500.0, "rem": 2200.0,
+      "loose": ("sc", "x0"), "les": 0, "wide": 1, "mode": 1, "adds": 1200.0, "soon": 1.0, "o1": 32, "o2": 40, "o3": (20, 34), "ks": 4, "js": 6, "spv": 0,
+      "passes": 4, "shakes": 0, "swaps": 10000, "heat": 30.0, "seed": 2, "weigh": 0.4, "vlate": 1000.0}
 _ORDER = []
 
 
@@ -61,11 +64,13 @@ def _queues(g, T):
     lines = {}
     cy = _C["cy"]
 
-    def A(n, a=0, b=None, s=1, rows=None):
+    def A(n, a=0, b=None, s=1, rows=None, part=None):
         m, off, w = _AT[n] if n in _AT else (n, 0, T[n].shape[1])
         b = w if b is None else b
         a, b, t = a + off, b + off, T[m]
-        if rows is not None:
+        if part is not None:
+            ap = t[part, a:b:s]
+        elif rows is not None:
             ap = t[rows, a:b]
         elif s < 0:
             ap = t[:, ::-1] if a == 0 and b == t.shape[1] else t[:, b - 1:a - 1:-1]
@@ -128,10 +133,11 @@ def _queues(g, T):
         ops.append((q, as_q, o, i, emit, busy, lat, chain, list(after)))
         return len(ops) - 1
 
-    def LINE(name):
-        if name in lines:
+    def LINE(name, joins=True, waits=True):
+        if name in lines and waits and name not in _C["loose"]:
             ops[-1][8].append(lines[name])
-        lines[name] = len(ops) - 1
+        if joins:
+            lines[name] = len(ops) - 1
 
     def run(q, outs, ins, call, busy, chain=False):
         o, i = split(outs, ins)
@@ -154,7 +160,7 @@ def _queues(g, T):
             return 50 + cy * _C["scat"] * o[3]
         if ins and ins[0][5]:
             return 50 + cy * _C["gath"] * o[3]
-        r = 0.5 if all(x[4] in (B16, U16) for x in (o,) + ins) else 1.0
+        r = 0.5 if all(x[4] in (B16, U16, F16) for x in (o,) + ins) else 1.0
         if tt and all(x[1][0][0] not in _PS for x in ins):
             r *= 2
         return cy * max(64, r * max(x[3] for x in (o,) + ins))
@@ -211,35 +217,35 @@ def _queues(g, T):
         run("g", [o], [a], lambda: g.affine_select(o[0], a[0], pat, op, 0.0, base, cm), 170 + 2 * cy * o[3])
         LINE("g")
 
-    def DMA(q, o, a, lat=0.0, after=()):
-        os_, is_ = split([o], [a])
+    def DMA(q, o, a, lat=0.0, after=(), adds=False, behind=()):
+        os_, is_ = split([o], [a, *behind])
 
         def emit():
             need(q, os_, is_)
             sem = "d%d" % no[1]
             no[1] += 1
-            Q[q].dma_start(o[0], a[0]).then_inc(T.sem[sem], 16)
+            (g.dma_start(o[0], a[0], accum_op=O.add) if adds else Q[q].dma_start(o[0], a[0])).then_inc(T.sem[sem], 16)
             cnt[sem] = 16
             clk = dict(seen[q])
             clk[sem] = 16
             note("dma", sem, 16, clk, os_, is_)
-        return add(q, "dma", os_, is_, emit, 60.0, _C["dma"] + lat, False, after)
+        return add(q, "dma", os_, is_, emit, 900.0 if adds else 60.0, _C["dma"] + lat, False, after)
 
-    def SEND(srcs, engines, call):
-        o, i = split([], srcs)
+    def SEND(srcs, engines, call, loc="loc", frees=()):
+        o, i = split(frees, srcs)
 
         def emit():
             need("g", o, i)
             call()
-            cnt["loc"] = cnt.get("loc", 0) + engines
-            note("rem", "loc", cnt["loc"], {}, o, i)
+            cnt[loc] = cnt.get(loc, 0) + engines
+            note("rem", loc, cnt[loc], {}, [], i)
         return add("g", "rem", o, i, emit, 400.0, 0.0)
 
-    def LAND(dst, sem, val, sent):
+    def LAND(dst, sem, val, sent, lat=0.0):
         def emit():
             cnt[sem] = val
             note("rem", sem, val, {sem: val}, list(dst[1]), [])
-        add(None, "rem", list(dst[1]), [], emit, 0.0, _C["rem"], False, (sent,))
+        add(None, "rem", list(dst[1]), [], emit, 0.0, lat or _C["rem"], False, (sent,))
 
     def order():
         n, book, bank = len(ops), {}, {}
@@ -378,7 +384,8 @@ def _queues(g, T):
                 w = why[k]
                 if w < -1:
                     w = -2 - w
-                    stood.append((w, k))
+                    if w not in pre[k] and (suc[w] != suc[k] or b0[w] != b0[k]):
+                        stood.append((w, k))
                 k = w
             return total, stood, (end, why)
 
@@ -445,10 +452,10 @@ def rank_program(g, core, T, topo):
     d0 = DMA("y", A("GI"), XT(T.gd[:, :]), 800)
     d1 = DMA("s", A("wti"), XT(T.wt[:, :]))
     d1 = DMA("s", A("kmi"), XT(T.km[:, :]), 200, [d1])
-    d1 = DMA("s", A("thi"), XT(T.th[:, :]), 400, [d1])
     d0 = DMA("y", A("X00"), XT(T.xs[0::16, :]), 1400, [d0])
-    DMA("s", A("X", W // 2, W), XT(T.xs[:, W // 2:W]), 7500, [d1])
-    DMA("y", A("X", 0, W // 2), XT(T.xs[:, 0:W // 2]), 7500, [d0])
+    d1 = DMA("s", A("X", W // 2, W), XT(T.xs[:, W // 2:W]), 5500, [d1])
+    DMA("s", A("thi"), XT(T.th[:, :]), 7500, [d1])
+    d0 = DMA("y", A("X", 0, W // 2), XT(T.xs[:, 0:W // 2]), 5500, [d0])
 
     MS(A("one"), 1.0)
     MS(A("oneb"), 1.0)
@@ -458,6 +465,8 @@ def rank_program(g, core, T, topo):
     AFF(A("ID"), A("GB"), [[-1, 128]], O.is_equal, 0, 1)
     for n, c in enumerate((0.5, 383.0 * BIG, 255.0, 2.0 ** 23 + 255)):
         MS(A("CB", n, n + 1), c)
+    MS(A("CB", 6, 7), float(CAP))
+    MS(A("CB", 8, 9), float(CAP * (1 + (_C["mode"] == 1))))
     TS(A("pi2"), A("pi"), 15, None, O.bitwise_and)
     TC(A("PI"), A("pi2"))
     TC(A("wtf"), A("wti"))
@@ -471,37 +480,40 @@ def rank_program(g, core, T, topo):
     MMS(A("pN", 0, 3), (A("GB"), A("wtf")))
     TS(A("CW3"), A("pN", 0, 3), 255.0, None, O.mult)
     TS(A("G0", 0, S), A("GI"), -1.0, 255.0, O.mult, O.add)
+    IOTA(A("i16"), [[1, 16]], 0, 0)
+    IOTA(A("PL0"), [[1, 512]], 2, 0)
     IOTA(A("QM"), [[0, 6], [1, 16]], 0, 0)
+    IOTA(A("QB0"), [[16, 6]], 0, 0)
+    IOTA(A("BI"), [[1, 64]], 0, 0)
     AFF(A("B0"), A("GB"), [[-16, 8], [0, 16]], O.is_equal, 0, 1)
     AFF(A("USf"), A("GB"), [[-1, 128]], O.is_gt, 0, 1)
     AFF(A("LSf"), A("GB"), [[1, 128]], O.is_gt, 0, -1)
-    IOTA(A("PL0"), [[1, 512]], 2, 0)
-    IOTA(A("QB0"), [[16, 6]], 0, 0)
-    IOTA(A("BI"), [[1, 64]], 0, 0)
-    IOTA(A("i16"), [[1, 16]], 0, 0)
+    AFF(A("B15f"), A("GB"), [[-16, 8], [0, 16]], O.is_equal, -15, 1)
     IOTA(A("it0"), [[0, 8], [1, 16]], 0, 0)
     for n, c, base in (("Q0", 96, 0), ("Q1", 96, 1), ("Q0b", 96, 0)):
         IOTA(A(n), [[1, c]], base, 0)
     IOTA(A("ROW"), [[16, 65]], -8, 0)
     IOTA(A("SLh"), [[16, 64]], 0, 0)
-    IOTA(A("M2C"), [[2, 8], [0, 64]], 0, 0)
-    for n, c in (("KD", 0), ("PW", -1.0), ("LWn", 0.0), ("C8K", STEP), ("C23", 2.0 ** 23), ("N4", -4.0), ("TWO", 2.0), ("CW", 0.0), ("RSB", -4 * FAR), ("DMP", -1.0), ("U2", 0.0)):
+    for m in range(M):
+        ACT(A("M2C", 64 * m, 64 * m + 64), A("oneb", 0, 64), CP, scale=2.0 * m)
+    for n, c in (("KD", 0), ("PW", -1.0), ("LWn", 0.0), ("C8K", STEP), ("C23", 2.0 ** 23), ("N4", -4.0), ("TWO", 2.0), ("CW", 0.0), ("RSB", -4 * FAR), ("DMP", -1.0), ("ZR", 0.0)):
         MS(A(n), c)
     for n, a, b in (("GQ", 96, 112), ("SPQ", 96, 112), ("STQ", 192, 208), ("G0", S, S + CAP), ("G1", S, S + CAP)):
         MS(A(n, a, b), 0.0)
     for a in range(0, 4096, 512):
-        ACT(A("FW", a, a + 512), A("U2"), CP)
+        d0 = DMA("y", A("FW", a, a + 512), A("ZR"), 1.3 * a, [d0], behind=[A("X")])
     for a in range(4096, FWW, 526):
         IOTA(A("FW", a, a + 526), [[0, 526]], 0, 0)
     for n, a, c in (("IDb", "ID", 1.0), ("nIDb", "ID", -1.0), ("GBb", "GB", 1.0), ("nUS", "USf", -1.0), ("nGB8", "GB", -8.0), ("nGB", "GB", -1.0),
-                    ("GBK", "GB", BIG), ("IDK", "ID", BIG), ("IDh", "ID", 0.5)):
+                    ("B15", "B15f", 1.0), ("GBK", "GB", BIG), ("IDK", "ID", BIG), ("IDh", "ID", 0.5)):
         ACT(A(n), A(a), CP, scale=c)
     TS(A("GBt"), A("ID"), 4096.0, None, O.mult)
     TT(A("LSK"), A("GBt"), A("LSf"), O.add)
     TS(A("th16"), A("thi"), 16.0, None, O.mult)
     TS(A("P512"), A("PI"), 512.0, None, O.mult)
     TS(A("P513"), A("PI"), 512.0, 1.0, O.mult, O.add)
-    TS(A("PIN"), A("PI"), 512.0, 0.25, O.mult, O.add)
+    TS(A("PIN"), A("PI"), 512.0 * STEP, 0.25 * STEP, O.mult, O.add)
+    TS(A("CB", 7, 8), A("PI"), -2048.0, None, O.mult)
     TS(A("P5K"), A("P513"), 10000.0, None, O.mult)
     TC(A("M20", 96, 97), A("P513"))
     TS(A("CB", 4, 5), A("PI"), 2.0, None, O.is_equal)
@@ -509,7 +521,7 @@ def rank_program(g, core, T, topo):
     TS(A("LB1"), A("CB", 4, 5), -4.0 - 1.25 * STEP, 1.25 * STEP, O.mult, O.add)
     TS(A("B0e"), A("B0"), 2.0 ** -9, None, O.mult)
     TT(A("IDE"), A("B0e"), A("ID"), O.max)
-    TS(A("PL"), A("PL0"), A("P512"), None, O.add)
+    TC(A("PL"), A("PL0"))
     TS(A("MK"), A("QM"), A("PI"), FAR, O.not_equal, O.mult)
     MS(A("RSB", 0, 96, 16), 2 * FAR)
     if _C["js"] < 6:
@@ -524,12 +536,12 @@ def rank_program(g, core, T, topo):
         MS(A("RS4"), 1.0)
         MS(A("RS4", 0, 384, 64), 0.0)
     TS(A("I16"), A("i16"), A("PI"), None, O.is_equal)
-    TS(A("LM"), A("i16"), A("PI"), BIG, O.is_le, O.mult)
+    TS(A("LM"), A("i16"), A("PI"), W + 1.0, O.is_le, O.mult)
     TS(A("SLi"), A("oneb", 0, 64), A("PI"), None, O.mult)
     TS(A("SLf"), A("SLh"), A("PI"), None, O.add)
     TS(A("GBt"), A("GB"), 8192.0, -8192.0 - 7.5, O.mult, O.add)
     TT(A("ITH"), A("GBt"), A("it0"), O.add)
-    TC(A("XF"), A("X00"))
+    ACT(A("XF"), A("X00"), CP)
     DMA("y", A("FW", 1, W + 1, rows=slice(1, 128, 16)), A("XF"), 500)
 
     def sel(n, i):
@@ -559,16 +571,14 @@ def rank_program(g, core, T, topo):
 
         def flag(a, b):
             TS(A("FL", 64 * a, 64 * b), A("OFF", 64 * a, 64 * b), W - 96.0, None, O.is_ge)
-        for f, *args in ((sums, 0), (rest, 0, 1), (offs, 0, 1), (sums, 1), (sums, 2), (sums, 3), (sums, 4), (sums, 5), (sums, 6), (sums, 7), (rest, 4, 8),
-                         (rest, 1, 4), (offs, 4, 8), (offs, 1, 4), (flag, 4, 8), (flag, 0, 4)):
+        for f, *args in ((sums, 0), (rest, 0, 1), (offs, 0, 1), (sums, 1), (sums, 2), (sums, 3), (sums, 4), (sums, 5), (sums, 6), (sums, 7), (rest, 1, 4),
+                         (rest, 4, 8), (offs, 1, 4), (offs, 4, 8), (flag, 0, 4), (flag, 4, 8)):
             f(*args)
             LINE("v")
 
     def scores(r):
         G = "G%d" % (r % 2)
-        left = [M] * 64
-
-        held, pairs = {}, [0, sum(1 for u in UNITS if u[1] - u[0] == 128)]
+        seen, pairs = [0, 0], [u for u in UNITS if u[1] - u[0] == 128]
 
         def rows(u, src, by, stop):
             a, b, bank, at = u
@@ -586,49 +596,58 @@ def rank_program(g, core, T, topo):
             if D:
                 rows(u, "DD", "Tn16", False)
 
-        def closes(u):
-            a, b, bank, at = u
-            rows(u, "RR", "T32", True)
-            if b - a == 128:
-                pairs[0] += 1
-                if pairs[0] == 1:
+        def least(key):
+            seen[1] += 1
+            if seen[1] == 1:
+                TS(A("KM"), key, FAR, None, O.min)
+            else:
+                TT(A("KMi" if seen[1] == len(UNITS) + 2 - len(pairs) else "KM"), key, A("KM"), O.min)
+            LINE("v")
+
+        def lower(a, b):
+            bank, at = ([u[2:] for u in UNITS if u[0] == a] + [pairs[-1][2:]])[0]
+            if a < 0:
+                least(A(bank, at + 128, at + 192))
+                least(A(bank, at + 192, at + 256))
+            elif b - a == 64:
+                least(A(bank, at, at + 64))
+            else:
+                seen[0] += 1
+                if seen[0] == 1:
                     TS(A("KT"), A(bank, at, at + 128), FAR, None, O.min)
                 else:
                     TT(A("KT"), A(bank, at, at + 128), A("KT"), O.min)
-                if pairs[0] < pairs[1]:
-                    return
-                for x in range(64):
-                    left[x] -= 2 * pairs[1] - 2
-                at += 128
-                MMS(A(bank, at, at + 128), (A("KT"), A("ID")))
-            held.setdefault(bank, []).append((a, b, bank, at))
-            if len(held[bank]) < sum(1 for x in UNITS if x[2] == bank):
-                return
-            for a, b, bank, at in held[bank]:
-                c = a
-                while c < b:
-                    e = c + 1
-                    while e < b and e % 64 and (left[e % 64] == 1) == (left[c % 64] == 1) and (e % 64 in held) == (c % 64 in held):
-                        e += 1
-                    key, c0, c1 = A(bank, at + c - a, at + e - a), c % 64, c % 64 + e - c
-                    if c0 not in held:
-                        held.update({x: 1 for x in range(c0, c1)})
-                        TS(A("KM", c0, c1), key, FAR, None, O.min)
-                    else:
-                        TT(A("KMi" if left[c0] == 1 else "KM", c0, c1), key, A("KM", c0, c1), O.min)
-                    for x in range(c0, c1):
-                        left[x] -= 1
-                    c = e
+                LINE("v")
+                if seen[0] == len(pairs):
+                    MMS(A(pairs[-1][2], pairs[-1][3] + 128, pairs[-1][3] + 256), (A("KT"), A("ID")))
 
         got, done, where, by_v = set(), set(), {}, {c for k, a, b in LINE_V if k == "cut" for c in range(a, b)}
+        lines = {q: [(k,) + tuple(CUTS[r] if x == CUT_AT else x for x in ab) for k, *ab in line] for q, line in (("v", LINE_V), ("s", LINE_S))}
+        lines = {q: [x for x in line if x[1] < x[2] or x[0] in ("min", "tab")] for q, line in lines.items()}
         t, at = {"v": _C["vlate"], "s": 0.0}, {"v": 0, "s": 0}
-        while at["v"] < len(LINE_V) or at["s"] < len(LINE_S):
-            can = [q for q, line in (("v", LINE_V), ("s", LINE_S)) if at[q] < len(line) and (line[at[q]][0] == "get" or got.issuperset(range(*line[at[q]][1:])))]
+        while any(at[q] < len(lines[q]) for q in at):
+            can = [q for q, line in lines.items() if at[q] < len(line) and {"get": set(range(512)), "raw": set(range(512)), "cut": got, "min": done, "tab": got}[line[at[q]][0]].issuperset(range(*line[at[q]][1:]))]
             q = min(can, key=lambda q: t[q])
-            k, a, b = (LINE_V if q == "v" else LINE_S)[at[q]]
+            k, a, b = lines[q][at[q]]
             at[q] += 1
-            t[q] += (b - a) * (24 if k == "get" else 8 if q == "v" else 16)
-            d, mine = A("DD", 16 * a, 16 * b), k == "get" and A(G, 16 * (a % 64), 16 * (a % 64 + b - a))
+            if k == "min":
+                lower(a, b)
+                continue
+            if k == "tab":
+                if r:
+                    utable(r, a)
+                continue
+            t[q] += (b - a) * (24 if k != "cut" else 8 if q == "v" else 16)
+            d, mine = A("DD", 16 * a, 16 * b), k != "cut" and A(G, 16 * (a % 64), 16 * (a % 64 + b - a))
+            if k == "raw":
+                ACT(d, IND(A("X"), A("OFF", a, b)), CP, scale=-1.0)
+                LINE(q)
+                DMA("g", d, mine, _C["adds"], adds=True)
+                got.update(range(a, b))
+                for u in UNITS:
+                    if u[0] < b and a < u[1] and got.issuperset(range(u[0], u[1])):
+                        opens(u, True)
+                continue
             if k == "get" and q == "v":
                 TT(d, IND(A("X"), A("OFF", a, b)), mine, O.subtract)
             elif k == "get":
@@ -640,7 +659,8 @@ def rank_program(g, core, T, topo):
             LINE(q)
             if k == "get" and q == "s":
                 where[a] = A("pD%d" % (len(where) % 2), 0, 16 * (b - a))
-                MMS(where[a], (A("nIDb"), mine), (A("IDb"), d))
+                MMS(where[a], (A("nIDb"), mine), stop=False)
+                MMS(where[a], (A("IDb"), d), start=False)
             for u in UNITS:
                 if u[0] < b and a < u[1]:
                     if k == "get" and u[0] in by_v and (got | set(range(a, b))).issuperset(range(u[0], u[1])):
@@ -648,25 +668,33 @@ def rank_program(g, core, T, topo):
                     if k == "cut" and (done | set(range(a, b))).issuperset(range(u[0], u[1])):
                         if u[0] not in by_v:
                             opens(u, False)
-                        closes(u)
+                        rows(u, "RR", "T32", True)
             (got if k == "get" else done).update(range(a, b))
 
     def own(dst, bank):
         SCAN(A(dst), A("RSB"), A(bank, 0, 96), 0.0, O.max, O.min)
 
-    def utable(r):
-        ACT(A("NO"), A("X0%d" % r), RL, bias=A("CB", 1, 2), scale=-2 * BIG)
-        SCAN(A("UL", s=-1), A("NO", s=-1), A("PL", s=-1), float(W + 1), O.min, O.max)
-        TS(A("OF"), A("I16"), A("UL", 0, 1), None, O.mult)
-        MMS(A("pA", 256, 272), (A("GB"), A("OF")))
-        TT(A("FM"), A("pA", 256, 272), A("LM"), O.max)
-        RED(A("UI"), A("FM"), O.min)
-        if _C["u2s"] and r:
-            ACT(A("NO"), A("UL"), RL, bias=A("UI"), scale=-1.0)
-            ACT(A("U2"), A("NO"), IDN, bias=A("UI"), scale=-1.0)
+    def utable(r, k):
+        if k == 0:
+            ACT(A("NO"), A("X0%d" % r), RL, bias=A("CB", 1, 2), scale=-2 * BIG)
+            SCAN(A("UL", s=-1), A("NO", s=-1), A("PL", s=-1), BIG, O.min, O.max)
+            return
+        if k == 1:
+            TS(A("UF"), A("UL", 0, 1), A("P512"), W + 1.0, O.add, O.min)
+        elif k == 2:
+            TS(A("OF"), A("I16"), A("UF"), None, O.mult)
+        elif k == 3:
+            TT(A("FM"), A("pA", 256, 272), A("LM"), O.max)
+        elif k == 4:
+            RED(A("UI"), A("FM"), O.min)
         else:
-            TS(A("U2"), A("UL"), A("UI"), None, O.min)
-        DMA("y", A("FW", 0, W, rows=slice(0, 128, 16)), A("U2"), 500)
+            TS(A("U2"), A("UL"), A("P512"), A("UI"), O.add, O.min)
+        if r:
+            LINE("v")
+        if k == 2:
+            MMS(A("pA", 256, 272), (A("GB"), A("OF")))
+        if k == 5:
+            DMA("y", A("FW", 2, W + 2, rows=slice(0, 128, 16)), A("U2"), 500)
 
     near, far = T.cores[rank ^ 1], T.cores[rank ^ 2]
 
@@ -682,15 +710,16 @@ def rank_program(g, core, T, topo):
         G, H = "G%d" % (r % 2), "YG" if last else "G%d" % ((r + 1) % 2)
         RK, SP, STn, RI, RJ, Z, M2, M3 = ("%s%d" % (n, k) for n, k in (("RK", r), ("SP", r), ("ST", r), ("RI", r), ("RJ", r), ("Z", r), ("M2", r), ("M2", r + 1)))
         lists(r)
-        utable(r)
+        for k in range(1 if r else 6):
+            utable(r, k)
         scores(r)
         TS(A("PAR"), A("KMi"), 1, None, O.bitwise_and)
         TS(A("F0"), A("KMi"), A("th16"), None, O.is_lt)
         TT(A("FIT"), A("F0"), A("PAR"), O.is_gt)
         SCAN(A("CS"), A("oneb", 0, 64), A("FIT"), 0.0, O.mult, O.add)
         MMS(A("pB", 0, 64), (A("GBb"), A("CS")))
-        MMS(A("pM", 0, 64), (A("GBb"), A("CS")), (A("nUS"), A("FIT")))
         MMS(A("pM", 64, 128), (A("GBb"), A("CS")))
+        MMS(A("pD1", 0, 64), (A("nUS"), A("FIT")), (A("GBb"), A("CS")))
         ks = _C["ks"]
         for a in range(ks):
             ACT(A("JK", 64 * a, 64 * a + 64), A("pB", 0, 64), AF.Sign, bias=A("QB", a, a + 1), scale=-1.0, acc=A("BQ", a, a + 1))
@@ -705,7 +734,7 @@ def rank_program(g, core, T, topo):
         TS(A("MX"), A("KMi"), 14, None, O.bitwise_and)
         TS(A("KD", 0, 64), A("KMi"), 65520, None, O.bitwise_and)
         TT(A("LWn", 0, 64), A("MX"), A("BI"), O.add)
-        TT(A("PW", 0, 64), A("pM", 0, 64), A("FIT"), O.mult)
+        TT(A("PW", 0, 64), A("pD1", 0, 64), A("FIT"), O.mult)
         TS(A("INV"), A("Q0"), A("pM", 127, 128), 2.0 ** -14, O.is_ge, O.add)
         inv = (A("IDK"), A("INV"))
 
@@ -731,26 +760,28 @@ def rank_program(g, core, T, topo):
         own("SC", "pA")
         for a in range(6):
             ACT(A("KB", 96 * a, 96 * a + 96), A("SGN", 96 * a, 96 * a + 96), CP, scale=A("SC", 16 * a + 15, 16 * a + 16))
-        TS(A("UO"), A("SC", *q6), 15.0, W - 1.0, O.add, O.min)
-        TC(A("EG"), IND(A("FW"), A("UO")))
+        TS(A("PO"), A("SC", *q6), 9.0, W - 7.0, O.add, O.min)
+        TC(A("EG"), IND(A("FW", 8, FWW), A("PO")))
         two(A("pM", 0, 96), [mk], [(A("B0"), A("EG"))])
         own("S1", "pM")
-        TS(A("UO2"), A("S1", *q6), 6.0, W - 1.0, O.add, O.min)
+        TS(A("UO2"), A("S1", *q6), 8.0, W + 1.0, O.add, O.min)
         TC(A("EG2"), IND(A("FW"), A("UO2")))
         two(A("pN", 0, 96), [mk], [(A("B0"), A("EG2"))])
         own("S2", "pN")
         TS(A("TO", 0, 6), A("S1", *q6), -2.0, None, O.add)
         TS(A("TO", 6, 12), A("S2", *q6), -2.0, None, O.add)
-        TS(A("PO"), A("SC", *q6), 9.0, W - 1.0, O.add, O.min)
         ACT(A("PG"), IND(A("X"), A("PO")), AF.Abs)
         two(A("pD0", 0, 96), [(A("IDb"), A("C23", 0, 96))], [(A("IDE"), A("PG"))])
         ACT(A("SPQ", 0, 96), A("pD0", 0, 96), RL, bias=A("CB", 3, 4), scale=-1.0)
         two(A("pD0", 96, 192), [(A("nGB"), A("CG"))], [(A("B0"), A("EG2"))])
         ACT(A("LEN"), A("pD0", 96, 192), IDN, bias=A("LB1"), scale=A("LS1"))
         MMS(A("pM", 96, 192), (A("B0"), A("EG2")))
-        ACT(A("TG"), IND(A("X"), A("TO")), AF.Abs)
-        two(A("pD1", 0, 192), [(A("IDb"), A("C23"))], [(A("IDE"), A("TG"))])
-        ACT(A("STQ", 0, 192), A("pD1", 0, 192), RL, bias=A("CB", 3, 4), scale=-1.0)
+        if r:
+            MMS(A("pD1", 0, 2), (A("B15"), A("X0%d" % r, 510, 512)))
+            ACT(A("LST"), A("pD1", 1, 2), RL, scale=-1.0)
+            TS(A("X", W - 1, W), A("X", W - 1, W), A("LST"), None, O.max)
+        for h in range(2):
+            ACT(A("STQ", 96 * h, 96 * h + 96), IND(A("X"), A("TO", 6 * h, 6 * h + 6)), RL, bias=A("CB", 2, 3), scale=-1.0)
         TT(A("T2"), A("SI", *q6), A("T1"), O.add)
         TS(A("SQ"), A("T2"), -4088.5, S - 1.0, O.add, O.min)
         ACT(A("GQ", 0, 96), IND(A(G, 0, S), A("SQ")), CP)
@@ -763,8 +794,8 @@ def rank_program(g, core, T, topo):
             MM(A("pK1", 0, 96), A("GBK"), A("KL", 96 * a, 96 * a + 96), False, a == 5)
             MM(A("pK0", 0, 96), A("GBK"), A("KL", 96 * a, 96 * a + 96), False, a == 5)
         TS(A("CUT"), A("pK1", 0, 96), 1.5, None, O.is_lt)
-        SCAN(A(RK), A("one", 0, 96), A("CUT"), 0.0, O.mult, O.add)
-        cnts = A(RK, 88, 96)
+        SCAN(A(RK), A("oneb", 0, 96), A("CUT"), 0.0, O.mult, O.add)
+        cnts = A(RK, 80, 96)
         k = SEND([cnts], 2 * hn, lambda: g.remote_dma_fused([to(near, en[:hn], "ai%d" % r, cnts, A(RI)), to(far, ef[hn:], "aj%d" % r, cnts, A(RJ))], local_sem=T.sem["loc"]))
         LAND(A(RI), "ai%d" % r, hn, k)
         LAND(A(RJ), "aj%d" % r, len(ef) - hn, k)
@@ -775,52 +806,69 @@ def rank_program(g, core, T, topo):
             TS(A("JL", 96 * a, 96 * a + 96), A(RK), A("QB", a, a + 1), None, O.is_le)
         if js:
             TS(A("KIu", 0, js), A("BK", 0, js), 0.5, 48.0, O.mult, O.add)
-            TS(A("KIu", 6, 6 + js), A("BK", 0, js), 0.5, 144.0, O.mult, O.add)
         if js < 6:
             SCAN(A("JV", 96 * js, 576), A("RS6", 96 * js, 576), A("JL", 96 * js, 576), 0.0, O.mult, O.add)
             TC(A("KIu", js, 6), A("JV", 96 * js + 95, 576, 96))
-            TS(A("KIu", 6 + js, 12), A("JV", 96 * js + 95, 576, 96), 96.0, None, O.add)
-        if _C["spv"]:
-            TC(A(SP), IND(A("SPQ"), A("KIu", 0, 6)))
-        else:
-            ACT(A(SP), IND(A("SPQ"), A("KIu", 0, 6)), CP)
-        k = SEND([A(SP)], len(en), lambda: g.remote_dma_fused([to(near, en, "ap%d" % r, A(SP), A(Z, 0, 96))], local_sem=T.sem["loc"]))
-        LAND(A(Z, 0, 96), "ap%d" % r, len(en), k)
-        ACT(A(STn), IND(A("STQ"), A("KIu")), CP)
-        k = SEND([A(STn)], len(ef), lambda: g.remote_dma_fused([to(far, ef, "at%d" % r, A(STn), A(Z, 96, ARR))], local_sem=T.sem["loc"]))
-        LAND(A(Z, 96, ARR), "at%d" % r, len(ef), k)
+        for h, win in enumerate((A("SPQ"), A("STQ", 0, 112), A("STQ", 96, 208))):
+            if h < _C["spv"]:
+                TC(A(STn, 96 * h, 96 * h + 96), IND(win, A("KIu", 0, 6)))
+            else:
+                ACT(A(STn, 96 * h, 96 * h + 96), IND(win, A("KIu", 0, 6)), CP)
+        for call in ([[(near, en, "ap", 0, 96, 0)], [(far, ef, "at", 96, ARR, 96)]], [[(near, en[:hn], "ap", 0, 192, 0), (far, ef[hn:], "at", 96, ARR, 192)]],
+                     [[(near, en[:hn], "ap", 0, 96, 0), (far, ef[hn:], "at", 96, 192, 96)], [(far, ef, "au", 192, ARR, 192)]])[_C["mode"]]:
+            k = SEND([A(STn, x[3], x[4]) for x in call], sum(len(x[1]) for x in call), lambda call=call: g.remote_dma_fused(
+                [to(dst, eng, sem + str(r), A(STn, a, b), A(Z, at, at + b - a)) for dst, eng, sem, a, b, at in call], local_sem=T.sem["loc"]))
+            for dst, eng, sem, a, b, at in call:
+                LAND(A(Z, at, at + b - a), sem + str(r), len(eng), k)
         ACT(A(G, S, S + CAP), IND(A("GQ"), A("KIu", 0, 6)), CP)
         SCAN(A("R6"), A("DMP"), A("pK0", 0, 96), 0.0, O.max, O.min)
         TC(A("ROu"), A("R6", *q6))
         TC(IND(A("FW"), A("ROu")), A("LEN"))
+        LINE("sc", True, False)
         DMA("y", A("LW"), A("FW", 1, W + 1, rows=slice(2 if last else 1, 128, 16)), 800)
         ACT(A("M1"), A("pB", 0, 96), RL, bias=A("P5K"), scale=-10000.0)
         TT(A(M2, 0, 96), A("pM", 96, 192), A("M1"), O.min)
         RED(A(M3, 96, 97), A(M2), O.max)
         if last:
-            TS(A("IN"), A(M3, 96, 97), A("P512"), 4.0, O.subtract, O.mult)
+            ACT(A("IN"), A(M3, 96, 97), IDN, bias=A("CB", 7, 8), scale=4.0)
             for k in range(2):
                 ACT(A("SG%d" % k), A("X0%d" % (k + 1)), AF.Sign, bias=A("CB", 0, 1))
             MMS(A("pD1"), (A("IDb"), A("TWO")), (A("IDh"), A("SG0")), (A("IDh"), A("SG1")))
             SCAN(A("STT"), A("N4"), A("LW"), A("IN"), O.add, O.max)
             TT(A("YC"), A("STT"), A("pD1"), O.min)
+            LINE("x0", True, False)
             DMA("s", XT(T.yc[:, :]), A("YC"), 800)
         else:
             X1 = "X0%d" % (r + 1)
-            TS(A("IN"), A(M3, 96, 97), A("PIN"), -STEP, O.subtract, O.mult)
+            ACT(A("IN"), A(M3, 96, 97), IDN, bias=A("PIN"), scale=-STEP)
             SCAN(A(X1), A("C8K"), A("LW"), A("IN"), O.add, O.min)
+            LINE("x0", True, False)
             DMA("y", A("X", 0, W, rows=slice(0, 128, 16)), A(X1), 400)
         TS(A("CW", 5, 11), A("R6", *q6), W + 0.5, None, O.is_lt)
-        MMS(A("pN", 0, 6), (A("LSK"), A("CW", 5, 11)), *[(A("GBb"), A("CW", 5 - s, 11 - s)) for s in range(1, 6)])
-        TT(A("VV"), A("T2"), A("pN", 0, 6), O.subtract)
+        MMS(A("pK1", 128, 134), (A("LSK"), A("CW", 5, 11)), *[(A("GBb"), A("CW", 5 - s, 11 - s)) for s in range(1, 6)])
+        TT(A("VV"), A("T2"), A("pK1", 128, 134), O.subtract)
         TS(A("VR"), A("VV"), 1.5 * 2 ** 27, -1.5 * 2 ** 27, O.add, O.add)
-        for a in range(6):
-            TS(A("LE", 65 * a, 65 * a + 65), A("ROW"), A("VV", a, a + 1), None, O.is_ge)
-        TT(A("EQ", 0, 389), A("LE", 1, 390), A("LE", 0, 389), O.subtract)
+        lw = 64 + _C["wide"]
+        if _C["wide"]:
+            for a in range(6):
+                TS(A("LE", 65 * a, 65 * a + 65), A("ROW"), A("VV", a, a + 1), None, O.is_ge)
+            TT(A("EQ", 0, 389), A("LE", 1, 390), A("LE", 0, 389), O.subtract)
+        for a in range(0 if _C["wide"] else 6):
+            TS(A("LE", 64 * a, 64 * a + 64), A("SLh"), A("VR", a, a + 1), None, O.is_gt)
+            LINE("sc", False)
+            if a < _C["les"]:
+                ACT(A("EA", 64 * a, 64 * a + 64), A("SLh"), AF.Abs, bias=A("VR", a, a + 1), scale=-1.0)
+            else:
+                TS(A("EQ", 64 * a, 64 * a + 64), A("SLh"), A("VR", a, a + 1), None, O.is_equal)
+        if _C["les"]:
+            ACT(A("EQ", 0, 64 * _C["les"]), A("EA", 0, 64 * _C["les"]), RL, bias=A("one", 0, 1), scale=-1.0)
         for a in range(6):
             TS(A("TA", 128 * a, 128 * a + 128), A("ITH"), A("VR", a, a + 1), A("VV", a, a + 1), O.add, O.is_ge)
-        MMS(A("pA", 0, 64), (A("IDb"), A("SLh")), (A("IDb"), A("SLi")), *([(A("GBb"), A("LE", 65 * a, 65 * a + 64)) for a in range(6)]
-                                                                         + [(A("TA", 128 * a, 128 * a + 128), A("EQ", 65 * a, 65 * a + 64)) for a in range(6)]))
+            LINE("sc", False)
+        MMS(A("pA", 0, 64), (A("IDb"), A("SLh")), (A("IDb"), A("SLi")), stop=False)
+        MMS(A("pA", 0, 64), *[(A("GBb"), A("LE", lw * a, lw * a + 64)) for a in range(6)], start=False, stop=False)
+        for a in range(6):
+            MM(A("pA", 0, 64), A("TA", 128 * a, 128 * a + 128), A("EQ", lw * a, lw * a + 64), False, a == 5)
         TC(A("IXu"), A("pA", 0, 64))
 
         def turn(q, out, win, off, flip):
@@ -832,28 +880,32 @@ def rank_program(g, core, T, topo):
                 ACT(out, IND(win, off), IDN, bias=A("CB", 2, 3), scale=-1.0)
             else:
                 ACT(out, IND(win, off), CP)
-        o1, o2 = _C["o1"], _C["o2"]
-        turn("v", A(Z, ARR, ARR + 16 * o1), A(G), A("IXu", 0, o1), True)
-        LINE("n")
-        turn("s", A(Z, ARR + 16 * o1, ARR + S), A(G), A("IXu", o1, 64), True)
-        n1, n2 = A(RI, 7, 8), A(RJ, 7, 8)
-        TT(A("NT", 0, 1), n1, n2, O.add)
-        LINE("n")
-        TT(A("NT", 1, 2), A("NT", 0, 1), n2, O.add)
+        o1, o2 = _C["o3"] if last else (_C["o1"], _C["o2"])
+        ZO = ARR + CAP * (_C["mode"] == 1)
+        turn("v", A(Z, ZO, ZO + 16 * o1), A(G), A("IXu", 0, o1), True)
+        turn("s", A(Z, ZO + 16 * o1, ZO + S), A(G), A("IXu", o1, 64), True)
+        LINE("os", True, False)
+        n1, n2 = A(RI, 15, 16), A(RJ, 15, 16)
+        ACT(A("NT", 1, 2), n2, IDN, bias=n1, scale=2.0)
+        LINE("os")
+        ACT(A("NT", 0, 1), n2, IDN, bias=n1)
+        LINE("os", False)
         TS(A("FX", 18, 64), A("SLf", 18, 64), A("NT", 1, 2), None, O.subtract)
-        turn("v", A(H, ARR, 16 * o2), A(Z, ARR, ARR + S), A("FX", 18, o2), not last)
-        turn("s", A(H, 16 * o2, S), A(Z, ARR, ARR + S), A("FX", o2, 64), not last)
-        TS(A("NM", 0, 1), n1, -1.0, float(CAP), O.mult, O.add)
-        LINE("n")
-        TS(A("NM", 1, 2), n2, -1.0, float(CAP), O.mult, O.add)
-        LINE("n")
-        TS(A("F1"), A("SLf", 0, 18), n1, A("NM", 0, 1), O.is_ge, O.mult)
+        turn("v", A(H, ARR, 16 * o2), A(Z, ZO, ZO + S), A("FX", 18, o2), not last)
+        LINE("x0", False)
+        turn("s", A(H, 16 * o2, S), A(Z, ZO, ZO + S), A("FX", o2, 64), not last)
+        ACT(A("NMb"), n1, IDN, bias=A("CB", 8, 9), scale=-1.0)
+        LINE("os", False)
+        ACT(A("NM", 1, 2), n2, IDN, bias=A("CB", 6, 7), scale=-1.0)
+        LINE("os", False)
+        TS(A("F1"), A("SLf", 0, 18), n1, A("NMb"), O.is_ge, O.mult)
         TS(A("F2"), A("SLf", 0, 18), A("NT", 0, 1), A("NM", 1, 2), O.is_ge, O.mult)
         TS(A("F3"), A("SLf", 0, 18), A("NT", 1, 2), A("NM", 1, 2), O.is_ge, O.mult)
-        MMS(A("pB", 0, 18), *[(A("IDb"), A(n, 0, 18)) for n in ("SLh", "SLi", "F1", "F2", "F3")])
+        two(A("pB", 0, 18), [(A("IDb"), A(n, 0, 18)) for n in ("SLh", "SLi")], [(A("IDb"), A(n, 0, 18)) for n in ("F1", "F2", "F3")])
         TC(A("FX", 0, 18), A("pB", 0, 18))
-        turn("v", A(H, 0, 160), A(Z), A("FX", 0, 10), not last)
-        turn("s", A(H, 160, ARR), A(Z), A("FX", 10, 18), not last)
+        turn("v", A(H, 0, 160), A(Z, 0, ZO + S), A("FX", 0, 10), not last)
+        LINE("x0", False)
+        turn("s", A(H, 160, ARR), A(Z, 0, ZO + S), A("FX", 10, 18), not last)
         if last:
             DMA("y", XT(T.yg[:, ARR:S]), A(H, ARR, S), 500)
             DMA("y", XT(T.yg[:, 0:ARR]), A(H, 0, ARR), 300)

import numpy as np
from concourse.bass import DstId, RemoteDMATransfer
from concourse.mybir import AluOpType as O, ActivationFunctionType as AF, AxisListType

W, S, M, CAP, RO = 8192, 1024, 8, 96, 3
BIG = 16384.0
FWW = W + 112
ARR = 3 * CAP
STEP = 2.0 ** 18
FAR = 2.0 ** 20

F32, B16, F16, I32, U16 = "float32", "bfloat16", "float16", "int32", "uint16"
_OWN = {
    "X": (W, B16), "FW": (FWW, F32), "GI": (S, B16), "G0": (S + CAP, B16), "G1": (S + CAP, B16), "YG": (S, B16),
    "wti": (3, I32), "kmi": (8, I32), "thi": (1, I32), "LW": (512, F32), "U2": (512, F32), "YC": (512, F32), "XF": (512, F32), "ZR": (512, F32),
    "DD": (M * S, B16), "RR": (M * S, B16), "C": (512, I32), "OFF": (512, U16),
}
for _r in range(RO):
    _OWN.update({"X0%d" % _r: (512, B16), "RK%d" % _r: (96, B16), "ST%d" % _r: (ARR, B16), "RI%d" % _r: (16, B16), "RJ%d" % _r: (16, B16),
                 "Z%d" % _r: (ARR + CAP + S, B16)})
_PART = {
    F32: {"wtf": 3, "kmf": 8, "th16": 1, "one": 128, "GB": 128, "GBt": 128, "nGB": 128, "nGB8": 128, "SI": 96, "B0": 128, "ID": 128, "USf": 128, "LSf": 128,
          "PI": 1, "P512": 1, "P513": 1, "P5K": 1, "PIN": 1, "LS1": 1, "LB1": 1, "CB": 16, "CW3": 3, "QM": 96, "MW": 96, "RSB": 96, "DMP": 96, "Q0": 96, "Q1": 96, "BI": 64, "QB0": 6, "QB": 6,
          "BK": 6, "i16": 16, "I16": 16, "LM": 16, "PL0": 512, "LST": 1, "UF": 1, "B15f": 128, "Uf": 64, "KM": 64, "KT": 128, "F0": 64, "PW": 72, "LWn": 72, "BQ": 6,
          "KG": 96, "SL": 96, "CG": 96, "SK": 96, "SC": 96, "EG": 96, "EG2": 96, "S1": 96, "S2": 96, "KB": 576, "SGN": 576, "R6": 96, "LEN": 96,
          "M1": 96, "M20": 97, "M21": 97, "M22": 97, "M23": 97, "IN": 1, "T1": 6, "T2": 6, "VV": 6, "VR": 6, "SLf": 64, "NT": 2, "NM": 2, "STT": 512, "OF": 16, "FM": 16, "UI": 1},
    B16: {"oneb": 128, "GBb": 128, "GBK": 128, "nUS": 128, "LSK": 128, "IDb": 128, "IDh": 128, "IDK": 128, "nIDb": 128, "IDE": 128, "B0e": 128, "B15": 128, "NMb": 1, "CUT": 96, "NO": 512, "C23": 96, "RS6": 576, "JV": 576, "RS4": 384, "JW": 384, "OH": 96, "GBi": 128, "TSL": 144, "T32": 144, "Tn16": 144,
          "WS0": 144, "WS1": 144, "WS2": 144, "it0": 128, "ITH": 128, "ROW": 65, "SLh": 64, "SLi": 64, "FL": 512, "M2C": 512, "MK": 96, "Q0b": 96, "C8K": 512, "N4": 512, "TWO": 512,

          "FIT": 64, "CS": 64, "JK": 384, "JL": 576, "SPQ": 112, "STQ": 208, "INV": 96, "KL": 576, "CW": 11, "LE": 390, "EQ": 390, "EA": 384, "TA": 768, "GQ": 112, "PG": 96, "PN": 96,
          "TG": 192, "TN": 192, "F1": 18, "F2": 18, "F3": 18, "SG0": 512, "SG1": 512},
    I32: {"pi": 1, "pi2": 1, "Ui": 64, "Um": 64, "UU": 64, "FQ": 64, "CA": 512, "KMi": 64, "PAR": 64, "MX": 64, "KD": 72},
    F16: {"GB32": 128, "LG": 96, "PL": 512, "UL": 512},
    U16: {"BQo": 6, "LO": 6, "UO": 6, "UO2": 6, "PO": 6, "TO": 12, "KIu": 12, "ROu": 6, "SQ": 6, "IXu": 64, "FX": 64},
}
_AT, SCRATCH = {}, {n: ("sbuf", [128, c], d) for n, (c, d) in _OWN.items()}
for _d, _n in ((F32, "SF"), (B16, "SB"), (I32, "SJ"), (U16, "SU"), (F16, "SH")):
    _c = 0
    for _k, _w in _PART[_d].items():
        _AT[_k] = (_n, _c, _w)
        _c += -(-_w // 16) * 16
    SCRATCH[_n] = ("sbuf", [128, _c], _d)
_PS = ["pA", "pB", "pM", "pN", "pK0", "pK1", "pD0", "pD1"]
SCRATCH.update({n: ("psum", [128, 512], F32) for n in _PS})
SEMAPHORES = ["sv", "ss", "st", "sg", "loc"] + ["a%s%d" % (k, r) for k in "ijptu" for r in range(RO)] + ["d%d" % k for k in range(45)]

CUT_AT, CUTS = 204, (192, 208, 208)
UNITS = [(0, 128, "pN", 0), (128, 192, "pK1", 0), (192, 256, "pM", 0), (256, 320, "pA", 0), (320, 448, "pK0", 0), (448, 512, "pB", 0)]
LINE_V = [("get", 448, 512), ("tab", 1, 1), ("get", 320, 384), ("tab", 2, 2), ("get", 384, 448), ("tab", 3, 3), ("cut", 448, 512), ("cut", 320, 448), ("tab", 4, 4), ("get", CUT_AT, 256),
          ("min", 0, 128), ("get", 256, 288), ("min", 320, 448), ("min", 448, 512), ("get", 288, 320), ("min", 128, 192), ("tab", 5, 5), ("min", -1, -1), ("min", 192, 256), ("min", 256, 320)]
LINE_S = [("get", 0, 32), ("get", 32, 64), ("cut", 0, 32), ("get", 64, 96), ("cut", 32, 64), ("get", 96, 128), ("cut", 64, 96), ("get", 128, 160), ("cut", 96, 128),
          ("get", 160, 192), ("cut", 128, 160), ("get", 192, CUT_AT), ("cut", 160, 192), ("cut", 192, CUT_AT), ("cut", CUT_AT, 256), ("cut", 256, 288), ("cut", 288, 320)]
_C = {"cy": np.array([0.88, 1.15, 0.92, 0.85]), "gath": np.array([1.56, 1.95, 1.1, 1.56]), "scat": np.array([3.8, 5.0, 2.0, 3.8]), "pe": np.array([0.45, 0.58, 0.47, 0.43]),
      "far": np.array([1.0, 1.3, 1.2, 0.7]), "rfar": np.array([1.0, 1.4, 1.6, 0.7]), "hop": 200.0, "own": 170.0, "dma": 1500.0, "rem": 2200.0,
      "loose": ("sc", "x0"), "les": 0, "wide": 1, "mode": 1, "adds": 1200.0, "soon": 1.0, "o1": 32, "o2": 40, "o3": (20, 34), "ks": 4, "js": 6, "spv": 0,
      "passes": 4, "shakes": 0, "swaps": 10000, "heat": 30.0, "seed": 2, "weigh": 0.4, "vlate": 1000.0}
_ORDER = []


def _queues(g, T):
    Q = {"v": g.vector, "s": g.scalar, "t": g.tensor, "g": g, "y": g.sync}
    ENG = {"v": "sv", "s": "ss", "t": "st", "g": "sg"}
    cnt, seen, acc, no, ops = {}, {q: {} for q in Q}, {}, [0, 0], []
    lines = {}
    cy = _C["cy"]

    def A(n, a=0, b=None, s=1, rows=None, part=None):
        m, off, w = _AT[n] if n in _AT else (n, 0, T[n].shape[1])
        b = w if b is None else b
        a, b, t = a + off, b + off, T[m]
        if part is not None:
            ap = t[part, a:b:s]
        elif rows is not None:
            ap = t[rows, a:b]
        elif s < 0:
            ap = t[:, ::-1] if a == 0 and b == t.shape[1] else t[:, b - 1:a - 1:-1]
        elif s > 1:
            ap = t[:, a:b:s]
        else:
            ap = t[:, a:b]
        return (ap, ((m, a, b, abs(s) if rows is None else -rows.start - 1),), (), -(-(b - a) // abs(s)), SCRATCH[m][2], 0)

    def X(ap):
        return (ap, (), (), 0, None, 0)

    def IND(win, off):
        return (win[0].indirect(off[0]), win[1], off[1], 16 * off[3], win[4], 1)

    def meets(w, q, reg, rec, chain):
        n, a, b, s = reg
        rw, rq, ra, rb, rs = rec[0:5]
        ps = n in _PS and rq != q
        if not (w or rw or ps):
            return False
        if not ps:
            if b <= ra or rb <= a or (s == rs and s > 1 and (a - ra) % s) or (s < 0 and rs < 0 and s != rs):
                return False
            if rq == q and chain and w:
                return False
        return True

    def keep(book, q, outs, ins, *what):
        for w, regs in ((True, outs), (False, ins)):
            for (n, a, b, s) in regs:
                old = book.get(n, [])
                if w and s == 1:
                    old = [x for x in old if not (a <= x[2] and x[3] <= b)]
                old.append((w, q, a, b, s) + what)
                book[n] = old

    def need(q, outs, ins, chain=False):
        deps = [rec[5:] for w, regs in ((True, outs), (False, ins)) for reg in regs for rec in acc.get(reg[0], ()) if meets(w, q, reg, rec, chain)]
        deps.sort(key=lambda d: -d[0])
        for k, sem, val, clk in deps:
            if seen[q].get(sem, 0) >= val:
                continue
            Q[q].wait_ge(T.sem[sem], val)
            for s2, v2 in clk.items():
                if seen[q].get(s2, 0) < v2:
                    seen[q][s2] = v2
            seen[q][sem] = max(val, seen[q].get(sem, 0))

    def note(q, sem, val, clk, outs, ins):
        no[0] += 1
        keep(acc, q, outs, ins, no[0], sem, val, clk)

    def split(outs, ins):
        o = [x for p in outs for x in p[1]]
        i = [x for p in outs for x in p[2]] + [x for p in ins if isinstance(p, tuple) for x in p[1] + p[2]]
        return o, i

    def add(q, as_q, o, i, emit, busy, lat, chain=False, after=()):
        ops.append((q, as_q, o, i, emit, busy, lat, chain, list(after)))
        return len(ops) - 1

    def LINE(name, joins=True, waits=True):
        if name in lines and waits and name not in _C["loose"]:
            ops[-1][8].append(lines[name])
        if joins:
            lines[name] = len(ops) - 1

    def run(q, outs, ins, call, busy, chain=False):
        o, i = split(outs, ins)

        def emit():
            need(q, o, i, chain)
            sem = ENG[q]
            cnt[sem] = cnt.get(sem, 0) + 1
            call().then_inc(T.sem[sem], 1)
            clk = dict(seen[q])
            clk[sem] = cnt[sem]
            note(q, sem, cnt[sem], clk, o, i)
        return add(q, q, o, i, emit, busy, 0.0, chain)

    def v(x):
        return x[0] if isinstance(x, tuple) else x

    def vlen(o, *ins, tt=False):
        if o[5]:
            return 50 + cy * _C["scat"] * o[3]
        if ins and ins[0][5]:
            return 50 + cy * _C["gath"] * o[3]
        r = 0.5 if all(x[4] in (B16, U16, F16) for x in (o,) + ins) else 1.0
        if tt and all(x[1][0][0] not in _PS for x in ins):
            r *= 2
        return cy * max(64, r * max(x[3] for x in (o,) + ins))

    V, SC, TE = g.vector, g.scalar, g.tensor

    def TT(o, a, b, op):
        run("v", [o], [a, b], lambda: V.tensor_tensor(out=o[0], in0=a[0], in1=b[0], op=op), vlen(o, a, b, tt=True))

    def TS(o, a, s1, s2, op0, op1=None):
        if op1 is None:
            run("v", [o], [a, s1], lambda: V.tensor_scalar(out=o[0], in0=a[0], scalar1=v(s1), scalar2=None, op0=op0), vlen(o, a))
        else:
            run("v", [o], [a, s1, s2], lambda: V.tensor_scalar(out=o[0], in0=a[0], scalar1=v(s1), scalar2=v(s2), op0=op0, op1=op1), vlen(o, a))

    def TC(o, a):
        run("v", [o], [a], lambda: V.tensor_copy(out=o[0], in_=a[0]), vlen(o, a))

    def MS(o, c):
        run("v", [o], [], lambda: V.memset(o[0], c), vlen(o))

    def RED(o, a, op):
        run("v", [o], [a], lambda: V.tensor_reduce(out=o[0], in_=a[0], axis=AxisListType.X, op=op), cy * max(64, a[3]))

    def SCAN(o, a, b, init, op0, op1):
        run("v", [o], [a, b, init], lambda: V.tensor_tensor_scan(out=o[0], data0=a[0], data1=b[0], initial=v(init), op0=op0, op1=op1), vlen(o, a, b))

    def ACT(o, a, f, bias=0.0, scale=1.0, acc=None):
        n = 65 + cy * _C["gath"] * o[3] if a[5] else 30 + cy * max(64, o[3])
        if acc is None:
            run("s", [o], [a, bias, scale], lambda: SC.activation(out=o[0], in_=a[0], func=f, bias=v(bias), scale=v(scale)), n)
        else:
            run("s", [o, acc], [a, bias, scale], lambda: SC.activation(out=o[0], in_=a[0], func=f, bias=v(bias), scale=v(scale), accum_out=acc[0]), n + 20)

    def MM(o, l, r, start, stop):
        run("t", [o], [l, r], lambda: TE.matmul(o[0], l[0], r[0], start=start, stop=stop), 5 + _C["pe"] * max(64, r[3]) * (4 if r[4] == F32 else 1), not start)

    def MMS(o, *pairs, start=True, stop=True):
        for k, (l, r, *part) in enumerate(pairs):
            MM(part[0] if part else o, l, r, start and k == 0, stop and k == len(pairs) - 1)
        part = ops[-len(pairs):]
        del ops[-len(pairs):]

        def emit():
            for op in part:
                op[4]()
        add("t", "t", list(o[1]), [x for op in part for x in op[3]], emit, sum(op[5] for op in part), 0.0, not start)

    def IOTA(o, pat, base, cm):
        run("g", [o], [], lambda: g.iota(o[0], pat, base, cm, allow_small_or_imprecise_dtypes=True), 130 + 2 * cy * o[3])
        LINE("g")

    def AFF(o, a, pat, op, base, cm):
        run("g", [o], [a], lambda: g.affine_select(o[0], a[0], pat, op, 0.0, base, cm), 170 + 2 * cy * o[3])
        LINE("g")

    def DMA(q, o, a, lat=0.0, after=(), adds=False, behind=()):
        os_, is_ = split([o], [a, *behind])

        def emit():
            need(q, os_, is_)
            sem = "d%d" % no[1]
            no[1] += 1
            (g.dma_start(o[0], a[0], accum_op=O.add) if adds else Q[q].dma_start(o[0], a[0])).then_inc(T.sem[sem], 16)
            cnt[sem] = 16
            clk = dict(seen[q])
            clk[sem] = 16
            note("dma", sem, 16, clk, os_, is_)
        return add(q, "dma", os_, is_, emit, 900.0 if adds else 60.0, _C["dma"] + lat, False, after)

    def SEND(srcs, engines, call, loc="loc", frees=()):
        o, i = split(frees, srcs)

        def emit():
            need("g", o, i)
            call()
            cnt[loc] = cnt.get(loc, 0) + engines
            note("rem", loc, cnt[loc], {}, [], i)
        return add("g", "rem", o, i, emit, 400.0, 0.0)

    def LAND(dst, sem, val, sent, lat=0.0):
        def emit():
            cnt[sem] = val
            note("rem", sem, val, {sem: val}, list(dst[1]), [])
        add(None, "rem", list(dst[1]), [], emit, 0.0, lat or _C["rem"], False, (sent,))

    def order():
        n, book, bank = len(ops), {}, {}
        pre, suc = [{} for _ in range(n)], [[] for _ in range(n)]
        for k, (q, aq, o, i, emit, busy, lat, chain, after) in enumerate(ops):
            for w, regs in ((True, o), (False, i)):
                for reg in regs:
                    for rec in book.get(reg[0], ()):
                        if meets(w, aq if aq != "dma" else q, reg, rec, chain):
                            j = rec[5]
                            pre[k][j] = ops[j][6] + (_C["own"] if ops[j][0] == q else _C["hop"])
            if q == "t":
                b = o[0][0]
                if b in bank:
                    pre[k].setdefault(bank[b], 0.0)
                bank[b] = k
            for j in after:
                pre[k].setdefault(j, 0.0)
            pre[k].pop(k, None)
            keep(book, aq, o, i, k)
            for j in pre[k]:
                suc[j].append(k)
        busy = [[float((op[5] + 0 * cy)[x]) for op in ops] for x in range(len(cy))]
        lat, on, b0 = [op[6] for op in ops], [op[0] for op in ops], busy[0]
        fore = [[(j, d) for j, d in p.items() if not any(j in pre[x] and pre[x][j] + p[x] >= d for x in p)] for p in pre]
        fores = [[[(j, d + (lat[j] * (float(_C["far" if on[j] else "rfar"][x]) - 1) if d else 0.0)) for j, d in p] for p in fore] for x in range(len(cy))]
        back = [[] for _ in range(n)]
        for k in range(n):
            for j, d in fore[k]:
                back[j].append((k, d))

        def place(seq, before, first):
            start, end, slots = [0.0] * n, [0.0] * n, {q: [(-1.0, 0.0)] for q in Q}
            for k in seq:
                t = first[k]
                for j, d in before[k]:
                    if end[j] + d > t:
                        t = end[j] + d
                if on[k] is not None:
                    sl = slots[on[k]]
                    at = len(sl)
                    if sl[-1][1] > t:
                        at, hi = 1, len(sl)
                        while at < hi:
                            mid = (at + hi) // 2
                            if sl[mid][0] < t:
                                at = mid + 1
                            else:
                                hi = mid
                        while at < len(sl) and max(t, sl[at - 1][1]) + b0[k] > sl[at][0]:
                            at += 1
                        t = max(t, sl[at - 1][1])
                    sl.insert(at, (t, t + b0[k]))
                start[k], end[k] = t, t + b0[k]
            return start

        def eager(key, ahead):
            start, ready, wait = [0.0] * n, [0.0] * n, [len(p) for p in fore]
            free, open_ = {q: 0.0 for q in list(Q) + [None]}, {q: [] for q in list(Q) + [None]}
            for k in range(n):
                if not wait[k]:
                    open_[on[k]].append(k)
            for _ in range(n):
                t, q = min((max(free[q], min(ready[k] for k in ks)), str(q)) for q, ks in open_.items() if ks)
                q = None if q == "None" else q
                k = min((k for k in open_[q] if ready[k] <= t + ahead), key=lambda k: key[k])
                open_[q].remove(k)
                start[k] = max(t, ready[k])
                end = start[k] + b0[k]
                if q:
                    free[q] = end
                for j, d in back[k]:
                    ready[j] = max(ready[j], end + d)
                    wait[j] -= 1
                    if not wait[j]:
                        open_[on[j]].append(j)
            return start

        def span(start):
            seq = sorted(range(n), key=lambda k: (start[k], k))
            total = max(start[k] + b0[k] + lat[k] for k in seq)
            for b in busy[1:]:
                end, free = [0.0] * n, {q: 0.0 for q in Q}
                free[None] = 0.0
                for k in seq:
                    t = free[on[k]] if on[k] else 0.0
                    for j, d in fore[k]:
                        if end[j] + d > t:
                            t = end[j] + d
                    end[k] = free[on[k]] = t + b[k]
                total += _C["weigh"] * max(end[k] + lat[k] for k in seq)
            return total, seq, start
        tail, zero = [0.0] * n, [0.0] * n
        for k in range(n - 1, -1, -1):
            tail[k] = b0[k] + max([lat[k]] + [d + tail[j] for j, d in back[k]])
        seq, best = sorted(range(n), key=lambda k: (-tail[k], k)), None
        for it in range(_C["passes"]):
            now = span(place(seq, fore, zero))
            best = now if best is None or now[0] < best[0] else best
            late = place(sorted(range(n), key=lambda k: (-now[2][k] - b0[k], -k)), back, lat)
            seq = sorted(range(n), key=lambda k: (-late[k] - b0[k], k))
            for ahead in (0.0, 100.0, 250.0):
                now = span(eager([-late[k] - b0[k] for k in range(n)], ahead))
                best = now if now[0] < best[0] else best
        rng = np.random.default_rng(_C["seed"])
        for it in range(_C["shakes"]):
            t0, width, key = rng.random() * max(best[2]), rng.choice([300.0, 1000.0, 3000.0]), list(best[2])
            noise = rng.random(n) * width
            for k in range(n):
                if t0 - 3000 < key[k] < t0 + 3000:
                    key[k] += noise[k]
                for j, d in fore[k]:
                    if key[j] >= key[k]:
                        key[k] = key[j] + 1e-3
            now = span(place(sorted(range(n), key=lambda k: key[k]), fore, zero))
            best = now if now[0] <= best[0] else best

        def walk(seq, b, fore, at, old):
            end, why, last = list(old[0]), list(old[1]), {q: -1 for q in Q}
            for k in seq[:at]:
                last[on[k]] = k
            for k in seq[at:]:
                q, t, w = on[k], 0.0, -1
                if q:
                    w = last[q]
                    t = end[w] if w >= 0 else 0.0
                    last[q] = k
                    w = -2 - w
                for j, d in fore[k]:
                    if end[j] + d > t:
                        t, w = end[j] + d, j
                end[k], why[k] = t + b[k], w
            k = max(ends, key=lambda k: end[k] + lat[k])
            total, stood = end[k] + lat[k] + _C["soon"] * sum(end) / n, []
            while k != -1:
                w = why[k]
                if w < -1:
                    w = -2 - w
                    if w not in pre[k] and (suc[w] != suc[k] or b0[w] != b0[k]):
                        stood.append((w, k))
                k = w
            return total, stood, (end, why)

        def judge(seq, at, old):
            res = [walk(seq, b, f, at, o) for b, f, o in zip(busy, fores, old)]
            return res[0][0] + _C["weigh"] * sum(x[0] for x in res[1:]), seq, [p for x in res for p in x[1]], [x[2] for x in res]
        ends = [k for k in range(n) if not suc[k]]
        best = now = judge(best[1], 0, [([0.0] * n, [-1] * n)] * len(busy))
        for it in range(_C["swaps"]):
            a, b = now[2][int(rng.integers(len(now[2])))]
            seq = now[1]
            i, j = seq.index(a), seq.index(b)
            if rng.random() < 0.5:
                for _ in range(int(rng.integers(3))):
                    i = max([x for x in range(max(0, i - 40), i) if on[seq[x]] == on[a]] + [-1])
                    if i < 0:
                        break
                if i < 0:
                    continue
                go, part = {b}, seq[i:j + 1]
                for k in part[::-1]:
                    if k in go:
                        go.update(pre[k])
                if a in go:
                    continue
                part = [k for k in part if k in go] + [k for k in part if k not in go]
            else:
                for _ in range(int(rng.integers(8)) - 2):
                    j = min([x for x in range(j + 1, min(n, j + 40)) if on[seq[x]] == on[a]] + [j + 40, n - 1])
                go, part = {a}, seq[i:j + 1]
                for k in part:
                    if k in go:
                        go.update(suc[k])
                if b in go:
                    continue
                part = [k for k in part if k not in go] + [k for k in part if k in go]
            new = judge(seq[:i] + part + seq[j + 1:], i, now[3])
            if new[0] <= now[0] - _C["heat"] * (1 - it / _C["swaps"]) * np.log(1 - rng.random()):
                now = new
                best = now if now[0] < best[0] else best
        _C["span"] = best[0]
        return best[1]

    def END():
        if not _ORDER:
            _ORDER.extend(order())
        for k in _ORDER:
            ops[k][4]()
        for sem in cnt:
            if max(seen[q].get(sem, 0) for q in Q) < cnt[sem]:
                g.wait_ge(T.sem[sem], cnt[sem])

    return A, X, IND, TT, TS, TC, MS, RED, SCAN, ACT, MM, MMS, IOTA, AFF, DMA, SEND, LAND, LINE, END


def rank_program(g, core, T, topo):
    rank = T.rank_of(core)
    if rank is None:
        return
    A, XT, IND, TT, TS, TC, MS, RED, SCAN, ACT, MM, MMS, IOTA, AFF, DMA, SEND, LAND, LINE, END = _queues(g, T)
    CP, RL, IDN = AF.Copy, AF.Relu, AF.Identity
    q6 = (15, 96, 16)

    d0 = DMA("y", A("GI"), XT(T.gd[:, :]), 800)
    d1 = DMA("s", A("wti"), XT(T.wt[:, :]))
    d1 = DMA("s", A("kmi"), XT(T.km[:, :]), 200, [d1])
    d0 = DMA("y", A("X00"), XT(T.xs[0::16, :]), 1400, [d0])
    d1 = DMA("s", A("X", W // 2, W), XT(T.xs[:, W // 2:W]), 5500, [d1])
    DMA("s", A("thi"), XT(T.th[:, :]), 7500, [d1])
    d0 = DMA("y", A("X", 0, W // 2), XT(T.xs[:, 0:W // 2]), 5500, [d0])

    MS(A("one"), 1.0)
    MS(A("oneb"), 1.0)
    IOTA(A("pi"), [[0, 1]], 0, 1)
    AFF(A("GBt"), A("one"), [[-16, 8], [0, 16]], O.is_ge, 0, 1)
    AFF(A("GB"), A("GBt"), [[16, 8], [0, 16]], O.is_ge, 15, -1)
    AFF(A("ID"), A("GB"), [[-1, 128]], O.is_equal, 0, 1)
    for n, c in enumerate((0.5, 383.0 * BIG, 255.0, 2.0 ** 23 + 255)):
        MS(A("CB", n, n + 1), c)
    MS(A("CB", 6, 7), float(CAP))
    MS(A("CB", 8, 9), float(CAP * (1 + (_C["mode"] == 1))))
    TS(A("pi2"), A("pi"), 15, None, O.bitwise_and)
    TC(A("PI"), A("pi2"))
    TC(A("wtf"), A("wti"))
    TC(A("kmf"), A("kmi"))
    MS(A("TSL"), 0.0)
    TC(A("TSL", 15, 128, 16), A("GB", 0, 128, 16))
    for r in range(RO):
        TS(A("WS%d" % r), A("TSL"), A("wtf", r, r + 1), -1.0 if r else 1.0, O.mult, O.mult)
    ACT(A("T32"), A("TSL"), CP, scale=32.0)
    ACT(A("Tn16"), A("TSL"), CP, scale=-16.0)
    MMS(A("pN", 0, 3), (A("GB"), A("wtf")))
    TS(A("CW3"), A("pN", 0, 3), 255.0, None, O.mult)
    TS(A("G0", 0, S), A("GI"), -1.0, 255.0, O.mult, O.add)
    IOTA(A("i16"), [[1, 16]], 0, 0)
    IOTA(A("PL0"), [[1, 512]], 2, 0)
    IOTA(A("QM"), [[0, 6], [1, 16]], 0, 0)
    IOTA(A("QB0"), [[16, 6]], 0, 0)
    IOTA(A("BI"), [[1, 64]], 0, 0)
    AFF(A("B0"), A("GB"), [[-16, 8], [0, 16]], O.is_equal, 0, 1)
    AFF(A("USf"), A("GB"), [[-1, 128]], O.is_gt, 0, 1)
    AFF(A("LSf"), A("GB"), [[1, 128]], O.is_gt, 0, -1)
    AFF(A("B15f"), A("GB"), [[-16, 8], [0, 16]], O.is_equal, -15, 1)
    IOTA(A("it0"), [[0, 8], [1, 16]], 0, 0)
    for n, c, base in (("Q0", 96, 0), ("Q1", 96, 1), ("Q0b", 96, 0)):
        IOTA(A(n), [[1, c]], base, 0)
    IOTA(A("ROW"), [[16, 65]], -8, 0)
    IOTA(A("SLh"), [[16, 64]], 0, 0)
    for m in range(M):
        ACT(A("M2C", 64 * m, 64 * m + 64), A("oneb", 0, 64), CP, scale=2.0 * m)
    for n, c in (("KD", 0), ("PW", -1.0), ("LWn", 0.0), ("C8K", STEP), ("C23", 2.0 ** 23), ("N4", -4.0), ("TWO", 2.0), ("CW", 0.0), ("RSB", -4 * FAR), ("DMP", -1.0), ("ZR", 0.0)):
        MS(A(n), c)
    for n, a, b in (("GQ", 96, 112), ("SPQ", 96, 112), ("STQ", 192, 208), ("G0", S, S + CAP), ("G1", S, S + CAP)):
        MS(A(n, a, b), 0.0)
    for a in range(0, 4096, 512):
        d0 = DMA("y", A("FW", a, a + 512), A("ZR"), 1.3 * a, [d0], behind=[A("X")])
    for a in range(4096, FWW, 526):
        IOTA(A("FW", a, a + 526), [[0, 526]], 0, 0)
    for n, a, c in (("IDb", "ID", 1.0), ("nIDb", "ID", -1.0), ("GBb", "GB", 1.0), ("nUS", "USf", -1.0), ("nGB8", "GB", -8.0), ("nGB", "GB", -1.0),
                    ("B15", "B15f", 1.0), ("GBK", "GB", BIG), ("IDK", "ID", BIG), ("IDh", "ID", 0.5)):
        ACT(A(n), A(a), CP, scale=c)
    TS(A("GBt"), A("ID"), 4096.0, None, O.mult)
    TT(A("LSK"), A("GBt"), A("LSf"), O.add)
    TS(A("th16"), A("thi"), 16.0, None, O.mult)
    TS(A("P512"), A("PI"), 512.0, None, O.mult)
    TS(A("P513"), A("PI"), 512.0, 1.0, O.mult, O.add)
    TS(A("PIN"), A("PI"), 512.0 * STEP, 0.25 * STEP, O.mult, O.add)
    TS(A("CB", 7, 8), A("PI"), -2048.0, None, O.mult)
    TS(A("P5K"), A("P513"), 10000.0, None, O.mult)
    TC(A("M20", 96, 97), A("P513"))
    TS(A("CB", 4, 5), A("PI"), 2.0, None, O.is_equal)
    TS(A("LS1"), A("CB", 4, 5), STEP + 4.0, -STEP, O.mult, O.add)
    TS(A("LB1"), A("CB", 4, 5), -4.0 - 1.25 * STEP, 1.25 * STEP, O.mult, O.add)
    TS(A("B0e"), A("B0"), 2.0 ** -9, None, O.mult)
    TT(A("IDE"), A("B0e"), A("ID"), O.max)
    TC(A("PL"), A("PL0"))
    TS(A("MK"), A("QM"), A("PI"), FAR, O.not_equal, O.mult)
    MS(A("RSB", 0, 96, 16), 2 * FAR)
    if _C["js"] < 6:
        MS(A("RS6"), 1.0)
        MS(A("RS6", 0, 576, 96), 0.0)
    TS(A("DMP", 0, 96, 16), A("QB0"), A("PI"), W + 1.0, O.add, O.add)
    TS(A("QB"), A("QB0"), A("PI"), 0.5, O.add, O.add)
    TS(A("BI"), A("BI"), 1.0 / 32, None, O.mult)
    TS(A("GBi"), A("GB"), A("PI"), None, O.mult)
    TS(A("GB32"), A("GB"), 32.0, None, O.mult)
    if _C["ks"] < 6:
        MS(A("RS4"), 1.0)
        MS(A("RS4", 0, 384, 64), 0.0)
    TS(A("I16"), A("i16"), A("PI"), None, O.is_equal)
    TS(A("LM"), A("i16"), A("PI"), W + 1.0, O.is_le, O.mult)
    TS(A("SLi"), A("oneb", 0, 64), A("PI"), None, O.mult)
    TS(A("SLf"), A("SLh"), A("PI"), None, O.add)
    TS(A("GBt"), A("GB"), 8192.0, -8192.0 - 7.5, O.mult, O.add)
    TT(A("ITH"), A("GBt"), A("it0"), O.add)
    ACT(A("XF"), A("X00"), CP)
    DMA("y", A("FW", 1, W + 1, rows=slice(1, 128, 16)), A("XF"), 500)

    def sel(n, i):
        return A(n, 15 - i, 143 - i)

    def lists(r):
        G = "G%d" % (r % 2) if r else "GI"
        MMS(A("pA", 0, 64), *[(sel("WS%d" % r, i), A(G, i, S, 16)) for i in range(16)])
        TS(A("Ui"), A("pA", 0, 64), A("CW3", r, r + 1) if r else 0.0, None, O.add)
        TS(A("Um"), A("Ui"), 4095, None, O.bitwise_and)
        TC(A("Uf"), A("Um"))
        TT(A("UU"), A("Um"), A("Um"), O.mult)
        TS(A("FQ"), A("UU"), 5, None, O.arith_shift_right)
        banks = {0: ("pB", 0), 1: ("pM", 0), 2: ("pM", 1), 3: ("pM", 2), 4: ("pN", 0), 5: ("pN", 1), 6: ("pK0", 0), 7: ("pK0", 1)}
        for m in range(M):
            ACT(A(banks[m][0], 64 * banks[m][1], 64 * banks[m][1] + 64), A("Uf"), CP, scale=A("kmf", m, m + 1))
            LINE("s")

        def sums(m):
            TT(A("CA", 64 * m, 64 * m + 64), A(banks[m][0], 64 * banks[m][1], 64 * banks[m][1] + 64), A("FQ"), O.add)

        def rest(a, b):
            TS(A("C", 64 * a, 64 * b), A("CA", 64 * a, 64 * b), W - 1, None, O.bitwise_and)

        def offs(a, b):
            TC(A("OFF", 64 * a, 64 * b), A("C", 64 * a, 64 * b))

        def flag(a, b):
            TS(A("FL", 64 * a, 64 * b), A("OFF", 64 * a, 64 * b), W - 96.0, None, O.is_ge)
        for f, *args in ((sums, 0), (rest, 0, 1), (offs, 0, 1), (sums, 1), (sums, 2), (sums, 3), (sums, 4), (sums, 5), (sums, 6), (sums, 7), (rest, 1, 4),
                         (rest, 4, 8), (offs, 1, 4), (offs, 4, 8), (flag, 0, 4), (flag, 4, 8)):
            f(*args)
            LINE("v")

    def scores(r):
        G = "G%d" % (r % 2)
        seen, pairs = [0, 0], [u for u in UNITS if u[1] - u[0] == 128]

        def rows(u, src, by, stop):
            a, b, bank, at = u
            if b - a == 128:
                MMS(A(bank, at, at + 128), *[(A(src, 16 * a + i, 16 * b, 16), A(by, 15, 128, 16), A(bank, at + i, at + 128, 16)) for i in range(16)], start=False, stop=stop)
            else:
                MMS(A(bank, at, at + b - a), *[(sel(by, i), A(src, 16 * a + i, 16 * b, 16)) for i in range(16)], start=False, stop=stop)

        def opens(u, D):
            a, b, bank, at = u
            if b - a == 128:
                MMS(A(bank, at, at + 128), (A("M2C", a, b), A("IDb")), (A("FL", a, b), A("IDb")), stop=False)
            else:
                MMS(A(bank, at, at + b - a), (A("IDb"), A("M2C", a, b)), (A("IDb"), A("FL", a, b)), stop=False)
            if D:
                rows(u, "DD", "Tn16", False)

        def least(key):
            seen[1] += 1
            if seen[1] == 1:
                TS(A("KM"), key, FAR, None, O.min)
            else:
                TT(A("KMi" if seen[1] == len(UNITS) + 2 - len(pairs) else "KM"), key, A("KM"), O.min)
            LINE("v")

        def lower(a, b):
            bank, at = ([u[2:] for u in UNITS if u[0] == a] + [pairs[-1][2:]])[0]
            if a < 0:
                least(A(bank, at + 128, at + 192))
                least(A(bank, at + 192, at + 256))
            elif b - a == 64:
                least(A(bank, at, at + 64))
            else:
                seen[0] += 1
                if seen[0] == 1:
                    TS(A("KT"), A(bank, at, at + 128), FAR, None, O.min)
                else:
                    TT(A("KT"), A(bank, at, at + 128), A("KT"), O.min)
                LINE("v")
                if seen[0] == len(pairs):
                    MMS(A(pairs[-1][2], pairs[-1][3] + 128, pairs[-1][3] + 256), (A("KT"), A("ID")))

        got, done, where, by_v = set(), set(), {}, {c for k, a, b in LINE_V if k == "cut" for c in range(a, b)}
        lines = {q: [(k,) + tuple(CUTS[r] if x == CUT_AT else x for x in ab) for k, *ab in line] for q, line in (("v", LINE_V), ("s", LINE_S))}
        lines = {q: [x for x in line if x[1] < x[2] or x[0] in ("min", "tab")] for q, line in lines.items()}
        t, at = {"v": _C["vlate"], "s": 0.0}, {"v": 0, "s": 0}
        while any(at[q] < len(lines[q]) for q in at):
            can = [q for q, line in lines.items() if at[q] < len(line) and {"get": set(range(512)), "raw": set(range(512)), "cut": got, "min": done, "tab": got}[line[at[q]][0]].issuperset(range(*line[at[q]][1:]))]
            q = min(can, key=lambda q: t[q])
            k, a, b = lines[q][at[q]]
            at[q] += 1
            if k == "min":
                lower(a, b)
                continue
            if k == "tab":
                if r:
                    utable(r, a)
                continue
            t[q] += (b - a) * (24 if k != "cut" else 8 if q == "v" else 16)
            d, mine = A("DD", 16 * a, 16 * b), k != "cut" and A(G, 16 * (a % 64), 16 * (a % 64 + b - a))
            if k == "raw":
                ACT(d, IND(A("X"), A("OFF", a, b)), CP, scale=-1.0)
                LINE(q)
                DMA("g", d, mine, _C["adds"], adds=True)
                got.update(range(a, b))
                for u in UNITS:
                    if u[0] < b and a < u[1] and got.issuperset(range(u[0], u[1])):
                        opens(u, True)
                continue
            if k == "get" and q == "v":
                TT(d, IND(A("X"), A("OFF", a, b)), mine, O.subtract)
            elif k == "get":
                ACT(d, IND(A("X"), A("OFF", a, b)), CP)
            elif q == "v":
                TS(A("RR", 16 * a, 16 * b), d, 0.0, None, O.max)
            else:
                ACT(A("RR", 16 * a, 16 * b), where.get(a, d), AF.Abs, scale=0.5)
            LINE(q)
            if k == "get" and q == "s":
                where[a] = A("pD%d" % (len(where) % 2), 0, 16 * (b - a))
                MMS(where[a], (A("nIDb"), mine), stop=False)
                MMS(where[a], (A("IDb"), d), start=False)
            for u in UNITS:
                if u[0] < b and a < u[1]:
                    if k == "get" and u[0] in by_v and (got | set(range(a, b))).issuperset(range(u[0], u[1])):
                        opens(u, True)
                    if k == "cut" and (done | set(range(a, b))).issuperset(range(u[0], u[1])):
                        if u[0] not in by_v:
                            opens(u, False)
                        rows(u, "RR", "T32", True)
            (got if k == "get" else done).update(range(a, b))

    def own(dst, bank):
        SCAN(A(dst), A("RSB"), A(bank, 0, 96), 0.0, O.max, O.min)

    def utable(r, k):
        if k == 0:
            ACT(A("NO"), A("X0%d" % r), RL, bias=A("CB", 1, 2), scale=-2 * BIG)
            SCAN(A("UL", s=-1), A("NO", s=-1), A("PL", s=-1), BIG, O.min, O.max)
            return
        if k == 1:
            TS(A("UF"), A("UL", 0, 1), A("P512"), W + 1.0, O.add, O.min)
        elif k == 2:
            TS(A("OF"), A("I16"), A("UF"), None, O.mult)
        elif k == 3:
            TT(A("FM"), A("pA", 256, 272), A("LM"), O.max)
        elif k == 4:
            RED(A("UI"), A("FM"), O.min)
        else:
            TS(A("U2"), A("UL"), A("P512"), A("UI"), O.add, O.min)
        if r:
            LINE("v")
        if k == 2:
            MMS(A("pA", 256, 272), (A("GB"), A("OF")))
        if k == 5:
            DMA("y", A("FW", 2, W + 2, rows=slice(0, 128, 16)), A("U2"), 500)

    near, far = T.cores[rank ^ 1], T.cores[rank ^ 2]

    def to(dst, eng, sem, src, out):
        rid, pid = topo.addr(dst)[0:2]
        return RemoteDMATransfer(dst_ids=[DstId(rid=rid, pnc=pid)], dma_engine_mask=sum(1 << e for e in eng), remote_sem=T.sem[sem], src=src[0], dst=out[0])
    en, ef = topo.engines(core, near), topo.engines(core, far)
    hn = len(en) // 2
    mk = (A("IDb"), A("MK"))

    def one_round(r):
        last = r == RO - 1
        G, H = "G%d" % (r % 2), "YG" if last else "G%d" % ((r + 1) % 2)
        RK, SP, STn, RI, RJ, Z, M2, M3 = ("%s%d" % (n, k) for n, k in (("RK", r), ("SP", r), ("ST", r), ("RI", r), ("RJ", r), ("Z", r), ("M2", r), ("M2", r + 1)))
        lists(r)
        for k in range(1 if r else 6):
            utable(r, k)
        scores(r)
        TS(A("PAR"), A("KMi"), 1, None, O.bitwise_and)
        TS(A("F0"), A("KMi"), A("th16"), None, O.is_lt)
        TT(A("FIT"), A("F0"), A("PAR"), O.is_gt)
        SCAN(A("CS"), A("oneb", 0, 64), A("FIT"), 0.0, O.mult, O.add)
        MMS(A("pB", 0, 64), (A("GBb"), A("CS")))
        MMS(A("pM", 64, 128), (A("GBb"), A("CS")))
        MMS(A("pD1", 0, 64), (A("nUS"), A("FIT")), (A("GBb"), A("CS")))
        ks = _C["ks"]
        for a in range(ks):
            ACT(A("JK", 64 * a, 64 * a + 64), A("pB", 0, 64), AF.Sign, bias=A("QB", a, a + 1), scale=-1.0, acc=A("BQ", a, a + 1))
        for a in range(ks, 6):
            TS(A("JK", 64 * a, 64 * a + 64), A("pM", 64, 128), A("QB", a, a + 1), None, O.is_le)
        TS(A("BQo", 0, ks), A("BQ", 0, ks), 0.5, 32.0, O.mult, O.add)
        TS(A("T1", 0, ks), A("BQ", 0, ks), 8.0, 512.0 + 4088.5, O.mult, O.add)
        if ks < 6:
            SCAN(A("JW", 64 * ks, 384), A("RS4", 64 * ks, 384), A("JK", 64 * ks, 384), 0.0, O.mult, O.add)
            TC(A("BQo", ks, 6), A("JW", 64 * ks + 63, 384, 64))
            TS(A("T1", ks, 6), A("JW", 64 * ks + 63, 384, 64), 16.0, 4088.5, O.mult, O.add)
        TS(A("MX"), A("KMi"), 14, None, O.bitwise_and)
        TS(A("KD", 0, 64), A("KMi"), 65520, None, O.bitwise_and)
        TT(A("LWn", 0, 64), A("MX"), A("BI"), O.add)
        TT(A("PW", 0, 64), A("pD1", 0, 64), A("FIT"), O.mult)
        TS(A("INV"), A("Q0"), A("pM", 127, 128), 2.0 ** -14, O.is_ge, O.add)
        inv = (A("IDK"), A("INV"))

        def two(o, early, late):
            MMS(o, *early, stop=False)
            MMS(o, *late, start=False)
        TT(A("OH"), IND(A("PW"), A("BQo")), A("Q1"), O.is_equal)
        TT(A("LG"), IND(A("LWn"), A("BQo")), A("OH"), O.mult)
        two(A("pA", 0, 96), [mk], [(A("GB32"), A("LG"))])
        TT(A("KG"), IND(A("KD"), A("BQo")), A("OH"), O.mult)
        own("SL", "pA")
        TC(A("LO"), A("SL", *q6))
        two(A("pN", 0, 96), [mk], [(A("GBi"), A("OH"))])
        own("SI", "pN")
        two(A("pK0", 0, 96), [mk, (A("nIDb"), A("Q0b"))], [(A("nGB8"), A("KG"))])
        two(A("pK1", 0, 96), [(A("nIDb"), A("Q0b"))], [(A("nGB8"), A("KG"))])
        TT(A("CG"), IND(A("C"), A("LO")), A("OH"), O.mult)
        two(A("pA", 0, 96), [mk, inv], [(A("GB"), A("CG"))])
        two(A("pB", 0, 96), [inv], [(A("GB"), A("CG"))])
        own("SK", "pK0")
        for a in range(6):
            ACT(A("SGN", 96 * a, 96 * a + 96), A("pK1", 0, 96), AF.Sign, bias=A("SK", 16 * a + 15, 16 * a + 16), scale=-1.0)
        own("SC", "pA")
        for a in range(6):
            ACT(A("KB", 96 * a, 96 * a + 96), A("SGN", 96 * a, 96 * a + 96), CP, scale=A("SC", 16 * a + 15, 16 * a + 16))
        TS(A("PO"), A("SC", *q6), 9.0, W - 7.0, O.add, O.min)
        TC(A("EG"), IND(A("FW", 8, FWW), A("PO")))
        two(A("pM", 0, 96), [mk], [(A("B0"), A("EG"))])
        own("S1", "pM")
        TS(A("UO2"), A("S1", *q6), 8.0, W + 1.0, O.add, O.min)
        TC(A("EG2"), IND(A("FW"), A("UO2")))
        two(A("pN", 0, 96), [mk], [(A("B0"), A("EG2"))])
        own("S2", "pN")
        TS(A("TO", 0, 6), A("S1", *q6), -2.0, None, O.add)
        TS(A("TO", 6, 12), A("S2", *q6), -2.0, None, O.add)
        ACT(A("PG"), IND(A("X"), A("PO")), AF.Abs)
        two(A("pD0", 0, 96), [(A("IDb"), A("C23", 0, 96))], [(A("IDE"), A("PG"))])
        ACT(A("SPQ", 0, 96), A("pD0", 0, 96), RL, bias=A("CB", 3, 4), scale=-1.0)
        two(A("pD0", 96, 192), [(A("nGB"), A("CG"))], [(A("B0"), A("EG2"))])
        ACT(A("LEN"), A("pD0", 96, 192), IDN, bias=A("LB1"), scale=A("LS1"))
        MMS(A("pM", 96, 192), (A("B0"), A("EG2")))
        if r:
            MMS(A("pD1", 0, 2), (A("B15"), A("X0%d" % r, 510, 512)))
            ACT(A("LST"), A("pD1", 1, 2), RL, scale=-1.0)
            TS(A("X", W - 1, W), A("X", W - 1, W), A("LST"), None, O.max)
        for h in range(2):
            ACT(A("STQ", 96 * h, 96 * h + 96), IND(A("X"), A("TO", 6 * h, 6 * h + 6)), RL, bias=A("CB", 2, 3), scale=-1.0)
        TT(A("T2"), A("SI", *q6), A("T1"), O.add)
        TS(A("SQ"), A("T2"), -4088.5, S - 1.0, O.add, O.min)
        ACT(A("GQ", 0, 96), IND(A(G, 0, S), A("SQ")), CP)
        MM(A("pK0", 0, 96), *mk, True, False)
        MM(A("pK0", 0, 96), *inv, False, False)
        MM(A("pK0", 0, 96), A("GB"), A("CG"), False, False)
        MM(A("pK1", 0, 96), *inv, True, False)
        for a in range(6):
            TT(A("KL", 96 * a, 96 * a + 96), A("KB", 96 * a, 96 * a + 96), A("pB", 0, 96), O.is_equal)
            MM(A("pK1", 0, 96), A("GBK"), A("KL", 96 * a, 96 * a + 96), False, a == 5)
            MM(A("pK0", 0, 96), A("GBK"), A("KL", 96 * a, 96 * a + 96), False, a == 5)
        TS(A("CUT"), A("pK1", 0, 96), 1.5, None, O.is_lt)
        SCAN(A(RK), A("oneb", 0, 96), A("CUT"), 0.0, O.mult, O.add)
        cnts = A(RK, 80, 96)
        k = SEND([cnts], 2 * hn, lambda: g.remote_dma_fused([to(near, en[:hn], "ai%d" % r, cnts, A(RI)), to(far, ef[hn:], "aj%d" % r, cnts, A(RJ))], local_sem=T.sem["loc"]))
        LAND(A(RI), "ai%d" % r, hn, k)
        LAND(A(RJ), "aj%d" % r, len(ef) - hn, k)
        js = _C["js"]
        for a in range(js):
            ACT(A("JL", 96 * a, 96 * a + 96), A(RK), AF.Sign, bias=A("QB", a, a + 1), scale=-1.0, acc=A("BK", a, a + 1))
        for a in range(js, 6):
            TS(A("JL", 96 * a, 96 * a + 96), A(RK), A("QB", a, a + 1), None, O.is_le)
        if js:
            TS(A("KIu", 0, js), A("BK", 0, js), 0.5, 48.0, O.mult, O.add)
        if js < 6:
            SCAN(A("JV", 96 * js, 576), A("RS6", 96 * js, 576), A("JL", 96 * js, 576), 0.0, O.mult, O.add)
            TC(A("KIu", js, 6), A("JV", 96 * js + 95, 576, 96))
        for h, win in enumerate((A("SPQ"), A("STQ", 0, 112), A("STQ", 96, 208))):
            if h < _C["spv"]:
                TC(A(STn, 96 * h, 96 * h + 96), IND(win, A("KIu", 0, 6)))
            else:
                ACT(A(STn, 96 * h, 96 * h + 96), IND(win, A("KIu", 0, 6)), CP)
        for call in ([[(near, en, "ap", 0, 96, 0)], [(far, ef, "at", 96, ARR, 96)]], [[(near, en[:hn], "ap", 0, 192, 0), (far, ef[hn:], "at", 96, ARR, 192)]],
                     [[(near, en[:hn], "ap", 0, 96, 0), (far, ef[hn:], "at", 96, 192, 96)], [(far, ef, "au", 192, ARR, 192)]])[_C["mode"]]:
            k = SEND([A(STn, x[3], x[4]) for x in call], sum(len(x[1]) for x in call), lambda call=call: g.remote_dma_fused(
                [to(dst, eng, sem + str(r), A(STn, a, b), A(Z, at, at + b - a)) for dst, eng, sem, a, b, at in call], local_sem=T.sem["loc"]))
            for dst, eng, sem, a, b, at in call:
                LAND(A(Z, at, at + b - a), sem + str(r), len(eng), k)
        ACT(A(G, S, S + CAP), IND(A("GQ"), A("KIu", 0, 6)), CP)
        SCAN(A("R6"), A("DMP"), A("pK0", 0, 96), 0.0, O.max, O.min)
        TC(A("ROu"), A("R6", *q6))
        TC(IND(A("FW"), A("ROu")), A("LEN"))
        LINE("sc", True, False)
        DMA("y", A("LW"), A("FW", 1, W + 1, rows=slice(2 if last else 1, 128, 16)), 800)
        ACT(A("M1"), A("pB", 0, 96), RL, bias=A("P5K"), scale=-10000.0)
        TT(A(M2, 0, 96), A("pM", 96, 192), A("M1"), O.min)
        RED(A(M3, 96, 97), A(M2), O.max)
        if last:
            ACT(A("IN"), A(M3, 96, 97), IDN, bias=A("CB", 7, 8), scale=4.0)
            for k in range(2):
                ACT(A("SG%d" % k), A("X0%d" % (k + 1)), AF.Sign, bias=A("CB", 0, 1))
            MMS(A("pD1"), (A("IDb"), A("TWO")), (A("IDh"), A("SG0")), (A("IDh"), A("SG1")))
            SCAN(A("STT"), A("N4"), A("LW"), A("IN"), O.add, O.max)
            TT(A("YC"), A("STT"), A("pD1"), O.min)
            LINE("x0", True, False)
            DMA("s", XT(T.yc[:, :]), A("YC"), 800)
        else:
            X1 = "X0%d" % (r + 1)
            ACT(A("IN"), A(M3, 96, 97), IDN, bias=A("PIN"), scale=-STEP)
            SCAN(A(X1), A("C8K"), A("LW"), A("IN"), O.add, O.min)
            LINE("x0", True, False)
            DMA("y", A("X", 0, W, rows=slice(0, 128, 16)), A(X1), 400)
        TS(A("CW", 5, 11), A("R6", *q6), W + 0.5, None, O.is_lt)
        MMS(A("pK1", 128, 134), (A("LSK"), A("CW", 5, 11)), *[(A("GBb"), A("CW", 5 - s, 11 - s)) for s in range(1, 6)])
        TT(A("VV"), A("T2"), A("pK1", 128, 134), O.subtract)
        TS(A("VR"), A("VV"), 1.5 * 2 ** 27, -1.5 * 2 ** 27, O.add, O.add)
        lw = 64 + _C["wide"]
        if _C["wide"]:
            for a in range(6):
                TS(A("LE", 65 * a, 65 * a + 65), A("ROW"), A("VV", a, a + 1), None, O.is_ge)
            TT(A("EQ", 0, 389), A("LE", 1, 390), A("LE", 0, 389), O.subtract)
        for a in range(0 if _C["wide"] else 6):
            TS(A("LE", 64 * a, 64 * a + 64), A("SLh"), A("VR", a, a + 1), None, O.is_gt)
            LINE("sc", False)
            if a < _C["les"]:
                ACT(A("EA", 64 * a, 64 * a + 64), A("SLh"), AF.Abs, bias=A("VR", a, a + 1), scale=-1.0)
            else:
                TS(A("EQ", 64 * a, 64 * a + 64), A("SLh"), A("VR", a, a + 1), None, O.is_equal)
        if _C["les"]:
            ACT(A("EQ", 0, 64 * _C["les"]), A("EA", 0, 64 * _C["les"]), RL, bias=A("one", 0, 1), scale=-1.0)
        for a in range(6):
            TS(A("TA", 128 * a, 128 * a + 128), A("ITH"), A("VR", a, a + 1), A("VV", a, a + 1), O.add, O.is_ge)
            LINE("sc", False)
        MMS(A("pA", 0, 64), (A("IDb"), A("SLh")), (A("IDb"), A("SLi")), stop=False)
        MMS(A("pA", 0, 64), *[(A("GBb"), A("LE", lw * a, lw * a + 64)) for a in range(6)], start=False, stop=False)
        for a in range(6):
            MM(A("pA", 0, 64), A("TA", 128 * a, 128 * a + 128), A("EQ", lw * a, lw * a + 64), False, a == 5)
        TC(A("IXu"), A("pA", 0, 64))

        def turn(q, out, win, off, flip):
            if q == "v" and flip:
                TS(out, IND(win, off), -1.0, 255.0, O.mult, O.add)
            elif q == "v":
                TC(out, IND(win, off))
            elif flip:
                ACT(out, IND(win, off), IDN, bias=A("CB", 2, 3), scale=-1.0)
            else:
                ACT(out, IND(win, off), CP)
        o1, o2 = _C["o3"] if last else (_C["o1"], _C["o2"])
        ZO = ARR + CAP * (_C["mode"] == 1)
        turn("v", A(Z, ZO, ZO + 16 * o1), A(G), A("IXu", 0, o1), True)
        turn("s", A(Z, ZO + 16 * o1, ZO + S), A(G), A("IXu", o1, 64), True)
        LINE("os", True, False)
        n1, n2 = A(RI, 15, 16), A(RJ, 15, 16)
        ACT(A("NT", 1, 2), n2, IDN, bias=n1, scale=2.0)
        LINE("os")
        ACT(A("NT", 0, 1), n2, IDN, bias=n1)
        LINE("os", False)
        TS(A("FX", 18, 64), A("SLf", 18, 64), A("NT", 1, 2), None, O.subtract)
        turn("v", A(H, ARR, 16 * o2), A(Z, ZO, ZO + S), A("FX", 18, o2), not last)
        LINE("x0", False)
        turn("s", A(H, 16 * o2, S), A(Z, ZO, ZO + S), A("FX", o2, 64), not last)
        ACT(A("NMb"), n1, IDN, bias=A("CB", 8, 9), scale=-1.0)
        LINE("os", False)
        ACT(A("NM", 1, 2), n2, IDN, bias=A("CB", 6, 7), scale=-1.0)
        LINE("os", False)
        TS(A("F1"), A("SLf", 0, 18), n1, A("NMb"), O.is_ge, O.mult)
        TS(A("F2"), A("SLf", 0, 18), A("NT", 0, 1), A("NM", 1, 2), O.is_ge, O.mult)
        TS(A("F3"), A("SLf", 0, 18), A("NT", 1, 2), A("NM", 1, 2), O.is_ge, O.mult)
        two(A("pB", 0, 18), [(A("IDb"), A(n, 0, 18)) for n in ("SLh", "SLi")], [(A("IDb"), A(n, 0, 18)) for n in ("F1", "F2", "F3")])
        TC(A("FX", 0, 18), A("pB", 0, 18))
        turn("v", A(H, 0, 160), A(Z, 0, ZO + S), A("FX", 0, 10), not last)
        LINE("x0", False)
        turn("s", A(H, 160, ARR), A(Z, 0, ZO + S), A("FX", 10, 18), not last)
        if last:
            DMA("y", XT(T.yg[:, ARR:S]), A(H, ARR, S), 500)
            DMA("y", XT(T.yg[:, 0:ARR]), A(H, 0, ARR), 300)

    for r in range(RO):
        one_round(r)
    END()
